import numpy as np, ml_dtypes
CORES = [25,29,65,69,153,157,193,197]
N = 8
import mx_ref
BF = ml_dtypes.bfloat16
def gentries(a):
    return np.ascontiguousarray(a.reshape(8, 16, -1).transpose(0, 2, 1)).reshape(8, -1)
def gtable(e):
    e = np.asarray(e); return np.ascontiguousarray(e.reshape(8, -1, 16).transpose(0, 2, 1)).reshape(128, -1).astype(np.int32)
def gcols(t, e):
    v = np.concatenate([t.reshape(8, 16, -1, 4), np.zeros((8, 16, 1, 4), BF)], axis=2)
    return np.ascontiguousarray(np.stack([v[g][:, e[g]] for g in range(8)])).reshape(128, -1)
def tile(rs):
    return np.stack(rs, axis=2).reshape(128, -1).astype(BF)
def pick(q, e):
    c = np.concatenate([q[0].reshape(128, -1, 4), np.zeros((128, 1, 4), np.uint8)], axis=1); s = np.concatenate([q[1], np.ones((16, 1), np.uint8)], axis=1)
    return (np.ascontiguousarray(c[:, e].reshape(128, -1)), np.ascontiguousarray(s[:, e]))
def join(*qs):
    return (np.concatenate([q[0] for q in qs], axis=1), np.concatenate([q[1] for q in qs], axis=1))
def put(q, e, v):
    c, s = q[0].reshape(128, -1, 4).copy(), q[1].copy(); c[:, e] = v[0].reshape(128, -1, 4); s[:, e] = v[1]
    return (c.reshape(128, -1), s)
def pk(c, s):
    return (np.ascontiguousarray(c), mx_ref.live(s))
def emit(q):
    return q[0], q[1]
def packed(v, rng):
    q = [mx_ref.quantize(np.ascontiguousarray(v[r])) for r in range(N)]
    return np.stack([a for a, b in q]), np.stack([mx_ref.plane(b, rng) for a, b in q])
def values_of_codes():
    e, c = np.zeros((128, 128, 4), np.float32), np.zeros((128, 2, 4), np.uint8)
    e[np.arange(128), np.arange(128), 0] = 1
    c[:127, :, 0] = np.arange(256).reshape(2, 128).T[:127]
    return mx_ref.matmul(mx_ref.quantize(e.reshape(128, 512).astype(BF)), (c.reshape(128, 8), np.full((16, 2), 127, np.uint8))).T.reshape(-1).astype(np.float64)
CODE_VALUE, SCALE_VALUE = values_of_codes(), 2.0 ** (np.arange(256) - 127.0)
def decode(q):
    return (CODE_VALUE[q[0]].reshape(16, 8, -1, 4) * SCALE_VALUE[q[1]][:, None, :, None] + 0.0).reshape(128, -1).astype(np.float32)
def f(rng, *shape):
    return mx_ref.flush((rng.standard_normal(shape, dtype=np.float32) * np.exp2(rng.integers(-2, 3, shape[:-1] + (1,)))).astype(BF))
def wide(rng, *shape, cols=0):
    v = rng.standard_normal(shape, dtype=np.float32) * np.exp2(rng.integers(-12, 13, shape)).astype(np.float32)
    if cols: v *= np.repeat(np.exp2(rng.integers(-cols, cols + 1, shape[:-2] + (1, shape[-1] // 4))) * (rng.random(shape[:-2] + (1, shape[-1] // 4)) > 0.0625), 4, axis=-1).astype(np.float32)
    return mx_ref.flush(v.astype(BF))
C = 288
STEP = [4, 1, 2]
HOPS = 128
def numbers_of(rng):
    return {"x": np.array(f(rng, N, 128, 4 * C)), "u": np.array(f(rng, N, 128, 512)), "v": np.array(f(rng, N, 128, 512))}
def orders(rng):
    e = np.tile(np.arange(C), (N, 8, 1))
    k, a, t = rng.permuted(e, axis=2), rng.permuted(e, axis=2)[:, :, 16:], e.copy()
    np.put_along_axis(t, a[:, :, 0::2], a[:, :, 1::2], axis=2)
    np.put_along_axis(t, a[:, :, 1::2], a[:, :, 0::2], axis=2)
    return k, t
def stored(k, t):
    return {"nx": np.stack([gtable(k[r]) for r in range(N)]), "mt": np.stack([gtable(t[r]) for r in range(N)])}
def layers(rng, still=[]):
    w = np.array(f(rng, N, 128, 2048)).reshape(N, 8, 16, 4, 8, 16, 4)
    for i in still:
        w[:, :, i] = 0
        w[:, :, :, :, :, i] = 0
    return w
def weights(rng, w):
    c, p = packed(np.ascontiguousarray(w).reshape(N, 128, 2048), rng)
    return {"wc": c, "ws": p}
def setup_inputs(rng):
    return {**numbers_of(rng), **stored(*orders(rng)), **weights(rng, layers(rng))}
def setup_inputs_ties(rng):
    d = numbers_of(rng)
    k, t = orders(rng)
    o = rng.permutation(N) % 4
    n = rng.integers(0, 4, (N, 8, C))
    c = np.ones((N, 8), np.float32)
    for r in range(N):
        c[r] = rng.permutation(8) % 2 * 2.0 - 1.0
        for g in range(8):
            if o[r] < 2:
                e = rng.permutation(C)
                a = np.arange(C) + 1 if c[r, g] < 0 else C - np.arange(C)
                n[r, g, e] = a if o[r] == 0 else (a + 1) // 2
                k[r, g, e] = np.roll(e, -1)
            if o[r] == 3: n[r, g] = rng.integers(0, 2, C) if g % 2 else 1
        if o[r] < 2: t[r, rng.permutation(8)[:4]] = np.arange(C)
    digits = (n[..., None] & (1 << np.arange(12))).reshape(N, 8, C, 3, 4)
    x = d["x"].reshape(N, 8, 16, C, 4)
    x[:, :, 8:] = 0
    x[:, :, 8:11] = digits.transpose(0, 1, 3, 2, 4).astype(np.float32).astype(BF)
    u = d["u"].reshape(N, 128, 128, 4)
    u[:, :, ::16] = 0
    for g in range(8): u[:, 16 * g + 8:16 * g + 11, 16 * g] = c[:, g].astype(BF)[:, None, None]
    w = layers(rng)
    w[:, :, :, :, :, 8:] = 0
    return {"x": x.reshape(N, 128, 4 * C), "u": u.reshape(N, 128, 512), "v": d["v"], **stored(k, t), **weights(rng, w)}
def setup_inputs_near(rng):
    d = numbers_of(rng)
    x = d["x"].astype(np.float32).reshape(N, 8, 16, C, 4)
    x[:, :, :2] = 0
    x[:, :, 8:] = 0
    u = d["u"].reshape(N, 128, 128, 4)
    u[:, :, ::16] = 0
    w = layers(rng, [0, 1, 8, 9, 10, 11, 12, 13, 14, 15])
    o = (np.arange(N) + rng.integers(N)) % 4
    for r in range(N):
        c = rng.choice([-1.0, 1.0], (8, 1))
        s = rng.integers(0, 16, (8, C))
        digits = ((s[:, :, None] >> np.arange(4)) & 1) * np.exp2(np.arange(4) - 23.0)
        if o[r] < 2:
            x[r, :, 0, :, 0] = c
            x[r, :, 8] = digits
            x[r, :, 11, :, 0] = 2.0 ** -10
        else:
            x[r, :, :8] = 0
            x[r, :, 13, :, 0] = 2.0 ** -30
            x[r, :, 1, :, 0] = rng.choice([-1.0, 1.0], (8, C)) * 2.0 ** -30
            w[r] = 0
            for g in range(8): w[r, g, 1, 0, g, 12, 0] = 2.0 ** -8
        if o[r] == 2: x[r, :, 8] = digits * rng.choice([-1.0, 1.0], (8, C, 1))
        if o[r] == 3:
            x[r, :, 8, :, 0] = np.where(s < 8, 1.25, 0.0) * 2.0 ** -30 * c
            x[r, :, 9, :, 0] = np.where(s < 8, 0.0, 1.125) * 2.0 ** -30 * c
            for g in rng.permutation(8)[:4]:
                e = rng.choice([-1.0, 1.0], C) * 2.0 ** -30
                x[r, g, 8, :, 0] = 1.25 * e
                x[r, g, 9, :, 0] = -1.125 * e
        at = [0, C - 1, int(rng.integers(C)), int(rng.integers(C))]
        for g, j in zip(rng.permutation(8)[:4], at): x[r, g, 0, j, 0] = 2.0 ** 29 * rng.choice([-1.0, 1.0])
        k = 1.0 if o[r] == 0 else 2.0 ** -30
        for h in range(0, 128, 16):
            u[r, h, h, 0] = k if o[r] < 2 else 1.0
            if o[r] < 2: u[r, h + 11, h, 0] = k
            if o[r] < 3: u[r, h + 8, h] = k
            else:
                u[r, h + 8, h, 0] = k
                u[r, h + 9, h, 0] = 1.125 * k
                u[r, h + 12, h, 0] = k
    return {"x": x.reshape(N, 128, 4 * C).astype(BF), "u": u.reshape(N, 128, 512), "v": d["v"], **stored(*orders(rng)), **weights(rng, w)}
def setup_inputs_odd(rng):
    d = numbers_of(rng)
    w = layers(rng, [0, 8])
    x = (1.0 + (2 * rng.integers(0, 64, (N, 16, 8, C, 4)) + 1) * 2.0 ** -7) * np.exp2(-rng.integers(0, 7, (N, 16, 8, C, 4)).astype(np.float64)) * rng.choice([-1.0, 1.0], (N, 16, 8, C, 4))
    x[:, 0::2, 0, :, 0] = 1.96875 * 2.0 ** 8 * rng.choice([-1.0, 1.0], (8, 1))
    x[:, 1::2, 0, :, 0] = rng.choice([1.96875 * 2.0 ** 8, 8.0], (N, 8, C)) * rng.choice([-1.0, 1.0], (N, 8, C))
    for g in range(8): w[:, g, 0, 0, g, 0, 0] = -0.5
    u = d["u"].reshape(N, 16, 8, 128, 4)
    u[:, :, 0, ::16] = 0
    for r in rng.permutation(N)[:N // 2]:
        for i, g in enumerate(rng.permutation(8)[:4]):
            x[r, 2 * g, 1, :, 0] = (8 + rng.integers(0, 2, C)) * 2.0 ** (i - 8)
            u[r, :, :, 16 * g] = 0
            u[r, 2 * g, 1, 16 * g, 0] = 1.0
            w[r, :, :, 0, g, 1] = 0
    return {"x": x.astype(np.float32).reshape(N, 128, 4 * C).astype(BF), "u": u.reshape(N, 128, 512), "v": d["v"], **stored(*orders(rng)), **weights(rng, w)}
def setup_inputs_ends(rng):
    d = numbers_of(rng)
    k, t = orders(rng)
    o, e, m = rng.permutation(N) % 4, rng.permutation(N) % 4, rng.permutation(N) % 4
    for r in range(N):
        s = (r - STEP[-1]) % N
        if o[r] == 3 and o[s] == 2:
            a = rng.choice([n for n in range(N) if o[n] < 2 and o[(n + STEP[-1]) % N] != 3])
            o[s] = o[a]
            o[a] = 2
    i = np.arange(C)
    k[e == 0] = i
    k[e == 1] = (i + 1) % C
    k[e == 2] = C - 1 - i
    k[e == 3] = (i - 1) % C
    t[m == 0] = i
    t[m == 1] = C - 1 - i
    t[m == 2] = i ^ 1
    x = np.zeros((N, 8, 16, C, 4))
    u = d["u"].astype(np.float32).reshape(N, 128, 128, 4)
    v = d["v"].astype(np.float32)
    w = np.zeros((N, 128, 4, 128, 4), np.float32)
    j = np.arange(128)
    for r in range(N):
        h = rng.permutation(8)
        c = np.where(h < 2, 0.0, h % 2 * 2.0 - 1.0)[None, :, None]
        low = -(0.7 + 0.1 * rng.random((8, 16, C, 4))) * 2.0 ** 30
        if o[r] == 0: x[r] = low
        if o[r] == 1: x[r] = low * rng.choice([-1.0, 1.0], (C, 1))
        if o[r] == 2: x[r] = -(1.0 + 0.125 * rng.integers(0, 8, (8, 16, C, 4))) * 2.0 ** -30
        if o[r] == 3: x[r] = d["x"][r].astype(np.float32).reshape(8, 16, C, 4)[:, :, :1]
        if o[r] < 2:
            u[r, :, ::16] = c * (0.9 + 0.1 * rng.random((128, 8, 4))) * 2.0 ** 30
            v[r] = rng.choice([-1.0, 1.0], (128, 512)) * (0.9 + 0.1 * rng.random((128, 512))) * 2.0 ** 30
        if o[r] == 2:
            u[r, :, ::16] = c * (1.0 + 0.125 * rng.integers(0, 8, (128, 8, 4))) * 2.0 ** -30
            v[r] = rng.choice([-1.0, 1.0], (128, 512)) * (1.0 + 0.125 * rng.integers(0, 8, (128, 512))) * 2.0 ** -30
        if o[r] == 3: u[r, :, ::16] *= np.abs(c).astype(np.float32)
        a = np.array([2.0, 2.0 ** -8, -0.25])[rng.permutation(8) % 3][j // 16]
        if o[r] == 2: a = np.zeros(128)
        a[120:] = 256.0
        for b in range(4): w[r, j, b, j, b] = a
    x[:, 7, 8:] = -2.0 ** -30
    return {"x": x.astype(np.float32).reshape(N, 128, 4 * C).astype(BF), "u": u.reshape(N, 128, 512).astype(BF), "v": v.astype(BF), **stored(k, t), **weights(rng, w.astype(BF))}
def setup_inputs_spread(rng):
    d = setup_inputs(rng)
    d["x"] = wide(rng, N, 128, 4 * C, cols=6)
    return d
def check_inputs(d):
    b = []
    for k in ("x", "u", "v"):
        a = np.abs(d[k].astype(np.float32))
        if not (np.isfinite(a).all() and ((a == 0) | (a >= 2.0 ** -30) & (a <= 2.0 ** 30)).all()): b.append("a value of " + k)
    none, least, most = [emit(mx_ref.quantize(np.full((128, 16), k, np.float32).astype(BF)))[1][0, 0] for k in (0.0, 2.0 ** -8, 2.0 ** 8)]
    for r in range(N):
        k, t = gentries(d["nx"][r]), gentries(d["mt"][r])
        if not (np.sort(k, axis=1) == np.arange(C)).all(): b.append("nx: not every column once")
        if not (((t >= 0) & (t < C)).all() and (np.take_along_axis(t, np.clip(t, 0, C - 1), axis=1) == np.arange(C)).all()): b.append("mt: not each other's")
        if ((d["wc"][r] == 0x7F) | (d["wc"][r] == 0xFF)).any(): b.append("wc: a code that is no number")
        s = mx_ref.live(d["ws"][r])
        if ((s != none) & ((s < least) | (s > most))).any(): b.append("ws: a scale out of range")
        if (((d["wc"][r].reshape(16, 8, 512, 4) & 0x7F) != 0) & (s == none)[:, None, :, None]).any(): b.append("wc: a code other than zero under the scale of zeros")
    return b
def at(a, e):
    return np.take_along_axis(a, e, axis=1)
def search(s, follow):
    b = np.tile(np.arange(C), (8, 1))
    p, left = b.copy(), np.ones((8, C), bool)
    for hop in range(1, HOPS + 1):
        to = at(follow, p)
        larger = left & (at(s, to) > s)
        b = np.where(larger, to, b)
        left = left & ~larger
        if hop < HOPS: p = np.where(left, to, p)
    return b, p
def layer(w, q):
    return tile([mx_ref.matmul(pick(w, np.arange(128 * k, 128 * k + 128)), q) * np.float32(0.03125) for k in range(4)])
def reference(x, u, v, nx, mt, wc, ws):
    qu = [mx_ref.quantize(u[r]) for r in range(N)]
    lay = [pk(wc[r], ws[r]) for r in range(N)]
    follow, mate = [gentries(nx[r]) for r in range(N)], [gentries(mt[r]) for r in range(N)]
    now = [x[r] for r in range(N)]
    for step in STEP:
        t, z, first = [], [], []
        for r in range(N):
            q = mx_ref.quantize(now[r])
            s = mx_ref.matmul(qu[r], q)[::16] + np.float32(0.0)
            b, p = search(s, follow[r])
            t.append(decode(q))
            c = t[r].astype(BF)
            z.append(mx_ref.quantize(((gcols(c, b).astype(np.float32) + gcols(c, p).astype(np.float32)) * np.float32(0.5)).astype(BF)))
            first.append(b)
            e = at(s, b)
            swap = at(e, np.minimum(mate[r], np.arange(C))) > at(e, np.maximum(mate[r], np.arange(C)))
            follow[r] = np.where(swap, at(follow[r], mate[r]), follow[r])
        now = [(t[r] + gcols(layer(lay[r], z[(r - step) % N]), first[r]).astype(np.float32)).astype(BF) for r in range(N)]
    y, nf = np.zeros((N, 128, C), np.float32), np.zeros((N, 8, C), np.float32)
    oc, osc = np.zeros((N, 128, 4 * C), np.uint8), np.zeros((N, 16, C), np.uint8)
    for r in range(N):
        q = mx_ref.quantize(now[r])
        y[r] = mx_ref.matmul(mx_ref.quantize(v[r]), q)
        nf[r] = follow[r]
        oc[r], osc[r] = emit(q)
    return {"y": y, "nf": nf, "oc": oc, "osc": osc}

@@ -1,0 +1,379 @@
+from concourse.mybir import dt, AluOpType, ActivationFunctionType
+
+C = 288
+L = 18
+B4 = 4 * C
+HALF = C // 2
+STEP = [4, 1, 2]
+N = 8
+BIG = 1e29
+KB = 1024.0
+F32, BF, I32, U16, F8, U8 = "float32", "bfloat16", "int32", "uint16", "float8_e4m3fn_x4", "uint8"
+
+
+def _scratch():
+    s = {}
+
+    def sb(names, n, d):
+        for k in names.split():
+            s[k] = ("sbuf", [128, n], d)
+    sb("pidx pi15", 1, I32)
+    sb("icol kj kb2", 1, F32)
+    sb("j16 dd kk pen idt sc sp jg0 jg1 sj e1 e2 sk yo n0 n1 m0 m1 m2 m3 m4 m5 m6 m7 h0 h1 h2 h3 h4 h5 h6", C, F32)
+    sb("kb rm cc sm cc2 sm2", C, BF)
+    sb("cl c0k posk dl el dl2 el2 dl3 bitl fk fmf dsix csix mtf mnf mxf", L, F32)
+    sb("nxi mti", L, I32)
+    sb("mnl mxl mtl jl0 jl1 jl2 jl3 jl4 jl5 pl0 pl1", L, U16)
+    sb("lst0 lst1 lst2 rl0 rl1 rl2 rr0 rr1 rr2", 2 * L, U16)
+    sb("uoi", 8, I32)
+    sb("uoff", 8, U16)
+    sb("ones wide", 516, BF)
+    sb("ut vt", 512, BF)
+    sb("x0 xt fo fz zp zt hh", B4, BF)
+    for k, n in (("uq", 128), ("u2", 128), ("vq", 128), ("ec", 512), ("wl", 512), ("zq", C)):
+        s[k] = ("sbuf", [128, n], F8)
+        s[k + "s"] = ("sbuf", [128, n], U8)
+    for t in range(4):
+        s["xq%d" % t] = ("sbuf", [128, C], F8)
+        s["xs%d" % t] = ("sbuf", [128, C], U8)
+    for t in range(3):
+        for a in "lr":
+            s[a + "c%d" % t] = ("sbuf", [128, C], F8)
+            s[a + "p%d" % t] = ("sbuf", [128, C], U8)
+    s["ps"] = ("psum", [128, 4096], F32)
+    return s
+
+
+SCRATCH = _scratch()
+SEMAPHORES = ["sv", "ss", "st", "sg", "ls", "out",
+              "dx", "du", "dv", "dwc", "dws", "dn", "dm"] + [a + str(t) for t in range(3) for a in ("rx", "rs")]
+
+
+def relay_of(topo, cores, a, b):
+    if topo.may_write(a, b):
+        return None
+    for q in topo.cores_of(a):
+        if q not in cores and topo.die(q) == topo.die(a) and topo.may_write(q, b):
+            return q
+    return None
+
+
+def targets(topo, cores, core):
+    out = []
+    for d in STEP:
+        for r in range(N):
+            a, b = cores[r], cores[(r + d) % N]
+            q = relay_of(topo, cores, a, b)
+            if a == core:
+                out.append(b if q is None else q)
+            elif q == core:
+                out.append(b)
+    return out
+
+
+def rank_program(g, core, T, topo):
+    cores = list(T.cores)
+    rank = T.rank_of(core)
+    todo = targets(topo, cores, core)
+    if not todo:
+        return
+    nsent = [0]
+
+    def send(dst, out, src, sem):
+        rid, pid = topo.addr(dst, core)
+        g.remote_dma(out, src, T.sem[sem], T.sem.ls, pid, rid, topo.mask(core, dst))
+        nsent[0] += len(topo.engines(core, dst))
+
+    if rank is None:
+        for t, d in enumerate(STEP):
+            for r in range(N):
+                a, b = cores[r], cores[(r + d) % N]
+                if relay_of(topo, cores, a, b) != core:
+                    continue
+                n = len(topo.engines(a, core))
+                g.wait_ge(T.sem["rx%d" % t], 2 * n)
+                send(b, T["lc%d" % t][:, 0:C].bitcast(dt.uint8), T["rc%d" % t][:, 0:C].bitcast(dt.uint8), "rx%d" % t)
+                send(b, T["lp%d" % t][:, 0:C], T["rp%d" % t][:, 0:C], "rx%d" % t)
+                g.wait_ge(T.sem["rs%d" % t], n)
+                send(b, T["rl%d" % t][:, 0:2 * L], T["rr%d" % t][:, 0:2 * L], "rs%d" % t)
+        g.wait_ge(T.sem.ls, nsent[0])
+        return
+
+    A = AluOpType
+    COPY = ActivationFunctionType.Copy
+    queues = {"v": g.vector, "s": g.scalar, "t": g.tensor, "g": g, "y": g.sync}
+    semname = {"v": "sv", "s": "ss", "t": "st", "g": "sg"}
+    cnt = {"v": 0, "s": 0, "t": 0, "g": 0}
+    seen, wrote, readers = {}, {}, {}
+
+    def wait(q, sem, n):
+        if seen.get((q, sem), 0) < n:
+            queues[q].wait_ge(T.sem[sem], n)
+            seen[(q, sem)] = n
+
+    def before(q, reads, writes):
+        need = {}
+        for k in reads + writes:
+            if k in wrote:
+                s, n = wrote[k]
+                need[s] = max(need.get(s, 0), n)
+        for k in writes:
+            for s, n in readers.get(k, {}).items():
+                need[s] = max(need.get(s, 0), n)
+        for s, n in need.items():
+            wait(q, s, n)
+
+    def op(q, writes, reads, fn, *args, **kw):
+        writes, reads = writes.split(), reads.split()
+        before(q, reads, writes)
+        cnt[q] += 1
+        fn(*args, **kw).then_inc(T.sem[semname[q]], 1)
+        for k in reads:
+            readers.setdefault(k, {})[semname[q]] = cnt[q]
+        for k in writes:
+            wrote[k] = (semname[q], cnt[q])
+            readers[k] = {}
+
+    V, S, P = g.vector, g.scalar, g.tensor
+    ts, tt, tc, scan = V.tensor_scalar, V.tensor_tensor, V.tensor_copy, V.tensor_tensor_scan
+
+    def load(q, name, out, src, sem):
+        queues[q].dma_start(out, src).then_inc(T.sem[sem], 16)
+        wrote[name] = (sem, 16)
+
+    nout = [0]
+
+    def store(q, reads, out, src):
+        before(q, reads.split(), [])
+        queues[q].dma_start(out, src).then_inc(T.sem.out, 16)
+        nout[0] += 16
+
+    def bank(b, n=C):
+        return T.ps[:, 512 * b:512 * b + n]
+
+    load("y", "x0", T.x0[:], T.x[:], "dx")
+    load("s", "nxi", T.nxi[:], T.nx[:], "dn")
+    load("s", "mti", T.mti[:], T.mt[:], "dm")
+    load("s", "ut", T.ut[:], T.u[:], "du")
+    wait("y", "dx", 16)
+    wait("y", "du", 16)
+    load("y", "wl", T.wl[:, 0:512].bitcast(dt.uint8), T.wc[:, 0:2048], "dwc")
+    load("y", "wls", T.wls[:, 0:512], T.ws[:, 0:512], "dws")
+    load("y", "vt", T.vt[:], T.v[:], "dv")
+
+    op("g", "pidx", "", g.iota, T.pidx[:], [[0, 1]], 0, 1)
+    op("g", "dl", "", g.iota, T.dl[:], [[16, L]], 0, 0, allow_small_or_imprecise_dtypes=True)
+    op("g", "j16", "", g.iota, T.j16[:], [[0, L], [1, 16]], 0, 0, allow_small_or_imprecise_dtypes=True)
+    op("g", "uoi", "", g.iota, T.uoi[:], [[16, 8]], 0, 0)
+    op("g", "idt", "", g.iota, T.idt[:], [[1, C]], 0, 0, allow_small_or_imprecise_dtypes=True)
+    op("v", "ones", "", V.memset, T.ones[:], 1.0)
+    op("g", "wide", "ones", g.affine_select, T.wide[:], T.ones[:], [[-1, 516]], A.is_equal, 0.0, 3, 4)
+    op("v", "pi15", "pidx", ts, T.pi15[:], T.pidx[:], 15, None, A.bitwise_and)
+    op("v", "icol", "pi15", tc, T.icol[:], T.pi15[:])
+    op("v", "kj", "icol", ts, T.kj[:], T.icol[:], 15.0, KB, A.is_lt, A.mult)
+    op("v", "kb2", "icol", ts, T.kb2[:], T.icol[:], 15.0, 2.0, A.is_lt, A.mult)
+    op("v", "cl", "dl icol", ts, T.cl[:], T.dl[:], T.icol[:, 0:1], None, A.add)
+    op("v", "c0k", "cl kj", ts, T.c0k[:], T.cl[:], T.kj[:, 0:1], None, A.add)
+    op("v", "dd", "j16 icol", ts, T.dd[:], T.j16[:], T.icol[:, 0:1], None, A.subtract)
+    op("v", "m0", "dd", ts, T.m0[:], T.dd[:], 0.0, -4.0 * KB, A.is_equal, A.mult)
+    op("v", "m1", "dd", ts, T.m1[:], T.dd[:], 1.0, KB, A.is_equal, A.mult)
+    op("v", "kk", "m0 m1", tt, T.kk[:], T.m0[:], T.m1[:], A.add)
+    op("v", "jl0", "nxi", tc, T.jl0[:], T.nxi[:])
+    op("v", "dl2", "nxi", tc, T.dl2[:], T.nxi[:])
+    kj, kb2 = T.kj[:, 0:1], T.kb2[:, 0:1]
+    op("v", "fk", "dl2 kj", ts, T.fk[:], T.dl2[:], kj, None, A.add)
+
+    last = T.sj[:, 15:C:16]
+    lastm = T.sm[:, 15:C:16]
+
+    def ind(buf, lst, a=0):
+        return buf[:, a:a + C].indirect(lst)
+
+    def jl(k):
+        return T["jl%d" % k][:, 0:L]
+
+    def keep(src):
+        op("v", "sj", "kk " + src, scan, T.sj[:], T.kk[:], T[src][:], 0.0, A.add, A.max)
+
+    def hop0():
+        op("s", "h0", "idt jl0", S.activation, T.h0[:], ind(T.idt, jl(0)), COPY)
+
+    def hop(k):
+        op("s", "h%d" % k, "h%d jl%d" % (k - 1, k - 1), S.activation, T["h%d" % k][:], ind(T["h%d" % (k - 1)], jl(k - 1)), COPY)
+
+    def tolist(k):
+        keep("h%d" % k)
+        if k < 6:
+            op("v", "jl%d" % k, "sj kj", ts, jl(k), last, kj, None, A.subtract)
+
+
+    def quantize_x(t):
+        src = "x0" if t == 0 else "xt"
+        op("v", "xq%d" % t, "xt0 xt1 xt2 xt3" if t else "x0", V.quantize_mx,
+           T["xq%d" % t][:, 0:C], T["xs%d" % t][:, 0:C], T[src][:, 0:B4])
+
+    FN = ActivationFunctionType
+    op("s", "rm", "j16", S.activation, T.rm[:], T.j16[:], FN.Sign)
+    op("s", "e1", "dd", S.activation, T.e1[:], T.dd[:], FN.Abs)
+    op("s", "e2", "e1", S.activation, T.e2[:], T.e1[:], FN.Relu, bias=1.0, scale=-1.0)
+    op("s", "pen", "e2", S.activation, T.pen[:], T.e2[:], FN.Identity, bias=-BIG, scale=2.0 * BIG)
+    hop0()
+    hop(1)
+    op("v", "uoff", "uoi", tc, T.uoff[:], T.uoi[:])
+    op("v", "uq", "ut", V.quantize_mx, T.uq[:, 0:128], T.uqs[:, 0:128], T.ut[:, 0:512])
+    op("v", "u2", "uq uoff", tc, T.u2[:, 0:128].bitcast(dt.uint32), T.uq[:, 0:128].bitcast(dt.uint32).indirect(T.uoff[:, 0:8]))
+    op("s", "u2s", "uq uoff", S.activation, T.u2s[:, 0:128], T.uqs[:, 0:128].indirect(T.uoff[:, 0:8]), COPY)
+    op("s", "kb", "kk", S.activation, T.kb[:], T.kk[:], COPY, scale=2.0 / KB)
+    quantize_x(0)
+    tolist(1)
+    op("v", "mtf", "mti", tc, T.mtf[:], T.mti[:])
+    op("v", "mtl", "mti", tc, T.mtl[:], T.mti[:])
+    op("v", "mnf", "mtf cl", tt, T.mnf[:], T.mtf[:], T.cl[:], A.min)
+    op("v", "mxf", "mtf cl", tt, T.mxf[:], T.mtf[:], T.cl[:], A.max)
+    op("v", "mnl", "mnf", tc, T.mnl[:], T.mnf[:])
+    op("v", "mxl", "mxf", tc, T.mxl[:], T.mxf[:])
+
+    def product(b, lhs, ls, a, rhs, rs, reads, lo=0, hi=C):
+        op("t", "b%d" % b, reads, P.matmul_mx, bank(b, hi - lo), lhs[:, a:a + 128], ls[:, a:a + 128], rhs[:, lo:hi], rs[:, lo:hi], True, True)
+
+    def plane(buf, b):
+        return buf[:, C * b:C * b + C]
+
+    for t, d in enumerate(STEP):
+        to, frm = cores[(rank + d) % N], cores[(rank - d) % N]
+        via, came = relay_of(topo, cores, core, to), relay_of(topo, cores, frm, core)
+        xq, xs = T["xq%d" % t], T["xs%d" % t]
+        if t:
+            quantize_x(t)
+        before("g", ["xq%d" % t], [])
+        nxt, lc, lp, ll = (to, "lc%d", "lp%d", "rl%d") if via is None else (via, "rc%d", "rp%d", "rr%d")
+        send(nxt, T[lc % t][:, 0:C].bitcast(dt.uint8), xq[:, 0:C].bitcast(dt.uint8), "rx%d" % t)
+        send(nxt, T[lp % t][:, 0:C], xs[:, 0:C], "rx%d" % t)
+        n = len(topo.engines(frm if came is None else came, core))
+        wrote["land"], wrote["rl"] = ("rx%d" % t, 2 * n), ("rs%d" % t, n)
+        product(0, T.u2, T.u2s, 0, xq, xs, "u2 u2s xq%d" % t, 0, HALF)
+        product(7, T.u2, T.u2s, 0, xq, xs, "u2 u2s xq%d" % t, HALF, C)
+        product(1, T.u2, T.u2s, 0, xq, xs, "u2 u2s xq%d" % t)
+        if t:
+            tolist(1)
+        op("s", "sca", "b0", S.activation, T.sc[:, 0:HALF], bank(0, HALF), COPY)
+        op("v", "scb", "b7", tc, T.sc[:, HALF:C], bank(7, C - HALF))
+        op("s", "n0", "sca scb jl0", S.activation, T.n0[:], ind(T.sc, jl(0)), COPY)
+        op("v", "m0", "sca scb jl0", tc, T.m0[:], ind(T.sc, jl(0)))
+        for k in range(6):
+            m, m2, n1, n2 = "m%d" % k, "m%d" % (k + 1), "n%d" % (k % 2), "n%d" % ((k + 1) % 2)
+            op("v", m2, "%s jl%d %s" % (m, k, n1), tt, T[m2][:], ind(T[m], jl(k)), T[n1][:], A.max)
+            if k < 5:
+                hop(k + 2)
+                op("s", n2, m2, S.activation, T[n2][:], T[m2][:], COPY)
+                tolist(k + 2)
+            if k < 4:
+                if t == 0:
+                    op("v", "ec%d" % k, "wide", V.quantize_mx, T.ec[:, 128 * k:128 * k + 128], T.ecs[:, 128 * k:128 * k + 128], T.wide[:, 3 - k:515 - k])
+                product(2 + k, T.ec, T.ecs, 128 * k, xq, xs, "ec%d xq%d" % (k, t))
+        op("s", "m7", "m0 jl0", S.activation, T.m7[:], ind(T.m0, jl(0)), COPY)
+        op("v", "dsix", "sj c0k", tt, T.dsix[:], last, T.c0k[:], A.subtract)
+        op("v", "cc", "m6 b1", tt, T.cc[:], T.m6[:], bank(1), A.is_le)
+        op("v", "dl", "dsix kb2", ts, T.dl[:], T.dsix[:], kb2, None, A.mult)
+        op("v", "sp", "b1 pen", tt, T.sp[:], bank(1), T.pen[:], A.min)
+        op("v", "csix", "c0k dl", tt, T.csix[:], T.c0k[:], T.dl[:], A.subtract)
+        op("v", "sm", "kb cc", scan, T.sm[:], T.kb[:], T.cc[:], 0.0, A.add, A.max)
+        op("v", "el", "sm dsix", tt, T.el[:], lastm, T.dsix[:], A.mult)
+        op("v", "posk", "csix el", tt, T.posk[:], T.csix[:], T.el[:], A.add)
+        op("v", "pl0", "posk kj", ts, T.pl0[:], T.posk[:], kj, None, A.subtract)
+        lst = T["lst%d" % t]
+        at, key = T.pl0[:, 0:L], "pl0"
+        for k in [5, 4, 3, 2, 1]:
+            jg = "jg%d" % (k % 2)
+            op("s", jg, "h%d %s" % (k, key), S.activation, T[jg][:], ind(T["h%d" % k], at), COPY)
+            op("v", "cc", "m%d sp %s" % (k, key), tt, T.cc[:], ind(T["m%d" % k], at), T.sp[:], A.is_le)
+            if k >= 2:
+                b = 5 - k
+                op("s", "fo%d" % b, "b%d" % (2 + b), S.activation, plane(T.fo, b), bank(2 + b), COPY)
+                product(2 + b, T.ec, T.ecs, 128 * b, T["lc%d" % t], T["lp%d" % t], "land ec%d" % b)
+            keep(jg)
+            op("v", "sm", "rm cc", scan, T.sm[:], T.rm[:], T.cc[:], 0.0, A.mult, A.add)
+            op("v", "dl", "sj posk", tt, T.dl[:], last, T.posk[:], A.subtract)
+            op("v", "el", "sm dl", tt, T.el[:], lastm, T.dl[:], A.mult)
+            op("v", "posk", "posk el", tt, T.posk[:], T.posk[:], T.el[:], A.add)
+            key = "pl%d" % (k % 2)
+            at = T[key][:, 0:L]
+            op("v", key, "posk kj", ts, at, T.posk[:], kj, None, A.subtract)
+        op("s", "jg0", "h0 " + key, S.activation, T.jg0[:], ind(T.h0, at), COPY)
+        op("v", "cc", "m0 sp " + key, tt, T.cc[:], ind(T.m0, at), T.sp[:], A.is_le)
+        op("s", "jg1", "h1 " + key, S.activation, T.jg1[:], ind(T.h1, at), COPY)
+        op("v", "cc2", "m7 sp " + key, tt, T.cc2[:], ind(T.m7, at), T.sp[:], A.is_le)
+        keep("jg0")
+        op("v", "sm", "rm cc", scan, T.sm[:], T.rm[:], T.cc[:], 0.0, A.mult, A.add)
+        op("v", "sm2", "rm cc2", scan, T.sm2[:], T.rm[:], T.cc2[:], 0.0, A.mult, A.add)
+        op("v", "sk", "kk jg1", scan, T.sk[:], T.kk[:], T.jg1[:], 0.0, A.add, A.max)
+        op("v", "dl", "sj posk", tt, T.dl[:], last, T.posk[:], A.subtract)
+        op("v", "dl2", "sk c0k", tt, T.dl2[:], T.c0k[:], T.sk[:, 15:C:16], A.subtract)
+        op("v", "dl3", "sk sj", tt, T.dl3[:], T.sk[:, 15:C:16], last, A.subtract)
+        op("v", "el", "sm dl", tt, T.el[:], lastm, T.dl[:], A.mult)
+        op("v", "el2", "sm2 dl2", tt, T.el2[:], T.sm2[:, 15:C:16], T.dl2[:], A.mult)
+        op("v", "dl3", "dl3 sm", tt, T.dl3[:], T.dl3[:], lastm, A.mult)
+        op("v", "el2", "el2 sm", tt, T.el2[:], T.el2[:], lastm, A.mult)
+        op("v", "posk", "posk el", tt, T.posk[:], T.posk[:], T.el[:], A.add)
+        op("v", "dl3", "dl3 sj", tt, T.dl3[:], T.dl3[:], last, A.add)
+        op("v", "lstp", "posk kj", ts, lst[:, L:2 * L], T.posk[:], kj, None, A.subtract)
+        op("v", "el2", "el2 dl3", tt, T.el2[:], T.el2[:], T.dl3[:], A.add)
+        op("v", "lstb", "el2 kj", ts, lst[:, 0:L], T.el2[:], kj, None, A.subtract)
+        before("g", ["lstb", "lstp"], [])
+        send(nxt, T[ll % t][:, 0:2 * L], lst[:, 0:2 * L], "rs%d" % t)
+        bl = lst[:, 0:L]
+        op("s", "jg0", "h0 mtl", S.activation, T.jg0[:], ind(T.h0, T.mtl[:, 0:L]), COPY)
+        for b in range(4):
+            op("s", "fz%d" % b, "b%d" % (2 + b), S.activation, plane(T.fz, b), bank(2 + b), COPY, scale=0.5)
+        op("v", "e1", "sca scb lstb", tc, T.e1[:], ind(T.sc, bl))
+        op("v", "e2", "e1 mxl", tc, T.e2[:], ind(T.e1, T.mxl[:, 0:L]))
+        op("v", "cc", "e1 e2 mnl", tt, T.cc[:], ind(T.e1, T.mnl[:, 0:L]), T.e2[:], A.is_gt)
+        keep("jg0")
+        op("v", "fmf", "sj fk", tt, T.fmf[:], last, T.fk[:], A.subtract)
+        if t == 1:
+            op("v", "vq", "vt", V.quantize_mx, T.vq[:, 0:128], T.vqs[:, 0:128], T.vt[:, 0:512])
+        rl = T["rl%d" % t]
+        for lo, hi, b in ((0, 160, 0), (160, C, 0), (0, C, 1), (0, C, 2), (0, C, 3)):
+            op("s", "zp%d.%d" % (b, lo), "fz%d rl" % b, S.activation, T.zp[:, C * b + lo:C * b + hi],
+               ind(T.fz, rl[:, L + lo // 16:L + hi // 16], C * b), COPY)
+            op("v", "zt%d.%d" % (b, lo), "fz%d zp%d.%d rl" % (b, b, lo), tt, T.zt[:, 4 * lo + b:4 * hi:4],
+               ind(T.fz, rl[:, lo // 16:hi // 16], C * b), T.zp[:, C * b + lo:C * b + hi], A.add)
+        op("v", "zq", "zt0.0 zt0.160 zt1.0 zt2.0 zt3.0", V.quantize_mx, T.zq[:, 0:C], T.zqs[:, 0:C], T.zt[:, 0:B4])
+        hb = [6, 7, 2, 3]
+        product(6, T.wl, T.wls, 0, T.zq, T.zqs, "wl wls zq", 0, HALF)
+        product(4, T.wl, T.wls, 0, T.zq, T.zqs, "wl wls zq", HALF, C)
+        for b in range(1, 4):
+            product(hb[b], T.wl, T.wls, 128 * b, T.zq, T.zqs, "wl wls zq")
+        op("s", "hh0", "b6", S.activation, T.hh[:, 0:HALF], bank(6, HALF), COPY, scale=0.03125)
+        for b in range(1, 4):
+            op("s", "hh%d" % b, "b%d" % hb[b], S.activation, plane(T.hh, b), bank(hb[b]), COPY, scale=0.03125)
+        op("v", "sm", "kb cc", scan, T.sm[:], T.kb[:], T.cc[:], 0.0, A.add, A.max)
+        op("v", "bitl", "sm kb2", ts, T.bitl[:], lastm, kb2, None, A.subtract)
+        op("v", "el", "bitl fmf", tt, T.el[:], T.bitl[:], T.fmf[:], A.mult)
+        op("v", "hhb", "b4", ts, T.hh[:, HALF:C], bank(4, C - HALF), 0.03125, None, A.mult)
+        for b in range(4):
+            op("v", "xt%d" % b, "hh%d fo%d lstb" % (b, b) + (" hhb" if b == 0 else ""), tt, T.xt[:, b:B4:4],
+               ind(T.hh, bl, C * b), plane(T.fo, b), A.add)
+            if b == 0:
+                op("v", "fk", "fk el", tt, T.fk[:], T.fk[:], T.el[:], A.add)
+            if b == 1:
+                op("v", "jl0", "fk kj", ts, jl(0), T.fk[:], kj, None, A.subtract)
+        hop0()
+        if t < 2:
+            hop(1)
+        else:
+            for i in range(8):
+                store("s", "h0", T.nf[i:i + 1, :], T.h0[16 * i:16 * i + 1, :])
+    quantize_x(3)
+    product(0, T.vq, T.vqs, 0, T.xq3, T.xs3, "vq xq3", 0, HALF)
+    product(7, T.vq, T.vqs, 0, T.xq3, T.xs3, "vq xq3", HALF, C)
+    store("y", "xq3", T.oc[:, 0:B4], T.xq3[:, 0:C].bitcast(dt.uint8))
+    op("s", "yoa", "b0", S.activation, T.yo[:, 0:HALF], bank(0, HALF), COPY)
+    op("v", "yob", "b7", tc, T.yo[:, HALF:C], bank(7, C - HALF))
+    for k in range(4):
+        store("s", "xq3", T.osc[4 * k:4 * k + 4, 0:C], T.xs3[32 * k:32 * k + 4, 0:C])
+    store("y", "yoa yob", T.y[:], T.yo[:])
+    for q in ("v", "s", "t", "g"):
+        wait("g", semname[q], cnt[q])
+    wait("g", "ls", nsent[0])
+    wait("g", "out", nout[0])

@@ -8,7 +8,10 @@ STEP = [4, 1, 2]
 N = 8
 BIG = 1e29
 KB = 1024.0
-F32, BF, I32, U16, F8, U8 = "float32", "bfloat16", "int32", "uint16", "float8_e4m3fn_x4", "uint8"
+MID = 144.0
+PARTS = ((0, 10, 32), (10, 18, 592))
+SLOTS = 1024
+F32, BF, I32, U16, F8, U8, F16 = "float32", "bfloat16", "int32", "uint16", "float8_e4m3fn_x4", "uint8", "float16"
 
 
 def _scratch():
@@ -19,11 +22,18 @@ def _scratch():
             s[k] = ("sbuf", [128, n], d)
     sb("pidx pi15", 1, I32)
     sb("icol kj kb2", 1, F32)
-    sb("j16 dd kk pen idt sc sp jg0 jg1 sj e1 e2 sk yo n0 n1 m0 m1 m2 m3 m4 m5 m6 m7 h0 h1 h2 h3 h4 h5 h6", C, F32)
-    sb("kb rm cc sm cc2 sm2", C, BF)
-    sb("cl c0k posk dl el dl2 el2 dl3 bitl fk fmf dsix csix mtf mnf mxf", L, F32)
+    sb("j16 dd pen sc sp e1 e2 yo n0 n1 m0 m1 m2 m3 m4 m5", C, F32)
+    sb("idt kk kb rm cc cc2 sm jg0 jg1 jm h0 h1 h2 h3 h4 h5 h6 h7", C, BF)
+    sb("sj s5 s6 s7", C, F16)
+    sb("v0 v1 vc", SLOTS, F16)
+    sb("ba bz", SLOTS, BF)
+    sb("bt", 64 + 5 * C, BF)
+    sb("top topo nn nno", 5 * L, F16)
+    sb("po bo", 3 * L, F16)
+    sb("cl c0k dl el fk fkx fmf mtf mnf mxf", L, F32)
     sb("nxi mti", L, I32)
-    sb("mnl mxl mtl jl0 jl1 jl2 jl3 jl4 jl5 pl0 pl1", L, U16)
+    sb("mnl mxl mtl pl0 pl1", L, U16)
+    sb("jls", 8 * L, U16)
     sb("lst0 lst1 lst2 rl0 rl1 rl2 rr0 rr1 rr2", 2 * L, U16)
     sb("uoi", 8, I32)
     sb("uoff", 8, U16)
@@ -100,7 +110,8 @@ def rank_program(g, core, T, topo):
         return
 
     A = AluOpType
-    COPY = ActivationFunctionType.Copy
+    FN = ActivationFunctionType
+    COPY = FN.Copy
     queues = {"v": g.vector, "s": g.scalar, "t": g.tensor, "g": g, "y": g.sync}
     semname = {"v": "sv", "s": "ss", "t": "st", "g": "sg"}
     cnt = {"v": 0, "s": 0, "t": 0, "g": 0}
@@ -153,8 +164,8 @@ def rank_program(g, core, T, topo):
 
     load("y", "x0", T.x0[:], T.x[:], "dx")
     load("s", "nxi", T.nxi[:], T.nx[:], "dn")
-    load("s", "mti", T.mti[:], T.mt[:], "dm")
     load("s", "ut", T.ut[:], T.u[:], "du")
+    load("s", "mti", T.mti[:], T.mt[:], "dm")
     wait("y", "dx", 16)
     wait("y", "du", 16)
     load("y", "wl", T.wl[:, 0:512].bitcast(dt.uint8), T.wc[:, 0:2048], "dwc")
@@ -162,76 +173,100 @@ def rank_program(g, core, T, topo):
     load("y", "vt", T.vt[:], T.v[:], "dv")
 
     op("g", "pidx", "", g.iota, T.pidx[:], [[0, 1]], 0, 1)
-    op("g", "dl", "", g.iota, T.dl[:], [[16, L]], 0, 0, allow_small_or_imprecise_dtypes=True)
     op("g", "j16", "", g.iota, T.j16[:], [[0, L], [1, 16]], 0, 0, allow_small_or_imprecise_dtypes=True)
+    op("g", "idt", "", g.iota, T.idt[:], [[1, C]], -int(MID), 0, allow_small_or_imprecise_dtypes=True)
+    op("g", "dl", "", g.iota, T.dl[:], [[16, L]], 0, 0, allow_small_or_imprecise_dtypes=True)
     op("g", "uoi", "", g.iota, T.uoi[:], [[16, 8]], 0, 0)
-    op("g", "idt", "", g.iota, T.idt[:], [[1, C]], 0, 0, allow_small_or_imprecise_dtypes=True)
     op("v", "ones", "", V.memset, T.ones[:], 1.0)
     op("g", "wide", "ones", g.affine_select, T.wide[:], T.ones[:], [[-1, 516]], A.is_equal, 0.0, 3, 4)
+    op("v", "ba", "", V.memset, T.ba[:], 0.0)
     op("v", "pi15", "pidx", ts, T.pi15[:], T.pidx[:], 15, None, A.bitwise_and)
+    op("v", "bz", "", V.memset, T.bz[:], 0.0)
     op("v", "icol", "pi15", tc, T.icol[:], T.pi15[:])
-    op("v", "kj", "icol", ts, T.kj[:], T.icol[:], 15.0, KB, A.is_lt, A.mult)
+    op("v", "bt", "", V.memset, T.bt[:, 75 + 64:64 + 5 * C:80], 0.0)
     op("v", "kb2", "icol", ts, T.kb2[:], T.icol[:], 15.0, 2.0, A.is_lt, A.mult)
-    op("v", "cl", "dl icol", ts, T.cl[:], T.dl[:], T.icol[:, 0:1], None, A.add)
-    op("v", "c0k", "cl kj", ts, T.c0k[:], T.cl[:], T.kj[:, 0:1], None, A.add)
     op("v", "dd", "j16 icol", ts, T.dd[:], T.j16[:], T.icol[:, 0:1], None, A.subtract)
+    op("v", "kj", "kb2", ts, T.kj[:], T.kb2[:], KB / 2, MID, A.mult, A.subtract)
     op("v", "m0", "dd", ts, T.m0[:], T.dd[:], 0.0, -4.0 * KB, A.is_equal, A.mult)
     op("v", "m1", "dd", ts, T.m1[:], T.dd[:], 1.0, KB, A.is_equal, A.mult)
+    op("v", "cl", "dl icol", ts, T.cl[:], T.dl[:], T.icol[:, 0:1], None, A.add)
+    op("v", "jl0", "nxi", tc, T.jls[:, 0:L], T.nxi[:])
     op("v", "kk", "m0 m1", tt, T.kk[:], T.m0[:], T.m1[:], A.add)
-    op("v", "jl0", "nxi", tc, T.jl0[:], T.nxi[:])
-    op("v", "dl2", "nxi", tc, T.dl2[:], T.nxi[:])
+    op("v", "fkx", "nxi", tc, T.fkx[:], T.nxi[:])
     kj, kb2 = T.kj[:, 0:1], T.kb2[:, 0:1]
-    op("v", "fk", "dl2 kj", ts, T.fk[:], T.dl2[:], kj, None, A.add)
+    op("v", "c0k", "cl kj", ts, T.c0k[:], T.cl[:], kj, None, A.add)
+    op("v", "fk", "fkx kj", ts, T.fk[:], T.fkx[:], kj, None, A.add)
 
-    last = T.sj[:, 15:C:16]
-    lastm = T.sm[:, 15:C:16]
+    def last(buf, lo=0, hi=L):
+        return buf[:, 16 * lo + 15:16 * hi:16]
 
     def ind(buf, lst, a=0):
         return buf[:, a:a + C].indirect(lst)
 
-    def jl(k):
-        return T["jl%d" % k][:, 0:L]
+    def jl(k, lo=0, hi=L):
+        return T.jls[:, L * k + lo:L * k + hi]
 
-    def keep(src):
-        op("v", "sj", "kk " + src, scan, T.sj[:], T.kk[:], T[src][:], 0.0, A.add, A.max)
+    def spread3(buf, part):
+        lo, hi, a = part
+        return buf[:, a:a + 48 * (hi - lo):3]
 
-    def hop0():
-        op("s", "h0", "idt jl0", S.activation, T.h0[:], ind(T.idt, jl(0)), COPY)
+    def slot(buf, part, i):
+        lo, hi, a = part
+        return buf[:, a + 45 + 16 * i:a + 45 + 16 * i + 48 * (hi - lo - 1) + 1:48]
 
-    def hop(k):
-        op("s", "h%d" % k, "h%d jl%d" % (k - 1, k - 1), S.activation, T["h%d" % k][:], ind(T["h%d" % (k - 1)], jl(k - 1)), COPY)
+    def three(buf, part, i):
+        lo, hi, a = part
+        return buf[:, a + 45 + 16 * i:a + 45 + 16 * i + 16 * (3 * (hi - lo) - 1) + 1:16]
 
-    def tolist(k):
-        keep("h%d" % k)
-        if k < 6:
-            op("v", "jl%d" % k, "sj kj", ts, jl(k), last, kj, None, A.subtract)
+    def cols(buf, part):
+        return buf[:, 16 * part[0]:16 * part[1]]
 
+    hops, lists = [0], [1]
+
+    def hop():
+        k = hops[0]
+        if k > 7:
+            return
+        hops[0] += 1
+        w, l = ("idt", 0) if k == 0 else ("h6", 5) if k == 7 else ("h%d" % (k - 1), k - 1)
+        op("s", "h%d" % k, "%s jl%d" % (w, l), S.activation, T["h%d" % k][:], ind(T[w], jl(l)), COPY)
+
+    def tolist():
+        k = lists[0]
+        if k >= hops[0]:
+            return
+        lists[0] += 1
+        sj = "s%d" % k if k >= 5 else "sj"
+        op("v", sj, "kk h%d" % k, scan, T[sj][:], T.kk[:], T["h%d" % k][:], 0.0, A.add, A.max)
+        op("v", "jl%d" % k, sj + " kj", ts, jl(k), last(T[sj]), kj, None, A.subtract)
 
     def quantize_x(t):
         src = "x0" if t == 0 else "xt"
         op("v", "xq%d" % t, "xt0 xt1 xt2 xt3" if t else "x0", V.quantize_mx,
            T["xq%d" % t][:, 0:C], T["xs%d" % t][:, 0:C], T[src][:, 0:B4])
 
-    FN = ActivationFunctionType
-    op("s", "rm", "j16", S.activation, T.rm[:], T.j16[:], FN.Sign)
     op("s", "e1", "dd", S.activation, T.e1[:], T.dd[:], FN.Abs)
+    op("s", "rm", "j16", S.activation, T.rm[:], T.j16[:], FN.Sign)
     op("s", "e2", "e1", S.activation, T.e2[:], T.e1[:], FN.Relu, bias=1.0, scale=-1.0)
+    hop()
     op("s", "pen", "e2", S.activation, T.pen[:], T.e2[:], FN.Identity, bias=-BIG, scale=2.0 * BIG)
-    hop0()
-    hop(1)
+    hop()
+    op("s", "kb", "kk", S.activation, T.kb[:], T.kk[:], COPY, scale=2.0 / KB)
     op("v", "uoff", "uoi", tc, T.uoff[:], T.uoi[:])
+    for p in PARTS:
+        op("v", "ba", "", V.memset, slot(T.ba, p, -1), 1.0)
+    a, b = [p[2] + 45 + 48 * (p[1] - p[0]) for p in PARTS]
+    op("v", "v0x", "ones", tc, T.v0[:, a:b + 1:b - a], T.ones[:, 0:2])
+    op("v", "top", "ones", ts, T.top[:], T.ones[:, 0:5 * L], 0.0, None, A.mult)
+    op("v", "nn", "ones", ts, T.nn[:], T.ones[:, 0:5 * L], 0.0, None, A.mult)
+    tolist()
+    hop()
+    op("v", "nn", "ones", tc, T.nn[:, 4:5 * L:5], T.ones[:, 0:L])
     op("v", "uq", "ut", V.quantize_mx, T.uq[:, 0:128], T.uqs[:, 0:128], T.ut[:, 0:512])
+    tolist()
     op("v", "u2", "uq uoff", tc, T.u2[:, 0:128].bitcast(dt.uint32), T.uq[:, 0:128].bitcast(dt.uint32).indirect(T.uoff[:, 0:8]))
     op("s", "u2s", "uq uoff", S.activation, T.u2s[:, 0:128], T.uqs[:, 0:128].indirect(T.uoff[:, 0:8]), COPY)
-    op("s", "kb", "kk", S.activation, T.kb[:], T.kk[:], COPY, scale=2.0 / KB)
-    quantize_x(0)
-    tolist(1)
-    op("v", "mtf", "mti", tc, T.mtf[:], T.mti[:])
-    op("v", "mtl", "mti", tc, T.mtl[:], T.mti[:])
-    op("v", "mnf", "mtf cl", tt, T.mnf[:], T.mtf[:], T.cl[:], A.min)
-    op("v", "mxf", "mtf cl", tt, T.mxf[:], T.mtf[:], T.cl[:], A.max)
-    op("v", "mnl", "mnf", tc, T.mnl[:], T.mnf[:])
-    op("v", "mxl", "mxf", tc, T.mxl[:], T.mxf[:])
+    hop()
 
     def product(b, lhs, ls, a, rhs, rs, reads, lo=0, hi=C):
         op("t", "b%d" % b, reads, P.matmul_mx, bank(b, hi - lo), lhs[:, a:a + 128], ls[:, a:a + 128], rhs[:, lo:hi], rs[:, lo:hi], True, True)
@@ -243,8 +278,7 @@ def rank_program(g, core, T, topo):
         to, frm = cores[(rank + d) % N], cores[(rank - d) % N]
         via, came = relay_of(topo, cores, core, to), relay_of(topo, cores, frm, core)
         xq, xs = T["xq%d" % t], T["xs%d" % t]
-        if t:
-            quantize_x(t)
+        quantize_x(t)
         before("g", ["xq%d" % t], [])
         nxt, lc, lp, ll = (to, "lc%d", "lp%d", "rl%d") if via is None else (via, "rc%d", "rp%d", "rr%d")
         send(nxt, T[lc % t][:, 0:C].bitcast(dt.uint8), xq[:, 0:C].bitcast(dt.uint8), "rx%d" % t)
@@ -254,91 +288,179 @@ def rank_program(g, core, T, topo):
         product(0, T.u2, T.u2s, 0, xq, xs, "u2 u2s xq%d" % t, 0, HALF)
         product(7, T.u2, T.u2s, 0, xq, xs, "u2 u2s xq%d" % t, HALF, C)
         product(1, T.u2, T.u2s, 0, xq, xs, "u2 u2s xq%d" % t)
-        if t:
-            tolist(1)
+        tolist()
         op("s", "sca", "b0", S.activation, T.sc[:, 0:HALF], bank(0, HALF), COPY)
         op("v", "scb", "b7", tc, T.sc[:, HALF:C], bank(7, C - HALF))
-        op("s", "n0", "sca scb jl0", S.activation, T.n0[:], ind(T.sc, jl(0)), COPY)
-        op("v", "m0", "sca scb jl0", tc, T.m0[:], ind(T.sc, jl(0)))
-        for k in range(6):
+        op("s", "n0.0 n0.1", "sca scb jl0", S.activation, T.n0[:], ind(T.sc, jl(0)), COPY)
+        op("v", "m0.0 m0.1", "sca scb jl0", tc, T.m0[:], ind(T.sc, jl(0)))
+        for k in range(5):
             m, m2, n1, n2 = "m%d" % k, "m%d" % (k + 1), "n%d" % (k % 2), "n%d" % ((k + 1) % 2)
-            op("v", m2, "%s jl%d %s" % (m, k, n1), tt, T[m2][:], ind(T[m], jl(k)), T[n1][:], A.max)
-            if k < 5:
-                hop(k + 2)
-                op("s", n2, m2, S.activation, T[n2][:], T[m2][:], COPY)
-                tolist(k + 2)
+            hop()
+            for i, p in enumerate(PARTS):
+                op("v", "%s.%d" % (m2, i), "%s.0 %s.1 jl%d %s.%d" % (m, m, k, n1, i), tt,
+                   cols(T[m2], p), ind(T[m], jl(k, p[0], p[1])), cols(T[n1], p), A.max)
+                if k < 4:
+                    op("s", "%s.%d" % (n2, i), "%s.%d" % (m2, i), S.activation, cols(T[n2], p), cols(T[m2], p), COPY)
+            tolist()
             if k < 4:
                 if t == 0:
                     op("v", "ec%d" % k, "wide", V.quantize_mx, T.ec[:, 128 * k:128 * k + 128], T.ecs[:, 128 * k:128 * k + 128], T.wide[:, 3 - k:515 - k])
                 product(2 + k, T.ec, T.ecs, 128 * k, xq, xs, "ec%d xq%d" % (k, t))
-        op("s", "m7", "m0 jl0", S.activation, T.m7[:], ind(T.m0, jl(0)), COPY)
-        op("v", "dsix", "sj c0k", tt, T.dsix[:], last, T.c0k[:], A.subtract)
-        op("v", "cc", "m6 b1", tt, T.cc[:], T.m6[:], bank(1), A.is_le)
-        op("v", "dl", "dsix kb2", ts, T.dl[:], T.dsix[:], kb2, None, A.mult)
-        op("v", "sp", "b1 pen", tt, T.sp[:], bank(1), T.pen[:], A.min)
-        op("v", "csix", "c0k dl", tt, T.csix[:], T.c0k[:], T.dl[:], A.subtract)
-        op("v", "sm", "kb cc", scan, T.sm[:], T.kb[:], T.cc[:], 0.0, A.add, A.max)
-        op("v", "el", "sm dsix", tt, T.el[:], lastm, T.dsix[:], A.mult)
-        op("v", "posk", "csix el", tt, T.posk[:], T.csix[:], T.el[:], A.add)
-        op("v", "pl0", "posk kj", ts, T.pl0[:], T.posk[:], kj, None, A.subtract)
+            if k == 3:
+                op("v", "sp", "b1 pen", tt, T.sp[:], bank(1), T.pen[:], A.min)
+        assert hops[0] == 8 and lists[0] == 8
+        if t == 0:
+            op("v", "mtf", "mti", tc, T.mtf[:], T.mti[:])
+            op("v", "mtl", "mti", tc, T.mtl[:], T.mti[:])
+        bt = T.bt
+        op("v", "cc.0 cc.1", "m5.0 m5.1 b1", tt, T.cc[:], T.m5[:], bank(1), A.is_le)
+        op("v", "top2", "top s5 c0k", tt, T.top[:, 2:5 * L:5], last(T.s5), T.c0k[:], A.subtract)
+        op("v", "top1", "top s5 s6", tt, T.top[:, 1:5 * L:5], last(T.s6), last(T.s5), A.subtract)
+        op("v", "cc2.0 cc2.1", "m5.0 m5.1 jl5 sp", tt, T.cc2[:], ind(T.m5, jl(5)), T.sp[:], A.is_le)
+        op("v", "sm", "kb cc.0 cc.1", scan, T.sm[:], T.kb[:], T.cc[:], 0.0, A.add, A.max)
+        op("v", "top0", "top s6 s7", tt, T.top[:, 0:5 * L:5], last(T.s7), last(T.s6), A.subtract)
+        op("v", "bt2", "bt rm cc2.0 cc2.1", scan, bt[:, 32:32 + 5 * C:5], T.rm[:], T.cc2[:], 0.0, A.mult, A.add)
+        op("v", "cc.0 cc.1", "m5.0 m5.1 jl6 sp", tt, T.cc[:], ind(T.m5, jl(6)), T.sp[:], A.is_le)
+        op("v", "bt3", "bt sm kb2", ts, bt[:, 75 + 48:64 + 5 * C:80], last(T.sm), kb2, None, A.subtract)
+        if t == 0:
+            op("v", "top3", "top c0k", tc, T.top[:, 3:5 * L:5], T.c0k[:])
+        op("v", "cc2.0 cc2.1", "m5.0 m5.1 jl7 sp", tt, T.cc2[:], ind(T.m5, jl(7)), T.sp[:], A.is_le)
+        op("v", "bt1", "bt rm cc.0 cc.1", scan, bt[:, 16:16 + 5 * C:5], T.rm[:], T.cc[:], 0.0, A.mult, A.add)
+        op("v", "bt0", "bt rm cc2.0 cc2.1", scan, bt[:, 0:5 * C:5], T.rm[:], T.cc2[:], 0.0, A.mult, A.add)
+        five = bt[:, 75:75 + 16 * (5 * L - 1) + 1:16]
+        op("v", "topo", "bt0 bt1 bt2 bt3 top0 top1 top2 top3", scan, T.topo[:], five, T.top[:], 0.0, A.mult, A.add)
+        op("v", "nno", "bt0 bt1 bt2 bt3 nn", scan, T.nno[:], five, T.nn[:], 1.0, A.mult, A.add)
+        op("v", "pl0.0 pl0.1", "topo kj", ts, T.pl0[:], T.topo[:, 3:5 * L:5], kj, None, A.subtract)
+        for b in range(4):
+            op("s", "fo%d" % b, "b%d" % (2 + b), S.activation, plane(T.fo, b), bank(2 + b), COPY)
+            product(2 + b, T.ec, T.ecs, 128 * b, T["lc%d" % t], T["lp%d" % t], "land ec%d" % b)
+        op("s", "jm", "h0 mtl", S.activation, T.jm[:], ind(T.h0, T.mtl[:, 0:L]), COPY)
         lst = T["lst%d" % t]
-        at, key = T.pl0[:, 0:L], "pl0"
-        for k in [5, 4, 3, 2, 1]:
-            jg = "jg%d" % (k % 2)
-            op("s", jg, "h%d %s" % (k, key), S.activation, T[jg][:], ind(T["h%d" % k], at), COPY)
-            op("v", "cc", "m%d sp %s" % (k, key), tt, T.cc[:], ind(T["m%d" % k], at), T.sp[:], A.is_le)
-            if k >= 2:
-                b = 5 - k
-                op("s", "fo%d" % b, "b%d" % (2 + b), S.activation, plane(T.fo, b), bank(2 + b), COPY)
-                product(2 + b, T.ec, T.ecs, 128 * b, T["lc%d" % t], T["lp%d" % t], "land ec%d" % b)
-            keep(jg)
-            op("v", "sm", "rm cc", scan, T.sm[:], T.rm[:], T.cc[:], 0.0, A.mult, A.add)
-            op("v", "dl", "sj posk", tt, T.dl[:], last, T.posk[:], A.subtract)
-            op("v", "el", "sm dl", tt, T.el[:], lastm, T.dl[:], A.mult)
-            op("v", "posk", "posk el", tt, T.posk[:], T.posk[:], T.el[:], A.add)
-            key = "pl%d" % (k % 2)
-            at = T[key][:, 0:L]
-            op("v", key, "posk kj", ts, at, T.posk[:], kj, None, A.subtract)
-        op("s", "jg0", "h0 " + key, S.activation, T.jg0[:], ind(T.h0, at), COPY)
-        op("v", "cc", "m0 sp " + key, tt, T.cc[:], ind(T.m0, at), T.sp[:], A.is_le)
-        op("s", "jg1", "h1 " + key, S.activation, T.jg1[:], ind(T.h1, at), COPY)
-        op("v", "cc2", "m7 sp " + key, tt, T.cc2[:], ind(T.m7, at), T.sp[:], A.is_le)
-        keep("jg0")
-        op("v", "sm", "rm cc", scan, T.sm[:], T.rm[:], T.cc[:], 0.0, A.mult, A.add)
-        op("v", "sm2", "rm cc2", scan, T.sm2[:], T.rm[:], T.cc2[:], 0.0, A.mult, A.add)
-        op("v", "sk", "kk jg1", scan, T.sk[:], T.kk[:], T.jg1[:], 0.0, A.add, A.max)
-        op("v", "dl", "sj posk", tt, T.dl[:], last, T.posk[:], A.subtract)
-        op("v", "dl2", "sk c0k", tt, T.dl2[:], T.c0k[:], T.sk[:, 15:C:16], A.subtract)
-        op("v", "dl3", "sk sj", tt, T.dl3[:], T.sk[:, 15:C:16], last, A.subtract)
-        op("v", "el", "sm dl", tt, T.el[:], lastm, T.dl[:], A.mult)
-        op("v", "el2", "sm2 dl2", tt, T.el2[:], T.sm2[:, 15:C:16], T.dl2[:], A.mult)
-        op("v", "dl3", "dl3 sm", tt, T.dl3[:], T.dl3[:], lastm, A.mult)
-        op("v", "el2", "el2 sm", tt, T.el2[:], T.el2[:], lastm, A.mult)
-        op("v", "posk", "posk el", tt, T.posk[:], T.posk[:], T.el[:], A.add)
-        op("v", "dl3", "dl3 sj", tt, T.dl3[:], T.dl3[:], last, A.add)
-        op("v", "lstp", "posk kj", ts, lst[:, L:2 * L], T.posk[:], kj, None, A.subtract)
-        op("v", "el2", "el2 dl3", tt, T.el2[:], T.el2[:], T.dl3[:], A.add)
-        op("v", "lstb", "el2 kj", ts, lst[:, 0:L], T.el2[:], kj, None, A.subtract)
-        before("g", ["lstb", "lstp"], [])
+
+        def look(k, i):
+            p, pl, jg, cc = PARTS[i], "pl%d" % (k % 2), "jg%d" % (k % 2), "cc" if k % 2 else "cc2"
+            at = T[pl][:, p[0]:p[1]]
+            op("s", "%s.%d" % (jg, i), "h%d %s.%d" % (k, pl, i), S.activation, cols(T[jg], p), ind(T["h%d" % k], at), COPY)
+            if k == 0:
+                op("s", "jg1.%d" % i, "h1 %s.%d" % (pl, i), S.activation, cols(T.jg1, p), ind(T.h1, at), COPY)
+            op("v", "%s.%d" % (cc, i), "m%d.0 m%d.1 sp %s.%d" % (k, k, pl, i), tt, cols(T[cc], p), ind(T["m%d" % k], at), cols(T.sp, p), A.is_le)
+
+        def bits(k, i):
+            p, cc, ba = PARTS[i], "cc" if k % 2 else "cc2", "ba" if k else "bz"
+            op("v", "%s.%d" % (ba, i), "%s rm %s.%d" % (ba, cc, i), scan, spread3(T[ba], p), cols(T.rm, p), cols(T[cc], p), 0.0, A.mult, A.add)
+
+        def keep(k, i):
+            p, jg, v = PARTS[i], "jg%d" % (k % 2), "v%d" % (k % 2) if k else "vc"
+            op("v", "%s.%d" % (v, i), "kk %s.%d" % (jg, i), scan, spread3(T[v], p), cols(T.kk, p), cols(T[jg], p), 0.0, A.add, A.max)
+
+        def move(k, i):
+            p, v, w = PARTS[i], "v%d" % (k % 2), "v%d" % ((k + 1) % 2)
+            op("v", "%s.%d %sn.%d %sp.%d" % (w, i, w, i, w, i), "ba.%d %s.%d %sn.%d %sp.%d" % (i, v, i, v, i, v, i), scan,
+               three(T[w], p, 0), three(T.ba, p, -2), three(T[v], p, 0), 0.0, A.mult, A.add)
+
+        def place(k, i):
+            p, w, pl = PARTS[i], "v%d" % ((k + 1) % 2), "pl%d" % ((k + 1) % 2)
+            op("v", "%s.%d" % (pl, i), "%sp.%d kj" % (w, i), ts, T[pl][:, p[0]:p[1]], slot(T[w], p, 2), kj, None, A.subtract)
+            if k > 1:
+                op("s", "%sn.%d" % (w, i), "%sp.%d" % (w, i), S.activation, slot(T[w], p, 1), slot(T[w], p, 2), COPY, scale=-1.0)
+
+        for i, p in enumerate(PARTS):
+            src = T.topo[:, 5 * p[0] + 3:5 * p[1]:5]
+            op("s", "v0p.%d" % i, "topo", S.activation, slot(T.v0, p, 2), src, COPY)
+            op("s", "v0n.%d" % i, "topo", S.activation, slot(T.v0, p, 1), src, COPY, scale=-1.0)
+        for k in (4, 3, 2, 1):
+            look(k, 0)
+            if k < 4:
+                move(k + 1, 1)
+            else:
+                for i, p in enumerate(PARTS):
+                    op("v", "vcn.%d" % i, "nno c0k", tt, slot(T.vc, p, 1), T.nno[:, 5 * p[0] + 3:5 * p[1]:5], T.c0k[:, p[0]:p[1]], A.mult)
+            bits(k, 0)
+            if k < 4:
+                place(k + 1, 1)
+            keep(k, 0)
+            look(k, 1)
+            if k == 4:
+                for i, p in enumerate(PARTS):
+                    op("s", "bzn.%d" % i, "bz nno", S.activation, slot(T.bz, p, 1), T.nno[:, 5 * p[0] + 3:5 * p[1]:5], FN.Identity, bias=1.0, scale=-1.0)
+            move(k, 0)
+            bits(k, 1)
+            place(k, 0)
+            keep(k, 1)
+            if k <= 2:
+                op("s", "fz%d" % (2 - k), "b%d" % (4 - k), S.activation, plane(T.fz, 2 - k), bank(4 - k), COPY, scale=0.5)
+
+        def ends(i):
+            p = PARTS[i]
+            return [
+                lambda: op("v", "sj.%d sj" % i, "kk jg1.%d" % i, scan, cols(T.sj, p), cols(T.kk, p), cols(T.jg1, p), 0.0, A.add, A.max),
+                lambda: op("v", "v0n.%d" % i, "vc.%d v0p.%d" % (i, i), tt, slot(T.v0, p, 1), slot(T.vc, p, 0), slot(T.v0, p, 2), A.subtract),
+                lambda: op("v", "vcd.%d" % i, "vc.%d sj.%d" % (i, i), tt, slot(T.vc, p, -1), last(T.sj, p[0], p[1]), slot(T.vc, p, 0), A.subtract),
+                lambda: op("v", "po.%d" % i, "bz.%d bzn.%d v0.%d v0n.%d v0p.%d v0x" % (i, i, i, i, i), scan,
+                           T.po[:, 3 * p[0]:3 * p[1]], three(T.bz, p, -1), three(T.v0, p, 1), 0.0, A.mult, A.add),
+                lambda: op("v", "bo.%d" % i, "bz.%d bzn.%d vc.%d vcd.%d vcn.%d" % (i, i, i, i, i), scan,
+                           T.bo[:, 3 * p[0]:3 * p[1]], three(T.bz, p, -1), three(T.vc, p, -1), 0.0, A.mult, A.add),
+                lambda: op("v", "lstp.%d" % i, "po.%d kj" % i, ts, lst[:, L + p[0]:L + p[1]], T.po[:, 3 * p[0] + 1:3 * p[1]:3], kj, None, A.subtract),
+                lambda: op("v", "lstb.%d" % i, "bo.%d kj" % i, ts, lst[:, p[0]:p[1]], T.bo[:, 3 * p[0] + 2:3 * p[1]:3], kj, None, A.subtract)]
+        ea, eb = ends(0), ends(1)
+        look(0, 0)
+        move(1, 1)
+        bits(0, 0)
+        place(1, 1)
+        keep(0, 0)
+        look(0, 1)
+        for f in ea[:3]:
+            f()
+        bits(0, 1)
+        keep(0, 1)
+        for f in (ea[3], ea[4], eb[0], eb[1], ea[5], eb[2], eb[3], ea[6], eb[4], eb[5], eb[6]):
+            f()
+        wrote["sj"] = wrote["lstb.1"]
+        before("g", ["lstb.0", "lstp.0", "lstb.1", "lstp.1"], [])
         send(nxt, T[ll % t][:, 0:2 * L], lst[:, 0:2 * L], "rs%d" % t)
         bl = lst[:, 0:L]
-        op("s", "jg0", "h0 mtl", S.activation, T.jg0[:], ind(T.h0, T.mtl[:, 0:L]), COPY)
-        for b in range(4):
+        for b in (2, 3):
             op("s", "fz%d" % b, "b%d" % (2 + b), S.activation, plane(T.fz, b), bank(2 + b), COPY, scale=0.5)
-        op("v", "e1", "sca scb lstb", tc, T.e1[:], ind(T.sc, bl))
+        if t == 0:
+            op("v", "mnf", "mtf cl", tt, T.mnf[:], T.mtf[:], T.cl[:], A.min)
+            op("v", "mxf", "mtf cl", tt, T.mxf[:], T.mtf[:], T.cl[:], A.max)
+        op("v", "e1", "sca scb lstb.0 lstb.1", tc, T.e1[:], ind(T.sc, bl))
+        if t == 0:
+            op("v", "mnl", "mnf", tc, T.mnl[:], T.mnf[:])
+            op("v", "mxl", "mxf", tc, T.mxl[:], T.mxf[:])
+        op("v", "s5", "kk jm", scan, T.s5[:], T.kk[:], T.jm[:], 0.0, A.add, A.max)
         op("v", "e2", "e1 mxl", tc, T.e2[:], ind(T.e1, T.mxl[:, 0:L]))
-        op("v", "cc", "e1 e2 mnl", tt, T.cc[:], ind(T.e1, T.mnl[:, 0:L]), T.e2[:], A.is_gt)
-        keep("jg0")
-        op("v", "fmf", "sj fk", tt, T.fmf[:], last, T.fk[:], A.subtract)
+        op("v", "fmf", "s5 fk", tt, T.fmf[:], last(T.s5), T.fk[:], A.subtract)
+        op("v", "cc.0 cc.1", "e1 e2 mnl", tt, T.cc[:], ind(T.e1, T.mnl[:, 0:L]), T.e2[:], A.is_gt)
+        op("v", "dl", "fmf kb2", ts, T.dl[:], T.fmf[:], kb2, None, A.mult)
+        op("v", "sm", "kb cc.0 cc.1", scan, T.sm[:], T.kb[:], T.cc[:], 0.0, A.add, A.max)
+        op("v", "fkx", "fk dl", tt, T.fkx[:], T.fk[:], T.dl[:], A.subtract)
+        op("v", "el", "sm fmf", tt, T.el[:], last(T.sm), T.fmf[:], A.mult)
+        op("v", "fk", "fkx el", tt, T.fk[:], T.fkx[:], T.el[:], A.add)
         if t == 1:
             op("v", "vq", "vt", V.quantize_mx, T.vq[:, 0:128], T.vqs[:, 0:128], T.vt[:, 0:512])
+        op("v", "jl0", "fk kj", ts, jl(0), T.fk[:], kj, None, A.subtract)
+        hops[0], lists[0] = 0, 1
+        if t == 2:
+            hops[0] = lists[0] = 9
+        else:
+            hop()
+            if came is not None:
+                hop()
+                tolist()
         rl = T["rl%d" % t]
         for lo, hi, b in ((0, 160, 0), (160, C, 0), (0, C, 1), (0, C, 2), (0, C, 3)):
             op("s", "zp%d.%d" % (b, lo), "fz%d rl" % b, S.activation, T.zp[:, C * b + lo:C * b + hi],
                ind(T.fz, rl[:, L + lo // 16:L + hi // 16], C * b), COPY)
             op("v", "zt%d.%d" % (b, lo), "fz%d zp%d.%d rl" % (b, b, lo), tt, T.zt[:, 4 * lo + b:4 * hi:4],
                ind(T.fz, rl[:, lo // 16:hi // 16], C * b), T.zp[:, C * b + lo:C * b + hi], A.add)
+        hop()
+        if t == 2:
+            op("s", "n0.0 n0.1", "idt jl0", S.activation, T.n0[:], ind(T.idt, jl(0)), FN.Identity, bias=MID)
+            for i in range(8):
+                store("y", "n0.0", T.nf[i:i + 1, :], T.n0[16 * i:16 * i + 1, :])
         op("v", "zq", "zt0.0 zt0.160 zt1.0 zt2.0 zt3.0", V.quantize_mx, T.zq[:, 0:C], T.zqs[:, 0:C], T.zt[:, 0:B4])
+        tolist()
         hb = [6, 7, 2, 3]
         product(6, T.wl, T.wls, 0, T.zq, T.zqs, "wl wls zq", 0, HALF)
         product(4, T.wl, T.wls, 0, T.zq, T.zqs, "wl wls zq", HALF, C)
@@ -347,23 +469,14 @@ def rank_program(g, core, T, topo):
         op("s", "hh0", "b6", S.activation, T.hh[:, 0:HALF], bank(6, HALF), COPY, scale=0.03125)
         for b in range(1, 4):
             op("s", "hh%d" % b, "b%d" % hb[b], S.activation, plane(T.hh, b), bank(hb[b]), COPY, scale=0.03125)
-        op("v", "sm", "kb cc", scan, T.sm[:], T.kb[:], T.cc[:], 0.0, A.add, A.max)
-        op("v", "bitl", "sm kb2", ts, T.bitl[:], lastm, kb2, None, A.subtract)
-        op("v", "el", "bitl fmf", tt, T.el[:], T.bitl[:], T.fmf[:], A.mult)
+        hop()
         op("v", "hhb", "b4", ts, T.hh[:, HALF:C], bank(4, C - HALF), 0.03125, None, A.mult)
         for b in range(4):
-            op("v", "xt%d" % b, "hh%d fo%d lstb" % (b, b) + (" hhb" if b == 0 else ""), tt, T.xt[:, b:B4:4],
+            op("v", "xt%d" % b, "hh%d fo%d lstb.0 lstb.1" % (b, b) + (" hhb" if b == 0 else ""), tt, T.xt[:, b:B4:4],
                ind(T.hh, bl, C * b), plane(T.fo, b), A.add)
-            if b == 0:
-                op("v", "fk", "fk el", tt, T.fk[:], T.fk[:], T.el[:], A.add)
-            if b == 1:
-                op("v", "jl0", "fk kj", ts, jl(0), T.fk[:], kj, None, A.subtract)
-        hop0()
-        if t < 2:
-            hop(1)
-        else:
-            for i in range(8):
-                store("s", "h0", T.nf[i:i + 1, :], T.h0[16 * i:16 * i + 1, :])
+            if b == 2 and came is None:
+                tolist()
+                hop()
     quantize_x(3)
     product(0, T.vq, T.vqs, 0, T.xq3, T.xs3, "vq xq3", 0, HALF)
     product(7, T.vq, T.vqs, 0, T.xq3, T.xs3, "vq xq3", HALF, C)

@@ -11,6 +11,9 @@ KB = 1024.0
 MID = 144.0
 PARTS = ((0, 10, 32), (10, 18, 592))
 SLOTS = 1024
+RUNS = ((0, 20), (20, 36))
+CUT = 5 * C // 8
+LEAD = 2
 F32, BF, I32, U16, F8, U8, F16 = "float32", "bfloat16", "int32", "uint16", "float8_e4m3fn_x4", "uint8", "float16"
 
 
@@ -22,15 +25,15 @@ def _scratch():
             s[k] = ("sbuf", [128, n], d)
     sb("pidx pi15", 1, I32)
     sb("icol kj kb2", 1, F32)
-    sb("j16 dd pen sc sp e1 e2 yo n0 n1 m0 m1 m2 m3 m4 m5", C, F32)
-    sb("idt kk kb rm cc cc2 sm jg0 jg1 jm h0 h1 h2 h3 h4 h5 h6 h7", C, BF)
+    sb("pen sc sp e1 e2 yo n0 n1 m0 m1 m2 m3 m4 m5", C, F32)
+    sb("j16 dd idt kk kb rm cc cc2 sm jg0 jg1 jm h0 h1 h2 h3 h4 h5 h6 h7", C, BF)
     sb("sj s5 s6 s7", C, F16)
     sb("v0 v1 vc", SLOTS, F16)
     sb("ba bz", SLOTS, BF)
     sb("bt", 64 + 5 * C, BF)
-    sb("top topo nn nno", 5 * L, F16)
+    sb("top topo nn nno five", 5 * L, F16)
     sb("po bo", 3 * L, F16)
-    sb("cl c0k dl el fk fkx fmf mtf mnf mxf", L, F32)
+    sb("cl c0k dl fk fkx fmf mtf mnf mxf", L, F32)
     sb("nxi mti", L, I32)
     sb("mnl mxl mtl pl0 pl1", L, U16)
     sb("jls", 8 * L, U16)
@@ -55,38 +58,20 @@ def _scratch():
 
 
 SCRATCH = _scratch()
-SEMAPHORES = ["sv", "ss", "st", "sg", "ls", "out",
-              "dx", "du", "dv", "dwc", "dws", "dn", "dm"] + [a + str(t) for t in range(3) for a in ("rx", "rs")]
+SEMAPHORES = ["sv", "ss", "st", "sg", "ls", "out", "dx", "du", "dv", "dwc", "dws", "dn", "dm"] + [
+    a + str(t) for t in range(3) for a in ("rx", "ry", "rz", "rs", "rt")]
 
 
 def relay_of(topo, cores, a, b):
     if topo.may_write(a, b):
         return None
-    for q in topo.cores_of(a):
-        if q not in cores and topo.die(q) == topo.die(a) and topo.may_write(q, b):
-            return q
-    return None
-
-
-def targets(topo, cores, core):
-    out = []
-    for d in STEP:
-        for r in range(N):
-            a, b = cores[r], cores[(r + d) % N]
-            q = relay_of(topo, cores, a, b)
-            if a == core:
-                out.append(b if q is None else q)
-            elif q == core:
-                out.append(b)
-    return out
+    q = [q for q in topo.cores_of(a) if q not in cores and topo.die(q) == topo.die(a) and topo.may_write(q, b)]
+    return q[0], q[-1]
 
 
 def rank_program(g, core, T, topo):
     cores = list(T.cores)
     rank = T.rank_of(core)
-    todo = targets(topo, cores, core)
-    if not todo:
-        return
     nsent = [0]
 
     def send(dst, out, src, sem):
@@ -98,15 +83,26 @@ def rank_program(g, core, T, topo):
         for t, d in enumerate(STEP):
             for r in range(N):
                 a, b = cores[r], cores[(r + d) % N]
-                if relay_of(topo, cores, a, b) != core:
+                via = relay_of(topo, cores, a, b)
+                if via is None or core not in via:
                     continue
                 n = len(topo.engines(a, core))
-                g.wait_ge(T.sem["rx%d" % t], 2 * n)
-                send(b, T["lc%d" % t][:, 0:C].bitcast(dt.uint8), T["rc%d" % t][:, 0:C].bitcast(dt.uint8), "rx%d" % t)
-                send(b, T["lp%d" % t][:, 0:C], T["rp%d" % t][:, 0:C], "rx%d" % t)
-                g.wait_ge(T.sem["rs%d" % t], n)
-                send(b, T["rl%d" % t][:, 0:2 * L], T["rr%d" % t][:, 0:2 * L], "rs%d" % t)
-        g.wait_ge(T.sem.ls, nsent[0])
+                lc, rc = T["lc%d" % t], T["rc%d" % t]
+                if core == via[0]:
+                    g.wait_ge(T.sem["rx%d" % t], n)
+                    send(b, lc[:, 0:CUT].bitcast(dt.uint8), rc[:, 0:CUT].bitcast(dt.uint8), "rx%d" % t)
+                if core == via[1]:
+                    g.wait_ge(T.sem["ry%d" % t], n)
+                    send(b, lc[:, CUT:C].bitcast(dt.uint8), rc[:, CUT:C].bitcast(dt.uint8), "rx%d" % t)
+                    g.wait_ge(T.sem["rz%d" % t], n)
+                    send(b, T["lp%d" % t][:, 0:C], T["rp%d" % t][:, 0:C], "rx%d" % t)
+                for i, (lo, hi) in enumerate(RUNS):
+                    if core == via[i]:
+                        sem = ("rs%d", "rt%d")[i] % t
+                        g.wait_ge(T.sem[sem], n)
+                        send(b, T["rl%d" % t][:, lo:hi], T["rr%d" % t][:, lo:hi], sem)
+        if nsent[0]:
+            g.wait_ge(T.sem.ls, nsent[0])
         return
 
     A = AluOpType
@@ -122,6 +118,9 @@ def rank_program(g, core, T, topo):
             queues[q].wait_ge(T.sem[sem], n)
             seen[(q, sem)] = n
 
+    def names(keys):
+        return [k for w in keys.split() for k in ((w[:-1] + ".0", w[:-1] + ".1") if w[-1] == "#" else (w,))]
+
     def before(q, reads, writes):
         need = {}
         for k in reads + writes:
@@ -135,7 +134,7 @@ def rank_program(g, core, T, topo):
             wait(q, s, n)
 
     def op(q, writes, reads, fn, *args, **kw):
-        writes, reads = writes.split(), reads.split()
+        writes, reads = names(writes), names(reads)
         before(q, reads, writes)
         cnt[q] += 1
         fn(*args, **kw).then_inc(T.sem[semname[q]], 1)
@@ -146,7 +145,7 @@ def rank_program(g, core, T, topo):
             readers[k] = {}
 
     V, S, P = g.vector, g.scalar, g.tensor
-    ts, tt, tc, scan = V.tensor_scalar, V.tensor_tensor, V.tensor_copy, V.tensor_tensor_scan
+    ts, tt, tc, scan, act = V.tensor_scalar, V.tensor_tensor, V.tensor_copy, V.tensor_tensor_scan, S.activation
 
     def load(q, name, out, src, sem):
         queues[q].dma_start(out, src).then_inc(T.sem[sem], 16)
@@ -155,47 +154,18 @@ def rank_program(g, core, T, topo):
     nout = [0]
 
     def store(q, reads, out, src):
-        before(q, reads.split(), [])
+        before(q, names(reads), [])
         queues[q].dma_start(out, src).then_inc(T.sem.out, 16)
         nout[0] += 16
 
-    def bank(b, n=C):
-        return T.ps[:, 512 * b:512 * b + n]
+    def bank(b, lo=0, hi=C):
+        return T.ps[:, 512 * b + lo:512 * b + hi]
 
-    load("y", "x0", T.x0[:], T.x[:], "dx")
-    load("s", "nxi", T.nxi[:], T.nx[:], "dn")
-    load("s", "ut", T.ut[:], T.u[:], "du")
-    load("s", "mti", T.mti[:], T.mt[:], "dm")
-    wait("y", "dx", 16)
-    wait("y", "du", 16)
-    load("y", "wl", T.wl[:, 0:512].bitcast(dt.uint8), T.wc[:, 0:2048], "dwc")
-    load("y", "wls", T.wls[:, 0:512], T.ws[:, 0:512], "dws")
-    load("y", "vt", T.vt[:], T.v[:], "dv")
+    def product(b, lhs, ls, a, rhs, rs, reads, lo=0, hi=C):
+        op("t", "b%d" % b, reads, P.matmul_mx, bank(b, 0, hi - lo), lhs[:, a:a + 128], ls[:, a:a + 128], rhs[:, lo:hi], rs[:, lo:hi], True, True)
 
-    op("g", "pidx", "", g.iota, T.pidx[:], [[0, 1]], 0, 1)
-    op("g", "j16", "", g.iota, T.j16[:], [[0, L], [1, 16]], 0, 0, allow_small_or_imprecise_dtypes=True)
-    op("g", "idt", "", g.iota, T.idt[:], [[1, C]], -int(MID), 0, allow_small_or_imprecise_dtypes=True)
-    op("g", "dl", "", g.iota, T.dl[:], [[16, L]], 0, 0, allow_small_or_imprecise_dtypes=True)
-    op("g", "uoi", "", g.iota, T.uoi[:], [[16, 8]], 0, 0)
-    op("v", "ones", "", V.memset, T.ones[:], 1.0)
-    op("g", "wide", "ones", g.affine_select, T.wide[:], T.ones[:], [[-1, 516]], A.is_equal, 0.0, 3, 4)
-    op("v", "ba", "", V.memset, T.ba[:], 0.0)
-    op("v", "pi15", "pidx", ts, T.pi15[:], T.pidx[:], 15, None, A.bitwise_and)
-    op("v", "bz", "", V.memset, T.bz[:], 0.0)
-    op("v", "icol", "pi15", tc, T.icol[:], T.pi15[:])
-    op("v", "bt", "", V.memset, T.bt[:, 75 + 64:64 + 5 * C:80], 0.0)
-    op("v", "kb2", "icol", ts, T.kb2[:], T.icol[:], 15.0, 2.0, A.is_lt, A.mult)
-    op("v", "dd", "j16 icol", ts, T.dd[:], T.j16[:], T.icol[:, 0:1], None, A.subtract)
-    op("v", "kj", "kb2", ts, T.kj[:], T.kb2[:], KB / 2, MID, A.mult, A.subtract)
-    op("v", "m0", "dd", ts, T.m0[:], T.dd[:], 0.0, -4.0 * KB, A.is_equal, A.mult)
-    op("v", "m1", "dd", ts, T.m1[:], T.dd[:], 1.0, KB, A.is_equal, A.mult)
-    op("v", "cl", "dl icol", ts, T.cl[:], T.dl[:], T.icol[:, 0:1], None, A.add)
-    op("v", "jl0", "nxi", tc, T.jls[:, 0:L], T.nxi[:])
-    op("v", "kk", "m0 m1", tt, T.kk[:], T.m0[:], T.m1[:], A.add)
-    op("v", "fkx", "nxi", tc, T.fkx[:], T.nxi[:])
-    kj, kb2 = T.kj[:, 0:1], T.kb2[:, 0:1]
-    op("v", "c0k", "cl kj", ts, T.c0k[:], T.cl[:], kj, None, A.add)
-    op("v", "fk", "fkx kj", ts, T.fk[:], T.fkx[:], kj, None, A.add)
+    def plane(buf, b, lo=0, hi=C):
+        return buf[:, C * b + lo:C * b + hi]
 
     def last(buf, lo=0, hi=L):
         return buf[:, 16 * lo + 15:16 * hi:16]
@@ -205,6 +175,15 @@ def rank_program(g, core, T, topo):
 
     def jl(k, lo=0, hi=L):
         return T.jls[:, L * k + lo:L * k + hi]
+
+    def cols(buf, part):
+        return buf[:, 16 * part[0]:16 * part[1]]
+
+    def plist(buf, i):
+        return buf[:, 0:10] if i == 0 else buf[:, 28:36]
+
+    def blist(buf, i):
+        return buf[:, 10:28] if i is None else buf[:, 10:20] if i == 0 else buf[:, 20:28]
 
     def spread3(buf, part):
         lo, hi, a = part
@@ -218,18 +197,26 @@ def rank_program(g, core, T, topo):
         lo, hi, a = part
         return buf[:, a + 45 + 16 * i:a + 45 + 16 * i + 16 * (3 * (hi - lo) - 1) + 1:16]
 
-    def cols(buf, part):
-        return buf[:, 16 * part[0]:16 * part[1]]
+    pa, pb = PARTS
+    kj, kb2 = T.kj[:, 0:1], T.kb2[:, 0:1]
+
+    def key(writes, reads, out, src):
+        op("v", writes, reads + " kj", ts, out, src, kj, None, A.subtract)
 
     hops, lists = [0], [1]
 
-    def hop():
+    def hop(shared=False):
         k = hops[0]
-        if k > 7:
+        if k > 7 or lists[0] < min(k, 6):
             return
         hops[0] += 1
         w, l = ("idt", 0) if k == 0 else ("h6", 5) if k == 7 else ("h%d" % (k - 1), k - 1)
-        op("s", "h%d" % k, "%s jl%d" % (w, l), S.activation, T["h%d" % k][:], ind(T[w], jl(l)), COPY)
+        h, reads = "h%d" % k, "%s# jl%d" % (w, l)
+        if shared:
+            op("s", h + ".1", reads, act, cols(T[h], pb), ind(T[w], jl(l, pb[0], pb[1])), COPY)
+            op("v", h + ".0", reads, tc, cols(T[h], pa), ind(T[w], jl(l, pa[0], pa[1])))
+        else:
+            op("s", h + "#", reads, act, T[h][:], ind(T[w], jl(l)), COPY)
 
     def tolist():
         k = lists[0]
@@ -237,255 +224,306 @@ def rank_program(g, core, T, topo):
             return
         lists[0] += 1
         sj = "s%d" % k if k >= 5 else "sj"
-        op("v", sj, "kk h%d" % k, scan, T[sj][:], T.kk[:], T["h%d" % k][:], 0.0, A.add, A.max)
-        op("v", "jl%d" % k, sj + " kj", ts, jl(k), last(T[sj]), kj, None, A.subtract)
+        op("v", sj, "kk h%d#" % k, scan, T[sj][:], T.kk[:], T["h%d" % k][:], 0.0, A.add, A.max)
+        key("jl%d" % k, sj, jl(k), last(T[sj]))
 
     def quantize_x(t):
-        src = "x0" if t == 0 else "xt"
-        op("v", "xq%d" % t, "xt0 xt1 xt2 xt3" if t else "x0", V.quantize_mx,
-           T["xq%d" % t][:, 0:C], T["xs%d" % t][:, 0:C], T[src][:, 0:B4])
+        op("v", "xq%d" % t, "xt0# xt1# xt2# xt3#" if t else "x0", V.quantize_mx,
+           T["xq%d" % t][:, 0:C], T["xs%d" % t][:, 0:C], T["xt" if t else "x0"][:, 0:B4])
 
-    op("s", "e1", "dd", S.activation, T.e1[:], T.dd[:], FN.Abs)
-    op("s", "rm", "j16", S.activation, T.rm[:], T.j16[:], FN.Sign)
-    op("s", "e2", "e1", S.activation, T.e2[:], T.e1[:], FN.Relu, bias=1.0, scale=-1.0)
-    hop()
-    op("s", "pen", "e2", S.activation, T.pen[:], T.e2[:], FN.Identity, bias=-BIG, scale=2.0 * BIG)
-    hop()
-    op("s", "kb", "kk", S.activation, T.kb[:], T.kk[:], COPY, scale=2.0 / KB)
-    op("v", "uoff", "uoi", tc, T.uoff[:], T.uoi[:])
-    for p in PARTS:
-        op("v", "ba", "", V.memset, slot(T.ba, p, -1), 1.0)
+    load("y", "x0", T.x0[:], T.x[:], "dx")
+    load("s", "nxi", T.nxi[:], T.nx[:], "dn")
+    load("s", "ut", T.ut[:], T.u[:], "du")
+    load("s", "mti", T.mti[:], T.mt[:], "dm")
+    wait("y", "dx", 16)
+    wait("y", "du", 16)
+    load("y", "wl", T.wl[:, 0:512].bitcast(dt.uint8), T.wc[:, 0:2048], "dwc")
+    load("y", "wls", T.wls[:, 0:512], T.ws[:, 0:512], "dws")
+    load("y", "vt", T.vt[:], T.v[:], "dv")
+
+    op("g", "pidx", "", g.iota, T.pidx[:], [[0, 1]], 0, 1)
+    op("g", "j16", "", g.iota, T.j16[:], [[0, L], [1, 16]], 0, 0, allow_small_or_imprecise_dtypes=True)
+    op("v", "ones", "", V.memset, T.ones[:], 1.0)
+    op("g", "wide", "ones", g.affine_select, T.wide[:], T.ones[:], [[-1, 516]], A.is_equal, 0.0, 3, 4)
+    op("g", "dl", "", g.iota, T.dl[:], [[16, L]], 0, 0, allow_small_or_imprecise_dtypes=True)
+    op("g", "uoi", "", g.iota, T.uoi[:], [[16, 8]], 0, 0)
+    op("v", "pi15", "pidx", ts, T.pi15[:], T.pidx[:], 15, None, A.bitwise_and)
+    op("v", "icol", "pi15", tc, T.icol[:], T.pi15[:])
+    op("v", "idt#", "ones", scan, T.idt[:], T.ones[:, 0:C], T.ones[:, 0:C], -MID - 1.0, A.add, A.mult)
+    op("v", "kb2", "icol", ts, T.kb2[:], T.icol[:], 15.0, 2.0, A.is_lt, A.mult)
+    op("v", "dd", "j16 icol", ts, T.dd[:], T.j16[:], T.icol[:, 0:1], None, A.subtract)
+    op("v", "kj", "kb2", ts, T.kj[:], T.kb2[:], KB / 2, MID, A.mult, A.subtract)
+    op("v", "cc#", "dd", ts, T.cc[:], T.dd[:], 0.0, -4.0 * KB, A.is_equal, A.mult)
+    op("v", "cc2#", "dd", ts, T.cc2[:], T.dd[:], 1.0, KB, A.is_equal, A.mult)
+    op("v", "kk", "cc# cc2#", tt, T.kk[:], T.cc[:], T.cc2[:], A.add)
+    op("s", "top", "ones", act, T.top[:], T.ones[:, 0:5 * L], COPY, scale=0.0)
+    op("s", "nn", "ones", act, T.nn[:], T.ones[:, 0:5 * L], COPY, scale=0.0)
     a, b = [p[2] + 45 + 48 * (p[1] - p[0]) for p in PARTS]
-    op("v", "v0x", "ones", tc, T.v0[:, a:b + 1:b - a], T.ones[:, 0:2])
-    op("v", "top", "ones", ts, T.top[:], T.ones[:, 0:5 * L], 0.0, None, A.mult)
-    op("v", "nn", "ones", ts, T.nn[:], T.ones[:, 0:5 * L], 0.0, None, A.mult)
+    op("s", "v0x", "ones", act, T.v0[:, a:b + 1:b - a], T.ones[:, 0:2], COPY)
+    op("s", "bt", "ones kb2", act, T.bt[:, 75:75 + 80 * L - 15:16], T.ones[:, 0:5 * L], COPY, scale=kb2)
+    op("s", "rm", "j16", act, T.rm[:], T.j16[:], FN.Sign)
+    op("s", "nn", "ones", act, T.nn[:, 4:5 * L:5], T.ones[:, 0:L], COPY)
+    op("s", "e1#", "dd", act, T.e1[:], T.dd[:], FN.Abs)
+    op("s", "e2#", "e1#", act, T.e2[:], T.e1[:], FN.Relu, bias=1.0, scale=-1.0)
+    op("s", "pen", "e2#", act, T.pen[:], T.e2[:], FN.Identity, bias=-BIG, scale=2.0 * BIG)
+
+    def units(ks):
+        for k in ks:
+            op("v", "ec%d" % k, "wide", V.quantize_mx, T.ec[:, 128 * k:128 * k + 128], T.ecs[:, 128 * k:128 * k + 128], T.wide[:, 3 - k:515 - k])
+    op("v", "jl0", "nxi", tc, jl(0), T.nxi[:])
+    units((0, 1))
+    hop(True)
+    op("v", "uoff", "uoi", tc, T.uoff[:], T.uoi[:])
+    units((2, 3))
+    hop(True)
+    op("v", "cl", "dl icol", ts, T.cl[:], T.dl[:], T.icol[:, 0:1], None, A.add)
+    quantize_x(0)
     tolist()
-    hop()
-    op("v", "nn", "ones", tc, T.nn[:, 4:5 * L:5], T.ones[:, 0:L])
+    hop(True)
     op("v", "uq", "ut", V.quantize_mx, T.uq[:, 0:128], T.uqs[:, 0:128], T.ut[:, 0:512])
-    tolist()
+    op("v", "c0k", "cl kj", ts, T.c0k[:], T.cl[:], kj, None, A.add)
     op("v", "u2", "uq uoff", tc, T.u2[:, 0:128].bitcast(dt.uint32), T.uq[:, 0:128].bitcast(dt.uint32).indirect(T.uoff[:, 0:8]))
-    op("s", "u2s", "uq uoff", S.activation, T.u2s[:, 0:128], T.uqs[:, 0:128].indirect(T.uoff[:, 0:8]), COPY)
+    op("s", "u2s", "uq uoff", act, T.u2s[:, 0:128], T.uqs[:, 0:128].indirect(T.uoff[:, 0:8]), COPY)
+    op("v", "fkx", "nxi", tc, T.fkx[:], T.nxi[:])
+    tolist()
+    op("v", "fk", "fkx kj", ts, T.fk[:], T.fkx[:], kj, None, A.add)
+    op("s", "top3", "top c0k", act, T.top[:, 3:5 * L:5], T.c0k[:], COPY)
     hop()
-
-    def product(b, lhs, ls, a, rhs, rs, reads, lo=0, hi=C):
-        op("t", "b%d" % b, reads, P.matmul_mx, bank(b, hi - lo), lhs[:, a:a + 128], ls[:, a:a + 128], rhs[:, lo:hi], rs[:, lo:hi], True, True)
-
-    def plane(buf, b):
-        return buf[:, C * b:C * b + C]
 
     for t, d in enumerate(STEP):
         to, frm = cores[(rank + d) % N], cores[(rank - d) % N]
         via, came = relay_of(topo, cores, core, to), relay_of(topo, cores, frm, core)
-        xq, xs = T["xq%d" % t], T["xs%d" % t]
-        quantize_x(t)
+        xq, xs, lst, rl = T["xq%d" % t], T["xs%d" % t], T["lst%d" % t], T["rl%d" % t]
+        if t:
+            quantize_x(t)
         before("g", ["xq%d" % t], [])
-        nxt, lc, lp, ll = (to, "lc%d", "lp%d", "rl%d") if via is None else (via, "rc%d", "rp%d", "rr%d")
-        send(nxt, T[lc % t][:, 0:C].bitcast(dt.uint8), xq[:, 0:C].bitcast(dt.uint8), "rx%d" % t)
-        send(nxt, T[lp % t][:, 0:C], xs[:, 0:C], "rx%d" % t)
-        n = len(topo.engines(frm if came is None else came, core))
-        wrote["land"], wrote["rl"] = ("rx%d" % t, 2 * n), ("rs%d" % t, n)
+        if via is None:
+            send(to, T["lc%d" % t][:, 0:C].bitcast(dt.uint8), xq[:, 0:C].bitcast(dt.uint8), "rx%d" % t)
+            send(to, T["lp%d" % t][:, 0:C], xs[:, 0:C], "rx%d" % t)
+        else:
+            send(via[1], T["rc%d" % t][:, CUT:C].bitcast(dt.uint8), xq[:, CUT:C].bitcast(dt.uint8), "ry%d" % t)
+            send(via[0], T["rc%d" % t][:, 0:CUT].bitcast(dt.uint8), xq[:, 0:CUT].bitcast(dt.uint8), "rx%d" % t)
+            send(via[1], T["rp%d" % t][:, 0:C], xs[:, 0:C], "rz%d" % t)
+        if t == 0:
+            for p in PARTS:
+                for name, buf, i, c in (("ba", T.ba, -2, 0), ("bb", T.ba, -1, 1), ("bz", T.bz, -1, 0)):
+                    op("g", name, "", g.iota, slot(buf, p, i), [[0, p[1] - p[0]]], c, 0, allow_small_or_imprecise_dtypes=True)
+        n = len(topo.engines(frm if came is None else came[0], core))
+        wrote["land"] = ("rx%d" % t, (2 if came is None else 3) * n)
+        wrote["rl.0"], wrote["rl.1"] = ("rs%d" % t, n), ("rt%d" % t, n)
         product(0, T.u2, T.u2s, 0, xq, xs, "u2 u2s xq%d" % t, 0, HALF)
         product(7, T.u2, T.u2s, 0, xq, xs, "u2 u2s xq%d" % t, HALF, C)
         product(1, T.u2, T.u2s, 0, xq, xs, "u2 u2s xq%d" % t)
         tolist()
-        op("s", "sca", "b0", S.activation, T.sc[:, 0:HALF], bank(0, HALF), COPY)
-        op("v", "scb", "b7", tc, T.sc[:, HALF:C], bank(7, C - HALF))
-        op("s", "n0.0 n0.1", "sca scb jl0", S.activation, T.n0[:], ind(T.sc, jl(0)), COPY)
-        op("v", "m0.0 m0.1", "sca scb jl0", tc, T.m0[:], ind(T.sc, jl(0)))
+        op("s", "sc.0", "b0", act, T.sc[:, 0:HALF], bank(0, 0, HALF), COPY)
+        op("v", "sc.1", "b7", tc, T.sc[:, HALF:C], bank(7, 0, C - HALF))
+        for i, p in enumerate(PARTS):
+            op("v", "m0.%d" % i, "sc# jl0", tc, cols(T.m0, p), ind(T.sc, jl(0, p[0], p[1])))
         for k in range(5):
             m, m2, n1, n2 = "m%d" % k, "m%d" % (k + 1), "n%d" % (k % 2), "n%d" % ((k + 1) % 2)
             hop()
             for i, p in enumerate(PARTS):
-                op("v", "%s.%d" % (m2, i), "%s.0 %s.1 jl%d %s.%d" % (m, m, k, n1, i), tt,
-                   cols(T[m2], p), ind(T[m], jl(k, p[0], p[1])), cols(T[n1], p), A.max)
+                if k == 0:
+                    op("v", "m1.%d" % i, "sc# jl1 m0.%d" % i, tt, cols(T.m1, p), ind(T.sc, jl(1, p[0], p[1])), cols(T.m0, p), A.max)
+                else:
+                    op("v", "%s.%d" % (m2, i), "%s# jl%d %s.%d" % (m, k, n1, i), tt,
+                       cols(T[m2], p), ind(T[m], jl(k, p[0], p[1])), cols(T[n1], p), A.max)
                 if k < 4:
-                    op("s", "%s.%d" % (n2, i), "%s.%d" % (m2, i), S.activation, cols(T[n2], p), cols(T[m2], p), COPY)
+                    op("s", "%s.%d" % (n2, i), "%s.%d" % (m2, i), act, cols(T[n2], p), cols(T[m2], p), COPY)
             tolist()
-            if k < 4:
-                if t == 0:
-                    op("v", "ec%d" % k, "wide", V.quantize_mx, T.ec[:, 128 * k:128 * k + 128], T.ecs[:, 128 * k:128 * k + 128], T.wide[:, 3 - k:515 - k])
-                product(2 + k, T.ec, T.ecs, 128 * k, xq, xs, "ec%d xq%d" % (k, t))
-            if k == 3:
+            if k == 2:
                 op("v", "sp", "b1 pen", tt, T.sp[:], bank(1), T.pen[:], A.min)
+            if t == 0 and k == 3:
+                op("v", "mtf", "mti", tc, T.mtf[:], T.mti[:])
+                op("v", "mtl", "mti", tc, T.mtl[:], T.mti[:])
+                op("s", "kb", "kk", act, T.kb[:], T.kk[:], COPY, scale=2.0 / KB)
+            if t == 0 and k == 4:
+                op("v", "mnf", "mtf cl", tt, T.mnf[:], T.mtf[:], T.cl[:], A.min)
+                op("v", "mxf", "mtf cl", tt, T.mxf[:], T.mtf[:], T.cl[:], A.max)
+            if k < 4:
+                product(2 + k, T.ec, T.ecs, 128 * k, xq, xs, "ec%d xq%d" % (k, t))
         assert hops[0] == 8 and lists[0] == 8
-        if t == 0:
-            op("v", "mtf", "mti", tc, T.mtf[:], T.mti[:])
-            op("v", "mtl", "mti", tc, T.mtl[:], T.mti[:])
-        bt = T.bt
-        op("v", "cc.0 cc.1", "m5.0 m5.1 b1", tt, T.cc[:], T.m5[:], bank(1), A.is_le)
+
+        def topbit(e, cc):
+            op("v", "bt%d" % e, "kb %s#" % cc, scan, T.bt[:, 16 * e:16 * e + 5 * C:5], T.kb[:], T[cc][:], 0.0, A.add, A.max)
+        op("s", "n0#", "m5# jl5", act, T.n0[:], ind(T.m5, jl(5)), COPY)
+        op("s", "n1#", "m5# jl7", act, T.n1[:], ind(T.m5, jl(7)), COPY)
+        for b in range(4):
+            op("s", "fo%d" % b, "b%d" % (2 + b), act, plane(T.fo, b), bank(2 + b), COPY)
+            product(2 + b, T.ec, T.ecs, 128 * b, T["lc%d" % t], T["lp%d" % t], "land ec%d" % b)
         op("v", "top2", "top s5 c0k", tt, T.top[:, 2:5 * L:5], last(T.s5), T.c0k[:], A.subtract)
         op("v", "top1", "top s5 s6", tt, T.top[:, 1:5 * L:5], last(T.s6), last(T.s5), A.subtract)
-        op("v", "cc2.0 cc2.1", "m5.0 m5.1 jl5 sp", tt, T.cc2[:], ind(T.m5, jl(5)), T.sp[:], A.is_le)
-        op("v", "sm", "kb cc.0 cc.1", scan, T.sm[:], T.kb[:], T.cc[:], 0.0, A.add, A.max)
+        op("v", "cc2#", "m5# jl6 sc#", tt, T.cc2[:], ind(T.m5, jl(6)), T.sc[:], A.is_le)
+        op("v", "cc#", "m5# b1", tt, T.cc[:], T.m5[:], bank(1), A.is_le)
+        topbit(1, "cc2")
+        op("v", "cc2#", "n0# b1", tt, T.cc2[:], T.n0[:], bank(1), A.is_le)
+        topbit(3, "cc")
+        topbit(2, "cc2")
         op("v", "top0", "top s6 s7", tt, T.top[:, 0:5 * L:5], last(T.s7), last(T.s6), A.subtract)
-        op("v", "bt2", "bt rm cc2.0 cc2.1", scan, bt[:, 32:32 + 5 * C:5], T.rm[:], T.cc2[:], 0.0, A.mult, A.add)
-        op("v", "cc.0 cc.1", "m5.0 m5.1 jl6 sp", tt, T.cc[:], ind(T.m5, jl(6)), T.sp[:], A.is_le)
-        op("v", "bt3", "bt sm kb2", ts, bt[:, 75 + 48:64 + 5 * C:80], last(T.sm), kb2, None, A.subtract)
-        if t == 0:
-            op("v", "top3", "top c0k", tc, T.top[:, 3:5 * L:5], T.c0k[:])
-        op("v", "cc2.0 cc2.1", "m5.0 m5.1 jl7 sp", tt, T.cc2[:], ind(T.m5, jl(7)), T.sp[:], A.is_le)
-        op("v", "bt1", "bt rm cc.0 cc.1", scan, bt[:, 16:16 + 5 * C:5], T.rm[:], T.cc[:], 0.0, A.mult, A.add)
-        op("v", "bt0", "bt rm cc2.0 cc2.1", scan, bt[:, 0:5 * C:5], T.rm[:], T.cc2[:], 0.0, A.mult, A.add)
-        five = bt[:, 75:75 + 16 * (5 * L - 1) + 1:16]
-        op("v", "topo", "bt0 bt1 bt2 bt3 top0 top1 top2 top3", scan, T.topo[:], five, T.top[:], 0.0, A.mult, A.add)
-        op("v", "nno", "bt0 bt1 bt2 bt3 nn", scan, T.nno[:], five, T.nn[:], 1.0, A.mult, A.add)
-        op("v", "pl0.0 pl0.1", "topo kj", ts, T.pl0[:], T.topo[:, 3:5 * L:5], kj, None, A.subtract)
-        for b in range(4):
-            op("s", "fo%d" % b, "b%d" % (2 + b), S.activation, plane(T.fo, b), bank(2 + b), COPY)
-            product(2 + b, T.ec, T.ecs, 128 * b, T["lc%d" % t], T["lp%d" % t], "land ec%d" % b)
-        op("s", "jm", "h0 mtl", S.activation, T.jm[:], ind(T.h0, T.mtl[:, 0:L]), COPY)
-        lst = T["lst%d" % t]
+        op("v", "five", "bt bt1 bt2 bt3 kb2", ts, T.five[:], T.bt[:, 75:75 + 80 * L - 15:16], kb2, None, A.subtract)
+        op("v", "sm", "n1# b1", tt, T.sm[:], T.n1[:], bank(1), A.is_le)
+        op("v", "topo", "five top0 top1 top2 top3", scan, T.topo[:], T.five[:], T.top[:], 0.0, A.mult, A.add)
+        op("v", "s7", "kb sm", scan, T.s7[:], T.kb[:], T.sm[:], 0.0, A.add, A.max)
+        key("pl0#", "topo", T.pl0[:], T.topo[:, 3:5 * L:5])
+        op("v", "five", "s7 kb2", ts, T.five[:, 0:5 * L:5], last(T.s7), kb2, None, A.subtract)
 
-        def look(k, i):
-            p, pl, jg, cc = PARTS[i], "pl%d" % (k % 2), "jg%d" % (k % 2), "cc" if k % 2 else "cc2"
-            at = T[pl][:, p[0]:p[1]]
-            op("s", "%s.%d" % (jg, i), "h%d %s.%d" % (k, pl, i), S.activation, cols(T[jg], p), ind(T["h%d" % k], at), COPY)
-            if k == 0:
-                op("s", "jg1.%d" % i, "h1 %s.%d" % (pl, i), S.activation, cols(T.jg1, p), ind(T.h1, at), COPY)
-            op("v", "%s.%d" % (cc, i), "m%d.0 m%d.1 sp %s.%d" % (k, k, pl, i), tt, cols(T[cc], p), ind(T["m%d" % k], at), cols(T.sp, p), A.is_le)
+        def nones(i):
+            p = lo, hi, _ = PARTS[i]
+            none = T.nno[:, 5 * lo + 3:5 * hi:5]
+            op("s", "bzn.%d" % i, "bz nno", act, slot(T.bz, p, 1), none, FN.Identity, bias=1.0, scale=-1.0)
+            op("v", "vcn.%d" % i, "nno c0k", tt, slot(T.vc, p, 1), none, T.c0k[:, lo:hi], A.mult)
+        aside = {0: lambda: op("v", "nno", "five nn", scan, T.nno[:], T.five[:], T.nn[:], 1.0, A.mult, A.add),
+                 1: lambda: nones(0), 2: lambda: nones(1),
+                 18: lambda: op("s", "jm", "h0# mtl", act, T.jm[:], ind(T.h0, T.mtl[:, 0:L]), COPY)}
 
-        def bits(k, i):
-            p, cc, ba = PARTS[i], "cc" if k % 2 else "cc2", "ba" if k else "bz"
-            op("v", "%s.%d" % (ba, i), "%s rm %s.%d" % (ba, cc, i), scan, spread3(T[ba], p), cols(T.rm, p), cols(T[cc], p), 0.0, A.mult, A.add)
+        def search(i):
+            p = lo, hi, _ = PARTS[i]
+            here = T.topo[:, 5 * lo + 3:5 * hi:5]
 
-        def keep(k, i):
-            p, jg, v = PARTS[i], "jg%d" % (k % 2), "v%d" % (k % 2) if k else "vc"
-            op("v", "%s.%d" % (v, i), "kk %s.%d" % (jg, i), scan, spread3(T[v], p), cols(T.kk, p), cols(T[jg], p), 0.0, A.add, A.max)
+            def mine(keys):
+                return keys.replace("@", ".%d" % i)
 
-        def move(k, i):
-            p, v, w = PARTS[i], "v%d" % (k % 2), "v%d" % ((k + 1) % 2)
-            op("v", "%s.%d %sn.%d %sp.%d" % (w, i, w, i, w, i), "ba.%d %s.%d %sn.%d %sp.%d" % (i, v, i, v, i, v, i), scan,
-               three(T[w], p, 0), three(T.ba, p, -2), three(T[v], p, 0), 0.0, A.mult, A.add)
+            def o(q, writes, reads, *args, **kw):
+                return lambda: op(q, mine(writes), mine(reads), *args, **kw)
 
-        def place(k, i):
-            p, w, pl = PARTS[i], "v%d" % ((k + 1) % 2), "pl%d" % ((k + 1) % 2)
-            op("v", "%s.%d" % (pl, i), "%sp.%d kj" % (w, i), ts, T[pl][:, p[0]:p[1]], slot(T[w], p, 2), kj, None, A.subtract)
-            if k > 1:
-                op("s", "%sn.%d" % (w, i), "%sp.%d" % (w, i), S.activation, slot(T[w], p, 1), slot(T[w], p, 2), COPY, scale=-1.0)
+            def both(*fs):
+                return lambda: [f() for f in fs]
 
-        for i, p in enumerate(PARTS):
-            src = T.topo[:, 5 * p[0] + 3:5 * p[1]:5]
-            op("s", "v0p.%d" % i, "topo", S.activation, slot(T.v0, p, 2), src, COPY)
-            op("s", "v0n.%d" % i, "topo", S.activation, slot(T.v0, p, 1), src, COPY, scale=-1.0)
-        for k in (4, 3, 2, 1):
-            look(k, 0)
-            if k < 4:
-                move(k + 1, 1)
-            else:
-                for i, p in enumerate(PARTS):
-                    op("v", "vcn.%d" % i, "nno c0k", tt, slot(T.vc, p, 1), T.nno[:, 5 * p[0] + 3:5 * p[1]:5], T.c0k[:, p[0]:p[1]], A.mult)
-            bits(k, 0)
-            if k < 4:
-                place(k + 1, 1)
-            keep(k, 0)
-            look(k, 1)
-            if k == 4:
-                for i, p in enumerate(PARTS):
-                    op("s", "bzn.%d" % i, "bz nno", S.activation, slot(T.bz, p, 1), T.nno[:, 5 * p[0] + 3:5 * p[1]:5], FN.Identity, bias=1.0, scale=-1.0)
-            move(k, 0)
-            bits(k, 1)
-            place(k, 0)
-            keep(k, 1)
-            if k <= 2:
-                op("s", "fz%d" % (2 - k), "b%d" % (4 - k), S.activation, plane(T.fz, 2 - k), bank(4 - k), COPY, scale=0.5)
+            def offsets(writes, reads, out, src):
+                return lambda: key(mine(writes), mine(reads), out, src)
+            out = []
+            for k in (4, 3, 2, 1, 0):
+                pl, jg, cc, v = "pl%d" % (k % 2), "jg%d" % (k % 2), "cc" if k % 2 else "cc2", "v%d" % (k % 2) if k else "vc"
+                at, ba, w, pw = T[pl][:, lo:hi], "ba" if k else "bz", "v%d" % ((k + 1) % 2), "pl%d" % ((k + 1) % 2)
+                look = [o("s", jg + "@", "h%d# %s@" % (k, pl), act, cols(T[jg], p), ind(T["h%d" % k], at), COPY)]
+                if k == 0:
+                    look.append(o("s", "jg1@", "h1# %s@" % pl, act, cols(T.jg1, p), ind(T.h1, at), COPY))
+                look.append(o("v", cc + "@", "m%d# sp %s@" % (k, pl), tt, cols(T[cc], p), ind(T["m%d" % k], at), cols(T.sp, p), A.is_le))
+                if 0 < k < 4:
+                    look.append(o("s", v + "n@", v + "p@", act, slot(T[v], p, 1), slot(T[v], p, 2), COPY, scale=-1.0))
+                if k == 4:
+                    look.append(o("s", "v0p@", "topo", act, slot(T.v0, p, 2), here, COPY))
+                    look.append(o("s", "v0n@", "topo", act, slot(T.v0, p, 1), here, COPY, scale=-1.0))
+                out += [both(*look),
+                        o("v", ba + "@", "%s bb rm %s@" % (ba, cc), scan, spread3(T[ba], p), cols(T.rm, p), cols(T[cc], p), 0.0, A.mult, A.add),
+                        o("v", v + "@", "kk %s@" % jg, scan, spread3(T[v], p), cols(T.kk, p), cols(T[jg], p), 0.0, A.add, A.max)]
+                if k:
+                    out += [o("v", "%s@ %sn@ %sp@" % (w, w, w), "ba@ %s@ %sn@ %sp@" % (v, v, v), scan,
+                              three(T[w], p, 0), three(T.ba, p, -2), three(T[v], p, 0), 0.0, A.mult, A.add),
+                            offsets(pw + "@", w + "p@", T[pw][:, lo:hi], slot(T[w], p, 2))]
 
-        def ends(i):
-            p = PARTS[i]
-            return [
-                lambda: op("v", "sj.%d sj" % i, "kk jg1.%d" % i, scan, cols(T.sj, p), cols(T.kk, p), cols(T.jg1, p), 0.0, A.add, A.max),
-                lambda: op("v", "v0n.%d" % i, "vc.%d v0p.%d" % (i, i), tt, slot(T.v0, p, 1), slot(T.vc, p, 0), slot(T.v0, p, 2), A.subtract),
-                lambda: op("v", "vcd.%d" % i, "vc.%d sj.%d" % (i, i), tt, slot(T.vc, p, -1), last(T.sj, p[0], p[1]), slot(T.vc, p, 0), A.subtract),
-                lambda: op("v", "po.%d" % i, "bz.%d bzn.%d v0.%d v0n.%d v0p.%d v0x" % (i, i, i, i, i), scan,
-                           T.po[:, 3 * p[0]:3 * p[1]], three(T.bz, p, -1), three(T.v0, p, 1), 0.0, A.mult, A.add),
-                lambda: op("v", "bo.%d" % i, "bz.%d bzn.%d vc.%d vcd.%d vcn.%d" % (i, i, i, i, i), scan,
-                           T.bo[:, 3 * p[0]:3 * p[1]], three(T.bz, p, -1), three(T.vc, p, -1), 0.0, A.mult, A.add),
-                lambda: op("v", "lstp.%d" % i, "po.%d kj" % i, ts, lst[:, L + p[0]:L + p[1]], T.po[:, 3 * p[0] + 1:3 * p[1]:3], kj, None, A.subtract),
-                lambda: op("v", "lstb.%d" % i, "bo.%d kj" % i, ts, lst[:, p[0]:p[1]], T.bo[:, 3 * p[0] + 2:3 * p[1]:3], kj, None, A.subtract)]
-        ea, eb = ends(0), ends(1)
-        look(0, 0)
-        move(1, 1)
-        bits(0, 0)
-        place(1, 1)
-        keep(0, 0)
-        look(0, 1)
-        for f in ea[:3]:
-            f()
-        bits(0, 1)
-        keep(0, 1)
-        for f in (ea[3], ea[4], eb[0], eb[1], ea[5], eb[2], eb[3], ea[6], eb[4], eb[5], eb[6]):
-            f()
-        wrote["sj"] = wrote["lstb.1"]
-        before("g", ["lstb.0", "lstp.0", "lstb.1", "lstp.1"], [])
-        send(nxt, T[ll % t][:, 0:2 * L], lst[:, 0:2 * L], "rs%d" % t)
-        bl = lst[:, 0:L]
-        for b in (2, 3):
-            op("s", "fz%d" % b, "b%d" % (2 + b), S.activation, plane(T.fz, b), bank(2 + b), COPY, scale=0.5)
-        if t == 0:
-            op("v", "mnf", "mtf cl", tt, T.mnf[:], T.mtf[:], T.cl[:], A.min)
-            op("v", "mxf", "mtf cl", tt, T.mxf[:], T.mtf[:], T.cl[:], A.max)
-        op("v", "e1", "sca scb lstb.0 lstb.1", tc, T.e1[:], ind(T.sc, bl))
+            def follow():
+                (a, b), sem = RUNS[i], ("rs%d", "rt%d")[i] % t
+                before("g", names(mine("lstb@ lstp@")), [])
+                if via is None:
+                    send(to, rl[:, a:b], lst[:, a:b], sem)
+                else:
+                    send(via[i], T["rr%d" % t][:, a:b], lst[:, a:b], sem)
+            return out + [
+                o("v", "sk@", "kk jg1@", scan, cols(T.s6, p), cols(T.kk, p), cols(T.jg1, p), 0.0, A.add, A.max),
+                o("v", "v0n@", "vc@ v0p@", tt, slot(T.v0, p, 1), slot(T.vc, p, 0), slot(T.v0, p, 2), A.subtract),
+                o("v", "vcd@", "vc@ sk@", tt, slot(T.vc, p, -1), last(T.s6, lo, hi), slot(T.vc, p, 0), A.subtract),
+                o("v", "po@", "bz@ bzn@ v0@ v0n@ v0p@ v0x", scan, T.po[:, 3 * lo:3 * hi], three(T.bz, p, -1), three(T.v0, p, 1), 0.0, A.mult, A.add),
+                o("v", "bo@", "bz@ bzn@ vc@ vcd@ vcn@", scan, T.bo[:, 3 * lo:3 * hi], three(T.bz, p, -1), three(T.vc, p, -1), 0.0, A.mult, A.add),
+                offsets("lstp@", "po@", plist(lst, i), T.po[:, 3 * lo + 1:3 * hi:3]),
+                both(offsets("lstb@", "bo@", blist(lst, i), T.bo[:, 3 * lo + 2:3 * hi:3]), follow)]
+
+        sa, sb = search(0), search(1)
+        for j in range(len(sa) + LEAD):
+            if j < len(sa):
+                sa[j]()
+            if j >= LEAD:
+                sb[j - LEAD]()
+            if j in aside:
+                aside[j]()
+        wrote["s6"] = wrote["lstb.1"]
+
+        def unpack(planes):
+            for b in planes:
+                op("s", "fz%d" % b, "b%d" % (2 + b), act, plane(T.fz, b), bank(2 + b), COPY, scale=0.5)
+        unpack((0, 1))
+        op("v", "e1.0", "sc# lstb.0", tc, cols(T.e1, pa), ind(T.sc, blist(lst, 0)))
         if t == 0:
             op("v", "mnl", "mnf", tc, T.mnl[:], T.mnf[:])
             op("v", "mxl", "mxf", tc, T.mxl[:], T.mxf[:])
+        op("s", "e1.1", "sc# lstb.1", act, cols(T.e1, pb), ind(T.sc, blist(lst, 1)), COPY)
         op("v", "s5", "kk jm", scan, T.s5[:], T.kk[:], T.jm[:], 0.0, A.add, A.max)
-        op("v", "e2", "e1 mxl", tc, T.e2[:], ind(T.e1, T.mxl[:, 0:L]))
+        op("s", "e2.1", "e1# mxl", act, cols(T.e2, pb), ind(T.e1, T.mxl[:, pb[0]:pb[1]]), COPY)
+        op("v", "e2.0", "e1# mxl", tc, cols(T.e2, pa), ind(T.e1, T.mxl[:, pa[0]:pa[1]]))
+        unpack((2, 3))
         op("v", "fmf", "s5 fk", tt, T.fmf[:], last(T.s5), T.fk[:], A.subtract)
-        op("v", "cc.0 cc.1", "e1 e2 mnl", tt, T.cc[:], ind(T.e1, T.mnl[:, 0:L]), T.e2[:], A.is_gt)
+        op("v", "cc#", "e1# e2# mnl", tt, T.cc[:], ind(T.e1, T.mnl[:, 0:L]), T.e2[:], A.is_gt)
         op("v", "dl", "fmf kb2", ts, T.dl[:], T.fmf[:], kb2, None, A.mult)
-        op("v", "sm", "kb cc.0 cc.1", scan, T.sm[:], T.kb[:], T.cc[:], 0.0, A.add, A.max)
-        op("v", "fkx", "fk dl", tt, T.fkx[:], T.fk[:], T.dl[:], A.subtract)
-        op("v", "el", "sm fmf", tt, T.el[:], last(T.sm), T.fmf[:], A.mult)
-        op("v", "fk", "fkx el", tt, T.fk[:], T.fkx[:], T.el[:], A.add)
         if t == 1:
             op("v", "vq", "vt", V.quantize_mx, T.vq[:, 0:128], T.vqs[:, 0:128], T.vt[:, 0:512])
-        op("v", "jl0", "fk kj", ts, jl(0), T.fk[:], kj, None, A.subtract)
-        hops[0], lists[0] = 0, 1
-        if t == 2:
-            hops[0] = lists[0] = 9
+        rest = [lambda: (op("v", "sm", "kb cc#", scan, T.sm[:], T.kb[:], T.cc[:], 0.0, A.add, A.max),
+                         op("v", "fkx", "fk dl", tt, T.fkx[:], T.fk[:], T.dl[:], A.subtract)),
+                lambda: op("v", "dl", "sm fmf", tt, T.dl[:], last(T.sm), T.fmf[:], A.mult),
+                lambda: op("v", "fk", "fkx dl", tt, T.fk[:], T.fkx[:], T.dl[:], A.add),
+                lambda: key("jl0", "fk", jl(0), T.fk[:])]
+
+        def followers(shared):
+            if t < 2:
+                hops[0], lists[0] = 0, 1
+                hop(shared)
+                hop(shared)
+            else:
+                op("s", "n0#", "idt# jl0", act, T.n0[:], ind(T.idt, jl(0)), FN.Identity, bias=MID)
+                for i in range(8):
+                    store("y", "n0#", T.nf[i:i + 1, :], T.n0[16 * i:16 * i + 1, :])
+        if came is not None:
+            while rest:
+                rest.pop(0)()
+            followers(True)
+            tolist()
+        for i, p in enumerate(PARTS):
+            lo, hi = 16 * p[0], 16 * p[1]
+            for b in range(4):
+                op("s", "zp%d.%d" % (b, i), "fz%d rl.%d" % (b, i), act, plane(T.zp, b, lo, hi), ind(T.fz, plist(rl, i), C * b), COPY)
+                op("v", "zt%d.%d" % (b, i), "fz%d zp%d.%d rl.%d" % (b, b, i, i), tt, T.zt[:, 4 * lo + b:4 * hi:4],
+                   ind(T.fz, blist(rl, i), C * b), plane(T.zp, b, lo, hi), A.add)
+                if rest:
+                    rest.pop(0)()
+        if came is None:
+            followers(False)
         else:
             hop()
-            if came is not None:
-                hop()
-                tolist()
-        rl = T["rl%d" % t]
-        for lo, hi, b in ((0, 160, 0), (160, C, 0), (0, C, 1), (0, C, 2), (0, C, 3)):
-            op("s", "zp%d.%d" % (b, lo), "fz%d rl" % b, S.activation, T.zp[:, C * b + lo:C * b + hi],
-               ind(T.fz, rl[:, L + lo // 16:L + hi // 16], C * b), COPY)
-            op("v", "zt%d.%d" % (b, lo), "fz%d zp%d.%d rl" % (b, b, lo), tt, T.zt[:, 4 * lo + b:4 * hi:4],
-               ind(T.fz, rl[:, lo // 16:hi // 16], C * b), T.zp[:, C * b + lo:C * b + hi], A.add)
-        hop()
-        if t == 2:
-            op("s", "n0.0 n0.1", "idt jl0", S.activation, T.n0[:], ind(T.idt, jl(0)), FN.Identity, bias=MID)
-            for i in range(8):
-                store("y", "n0.0", T.nf[i:i + 1, :], T.n0[16 * i:16 * i + 1, :])
-        op("v", "zq", "zt0.0 zt0.160 zt1.0 zt2.0 zt3.0", V.quantize_mx, T.zq[:, 0:C], T.zqs[:, 0:C], T.zt[:, 0:B4])
+        op("v", "zq", "zt0# zt1# zt2# zt3#", V.quantize_mx, T.zq[:, 0:C], T.zqs[:, 0:C], T.zt[:, 0:B4])
         tolist()
         hb = [6, 7, 2, 3]
         product(6, T.wl, T.wls, 0, T.zq, T.zqs, "wl wls zq", 0, HALF)
         product(4, T.wl, T.wls, 0, T.zq, T.zqs, "wl wls zq", HALF, C)
         for b in range(1, 4):
             product(hb[b], T.wl, T.wls, 128 * b, T.zq, T.zqs, "wl wls zq")
-        op("s", "hh0", "b6", S.activation, T.hh[:, 0:HALF], bank(6, HALF), COPY, scale=0.03125)
+        op("s", "hh0", "b6", act, T.hh[:, 0:HALF], bank(6, 0, HALF), COPY, scale=0.03125)
         for b in range(1, 4):
-            op("s", "hh%d" % b, "b%d" % hb[b], S.activation, plane(T.hh, b), bank(hb[b]), COPY, scale=0.03125)
-        hop()
-        op("v", "hhb", "b4", ts, T.hh[:, HALF:C], bank(4, C - HALF), 0.03125, None, A.mult)
-        for b in range(4):
-            op("v", "xt%d" % b, "hh%d fo%d lstb.0 lstb.1" % (b, b) + (" hhb" if b == 0 else ""), tt, T.xt[:, b:B4:4],
-               ind(T.hh, bl, C * b), plane(T.fo, b), A.add)
-            if b == 2 and came is None:
-                tolist()
-                hop()
-    quantize_x(3)
-    product(0, T.vq, T.vqs, 0, T.xq3, T.xs3, "vq xq3", 0, HALF)
-    product(7, T.vq, T.vqs, 0, T.xq3, T.xs3, "vq xq3", HALF, C)
-    store("y", "xq3", T.oc[:, 0:B4], T.xq3[:, 0:C].bitcast(dt.uint8))
-    op("s", "yoa", "b0", S.activation, T.yo[:, 0:HALF], bank(0, HALF), COPY)
-    op("v", "yob", "b7", tc, T.yo[:, HALF:C], bank(7, C - HALF))
+            op("s", "hh%d" % b, "b%d" % hb[b], act, plane(T.hh, b), bank(hb[b]), COPY, scale=0.03125)
+        op("v", "hhb", "b4", ts, T.hh[:, HALF:C], bank(4, 0, C - HALF), 0.03125, None, A.mult)
+
+        def state(i, b):
+            lo, hi = (0, C) if i is None else (16 * PARTS[i][0], 16 * PARTS[i][1])
+            at, me = blist(lst, i), "#" if i is None else ".%d" % i
+            if b < 4:
+                op("v", "xt%d%s" % (b, me), "hh%d fo%d hhb lstb%s" % (b, b, me), tt, T.xt[:, 4 * lo + b:4 * hi:4],
+                   ind(T.hh, at, C * b), plane(T.fo, b, lo, hi), A.add)
+            else:
+                op("v", "xq3" + me, " ".join("xt%d%s" % (b, me) for b in range(4)), V.quantize_mx, T.xq3[:, lo:hi], T.xs3[:, lo:hi], T.xt[:, 4 * lo:4 * hi])
+                product(i, T.vq, T.vqs, 0, T.xq3, T.xs3, "vq xq3" + me, lo, hi)
+                store("y", "xq3" + me, T.oc[:, 4 * lo:4 * hi], T.xq3[:, lo:hi].bitcast(dt.uint8))
+                op("s", "yo" + me, "b%d" % i, act, T.yo[:, lo:hi], bank(i, 0, hi - lo), COPY)
+                store("s", "yo" + me, T.y[:, lo:hi], T.yo[:, lo:hi])
+        if t < 2:
+            hop()
+            for b in range(4):
+                state(None, b)
+                if b == 2:
+                    tolist()
+                    hop()
+        else:
+            for i, b in ((0, 0), (0, 1), (0, 2), (0, 3), (1, 0), (0, 4), (1, 1), (1, 2), (1, 3), (1, 4)):
+                state(i, b)
     for k in range(4):
-        store("s", "xq3", T.osc[4 * k:4 * k + 4, 0:C], T.xs3[32 * k:32 * k + 4, 0:C])
-    store("y", "yoa yob", T.y[:], T.yo[:])
+        store("y", "xq3#", T.osc[4 * k:4 * k + 4, 0:C], T.xs3[32 * k:32 * k + 4, 0:C])
     for q in ("v", "s", "t", "g"):
         wait("g", semname[q], cnt[q])
     wait("g", "ls", nsent[0])

@@ -13,8 +13,25 @@ PARTS = ((0, 10, 32), (10, 18, 592))
 SLOTS = 1024
 RUNS = ((0, 20), (20, 36))
 CUT = 5 * C // 8
-LEAD = 2
 F32, BF, I32, U16, F8, U8, F16 = "float32", "bfloat16", "int32", "uint16", "float8_e4m3fn_x4", "uint8", "float16"
+
+MEANS = "pick " + "add pick " * 7 + "add"
+ORDER = {
+    "first": ["list0 e0 hop2 e1 e2 e3 hop2 uoff keep cl list leave unpack hop2 uq u2s c0k fkx keep u2 list fk hopv keep",
+              "scores scb sca top3 list maxa maxb hop",
+              "maxa copya keep maxb list copyb hop", "maxa copya maxb copyb keep list hop", "maxa copya maxb own copyb hop keep",
+              "maxa copya maxb copyb keep mtf mtl list list kb", "maxa maxb mnf mxf"],
+    "near": ["swap", MEANS, "hop layer hop2 h0a keep h0b h h list hop x h x x keep list x hop",
+             "leave keep scores list unpack sca scb maxa maxb hop",
+             "maxa copya keep maxb list copyb hop2", "maxa maxb keep vcopya list copyb hop", "maxa maxb vcopya copyb own hop",
+             "maxa copya maxb keep copyb keep list", "maxa list maxb"],
+    "far": ["swap hop2 hop2 keep list", MEANS, "layer hop keep h0b h0a h h list hop x h x x keep list x",
+            "leave hop scores keep unpack list sca scb maxa maxb hop",
+            "maxa copya keep maxb list copyb hop", "maxa copya maxb copyb keep hop", "maxa copya maxb own copyb keep",
+            "maxa copya maxb copyb list list", "maxa maxb"],
+    "last": ["swap nf vpick pick " + "add pick " * 6 + "add add", "layer h0b h0a h h h", "xa " * 5, "xb " * 5],
+}
+TURNS = "a b none a a nonea noneb " + "b a b a b b a b a a " * 4 + "mates " + "a a b " * 3 + "a " + "b " * 6
 
 
 def _scratch():
@@ -144,6 +161,18 @@ def rank_program(g, core, T, topo):
             wrote[k] = (semname[q], cnt[q])
             readers[k] = {}
 
+    def later(*args, **kw):
+        return lambda: op(*args, **kw)
+
+    def series(calls):
+        calls = list(calls)
+        return lambda: calls.pop(0)()
+
+    def run(order, *tables):
+        calls = {k: f for x in tables for k, f in x.items()}
+        for name in " ".join(order).split():
+            calls[name]()
+
     V, S, P = g.vector, g.scalar, g.tensor
     ts, tt, tc, scan, act = V.tensor_scalar, V.tensor_tensor, V.tensor_copy, V.tensor_tensor_scan, S.activation
 
@@ -157,6 +186,12 @@ def rank_program(g, core, T, topo):
         before(q, names(reads), [])
         queues[q].dma_start(out, src).then_inc(T.sem.out, 16)
         nout[0] += 16
+
+    def copy(q, writes, reads, out, src):
+        if q == "s":
+            op("s", writes, reads, act, out, src, COPY)
+        else:
+            op("v", writes, reads, tc, out, src)
 
     def bank(b, lo=0, hi=C):
         return T.ps[:, 512 * b + lo:512 * b + hi]
@@ -203,33 +238,34 @@ def rank_program(g, core, T, topo):
     def key(writes, reads, out, src):
         op("v", writes, reads + " kj", ts, out, src, kj, None, A.subtract)
 
-    hops, lists = [0], [1]
+    made = {"hops": 0, "kept": 1, "lists": 1}
 
-    def hop(shared=False):
-        k = hops[0]
-        if k > 7 or lists[0] < min(k, 6):
-            return
-        hops[0] += 1
+    def hop(by):
+        k = made["hops"]
+        assert k <= 7 and made["lists"] >= min(k, 6)
+        made["hops"] += 1
         w, l = ("idt", 0) if k == 0 else ("h6", 5) if k == 7 else ("h%d" % (k - 1), k - 1)
-        h, reads = "h%d" % k, "%s# jl%d" % (w, l)
-        if shared:
-            op("s", h + ".1", reads, act, cols(T[h], pb), ind(T[w], jl(l, pb[0], pb[1])), COPY)
-            op("v", h + ".0", reads, tc, cols(T[h], pa), ind(T[w], jl(l, pa[0], pa[1])))
+        if len(by) == 1:
+            copy(by, "h%d#" % k, "%s# jl%d" % (w, l), T["h%d" % k][:], ind(T[w], jl(l)))
         else:
-            op("s", h + "#", reads, act, T[h][:], ind(T[w], jl(l)), COPY)
+            for q, i in (("s", 1), ("v", 0)):
+                p = PARTS[i]
+                copy(q, "h%d.%d" % (k, i), "%s# jl%d" % (w, l), cols(T["h%d" % k], p), ind(T[w], jl(l, p[0], p[1])))
 
-    def tolist():
-        k = lists[0]
-        if k >= hops[0]:
-            return
-        lists[0] += 1
+    def keep():
+        k = made["kept"]
+        assert k < made["hops"] and (k == made["lists"] or k > 5)
+        made["kept"] += 1
         sj = "s%d" % k if k >= 5 else "sj"
         op("v", sj, "kk h%d#" % k, scan, T[sj][:], T.kk[:], T["h%d" % k][:], 0.0, A.add, A.max)
-        key("jl%d" % k, sj, jl(k), last(T[sj]))
 
-    def quantize_x(t):
-        op("v", "xq%d" % t, "xt0# xt1# xt2# xt3#" if t else "x0", V.quantize_mx,
-           T["xq%d" % t][:, 0:C], T["xs%d" % t][:, 0:C], T["xt" if t else "x0"][:, 0:B4])
+    def tolist():
+        k = made["lists"]
+        assert k < made["kept"]
+        made["lists"] += 1
+        sj = "s%d" % k if k >= 5 else "sj"
+        key("jl%d" % k, sj, jl(k), last(T[sj]))
+    hopping = dict(hop=lambda: hop("s"), hopv=lambda: hop("v"), hop2=lambda: hop("sv"), keep=keep, list=tolist)
 
     load("y", "x0", T.x0[:], T.x[:], "dx")
     load("s", "nxi", T.nxi[:], T.nx[:], "dn")
@@ -266,83 +302,89 @@ def rank_program(g, core, T, topo):
     op("s", "e1#", "dd", act, T.e1[:], T.dd[:], FN.Abs)
     op("s", "e2#", "e1#", act, T.e2[:], T.e1[:], FN.Relu, bias=1.0, scale=-1.0)
     op("s", "pen", "e2#", act, T.pen[:], T.e2[:], FN.Identity, bias=-BIG, scale=2.0 * BIG)
+    once = dict(
+        list0=later("v", "jl0", "nxi", tc, jl(0), T.nxi[:]),
+        fkx=later("v", "fkx", "nxi", tc, T.fkx[:], T.nxi[:]),
+        fk=later("v", "fk", "fkx kj", ts, T.fk[:], T.fkx[:], kj, None, A.add),
+        cl=later("v", "cl", "dl icol", ts, T.cl[:], T.dl[:], T.icol[:, 0:1], None, A.add),
+        c0k=later("v", "c0k", "cl kj", ts, T.c0k[:], T.cl[:], kj, None, A.add),
+        top3=later("s", "top3", "top c0k", act, T.top[:, 3:5 * L:5], T.c0k[:], COPY),
+        uoff=later("v", "uoff", "uoi", tc, T.uoff[:], T.uoi[:]),
+        uq=later("v", "uq", "ut", V.quantize_mx, T.uq[:, 0:128], T.uqs[:, 0:128], T.ut[:, 0:512]),
+        u2=later("v", "u2", "uq uoff", tc, T.u2[:, 0:128].bitcast(dt.uint32), T.uq[:, 0:128].bitcast(dt.uint32).indirect(T.uoff[:, 0:8])),
+        u2s=later("s", "u2s", "uq uoff", act, T.u2s[:, 0:128], T.uqs[:, 0:128].indirect(T.uoff[:, 0:8]), COPY),
+        kb=later("s", "kb", "kk", act, T.kb[:], T.kk[:], COPY, scale=2.0 / KB),
+        mtf=later("v", "mtf", "mti", tc, T.mtf[:], T.mti[:]),
+        mtl=later("v", "mtl", "mti", tc, T.mtl[:], T.mti[:]),
+        mnf=later("v", "mnf", "mtf cl", tt, T.mnf[:], T.mtf[:], T.cl[:], A.min),
+        mxf=later("v", "mxf", "mtf cl", tt, T.mxf[:], T.mtf[:], T.cl[:], A.max))
+    for k in range(4):
+        once["e%d" % k] = later("v", "ec%d" % k, "wide", V.quantize_mx, T.ec[:, 128 * k:128 * k + 128], T.ecs[:, 128 * k:128 * k + 128], T.wide[:, 3 - k:515 - k])
 
-    def units(ks):
-        for k in ks:
-            op("v", "ec%d" % k, "wide", V.quantize_mx, T.ec[:, 128 * k:128 * k + 128], T.ecs[:, 128 * k:128 * k + 128], T.wide[:, 3 - k:515 - k])
-    op("v", "jl0", "nxi", tc, jl(0), T.nxi[:])
-    units((0, 1))
-    hop(True)
-    op("v", "uoff", "uoi", tc, T.uoff[:], T.uoi[:])
-    units((2, 3))
-    hop(True)
-    op("v", "cl", "dl icol", ts, T.cl[:], T.dl[:], T.icol[:, 0:1], None, A.add)
-    quantize_x(0)
-    tolist()
-    hop(True)
-    op("v", "uq", "ut", V.quantize_mx, T.uq[:, 0:128], T.uqs[:, 0:128], T.ut[:, 0:512])
-    op("v", "c0k", "cl kj", ts, T.c0k[:], T.cl[:], kj, None, A.add)
-    op("v", "u2", "uq uoff", tc, T.u2[:, 0:128].bitcast(dt.uint32), T.uq[:, 0:128].bitcast(dt.uint32).indirect(T.uoff[:, 0:8]))
-    op("s", "u2s", "uq uoff", act, T.u2s[:, 0:128], T.uqs[:, 0:128].indirect(T.uoff[:, 0:8]), COPY)
-    op("v", "fkx", "nxi", tc, T.fkx[:], T.nxi[:])
-    tolist()
-    op("v", "fk", "fkx kj", ts, T.fk[:], T.fkx[:], kj, None, A.add)
-    op("s", "top3", "top c0k", act, T.top[:, 3:5 * L:5], T.c0k[:], COPY)
-    hop()
+    def head(t):
+        to = cores[(rank + STEP[t]) % N]
+        via = relay_of(topo, cores, core, to)
+        xq, xs = T["xq%d" % t], T["xs%d" % t]
 
+        def leave():
+            op("v", "xq%d" % t, "xt0# xt1# xt2# xt3#" if t else "x0", V.quantize_mx, xq[:, 0:C], xs[:, 0:C], T["xt" if t else "x0"][:, 0:B4])
+            before("g", ["xq%d" % t], [])
+            if via is None:
+                send(to, T["lc%d" % t][:, 0:C].bitcast(dt.uint8), xq[:, 0:C].bitcast(dt.uint8), "rx%d" % t)
+                send(to, T["lp%d" % t][:, 0:C], xs[:, 0:C], "rx%d" % t)
+            else:
+                send(via[1], T["rc%d" % t][:, CUT:C].bitcast(dt.uint8), xq[:, CUT:C].bitcast(dt.uint8), "ry%d" % t)
+                send(via[0], T["rc%d" % t][:, 0:CUT].bitcast(dt.uint8), xq[:, 0:CUT].bitcast(dt.uint8), "rx%d" % t)
+                send(via[1], T["rp%d" % t][:, 0:C], xs[:, 0:C], "rz%d" % t)
+            if t == 0:
+                for p in PARTS:
+                    for name, buf, i, c in (("ba", T.ba, -2, 0), ("bb", T.ba, -1, 1), ("bz", T.bz, -1, 0)):
+                        op("g", name, "", g.iota, slot(buf, p, i), [[0, p[1] - p[0]]], c, 0, allow_small_or_imprecise_dtypes=True)
+
+        def scores():
+            product(0, T.u2, T.u2s, 0, xq, xs, "u2 u2s xq%d" % t, 0, HALF)
+            product(7, T.u2, T.u2s, 0, xq, xs, "u2 u2s xq%d" % t, HALF, C)
+            product(1, T.u2, T.u2s, 0, xq, xs, "u2 u2s xq%d" % t)
+
+        def unpack():
+            for k in range(4):
+                product(2 + k, T.ec, T.ecs, 128 * k, xq, xs, "ec%d xq%d" % (k, t))
+        level, copied = [0, 0], [1, 1]
+
+        def maximum(i):
+            k, p = level[i], PARTS[i]
+            level[i] += 1
+            assert made["lists"] >= max(k, 2) and min(level) >= k and copied[i] >= k
+            if k == 0:
+                op("v", "m0.%d" % i, "sc# jl0", tc, cols(T.m0, p), ind(T.sc, jl(0, p[0], p[1])))
+            elif k == 1:
+                op("v", "m1.%d" % i, "sc# jl1 m0.%d" % i, tt, cols(T.m1, p), ind(T.sc, jl(1, p[0], p[1])), cols(T.m0, p), A.max)
+            else:
+                m, n1 = "m%d" % (k - 1), "n%d" % ((k - 1) % 2)
+                op("v", "m%d.%d" % (k, i), "%s# jl%d %s.%d" % (m, k - 1, n1, i), tt,
+                   cols(T["m%d" % k], p), ind(T[m], jl(k - 1, p[0], p[1])), cols(T[n1], p), A.max)
+
+        def twin(q, i):
+            k, p = copied[i], PARTS[i]
+            assert level[i] == k + 1
+            copied[i] += 1
+            copy(q, "n%d.%d" % (k % 2, i), "m%d.%d" % (k, i), cols(T["n%d" % (k % 2)], p), cols(T["m%d" % k], p))
+        return dict(
+            leave=leave, scores=scores, unpack=unpack, maxa=lambda: maximum(0), maxb=lambda: maximum(1),
+            copya=lambda: twin("s", 0), copyb=lambda: twin("s", 1), vcopya=lambda: twin("v", 0), vcopyb=lambda: twin("v", 1),
+            sca=later("s", "sc.0", "b0", act, T.sc[:, 0:HALF], bank(0, 0, HALF), COPY),
+            scb=later("v", "sc.1", "b7", tc, T.sc[:, HALF:C], bank(7, 0, C - HALF)),
+            own=later("v", "sp", "b1 pen", tt, T.sp[:], bank(1), T.pen[:], A.min))
+
+    run(ORDER["first"], hopping, once, head(0))
     for t, d in enumerate(STEP):
         to, frm = cores[(rank + d) % N], cores[(rank - d) % N]
         via, came = relay_of(topo, cores, core, to), relay_of(topo, cores, frm, core)
-        xq, xs, lst, rl = T["xq%d" % t], T["xs%d" % t], T["lst%d" % t], T["rl%d" % t]
-        if t:
-            quantize_x(t)
-        before("g", ["xq%d" % t], [])
-        if via is None:
-            send(to, T["lc%d" % t][:, 0:C].bitcast(dt.uint8), xq[:, 0:C].bitcast(dt.uint8), "rx%d" % t)
-            send(to, T["lp%d" % t][:, 0:C], xs[:, 0:C], "rx%d" % t)
-        else:
-            send(via[1], T["rc%d" % t][:, CUT:C].bitcast(dt.uint8), xq[:, CUT:C].bitcast(dt.uint8), "ry%d" % t)
-            send(via[0], T["rc%d" % t][:, 0:CUT].bitcast(dt.uint8), xq[:, 0:CUT].bitcast(dt.uint8), "rx%d" % t)
-            send(via[1], T["rp%d" % t][:, 0:C], xs[:, 0:C], "rz%d" % t)
-        if t == 0:
-            for p in PARTS:
-                for name, buf, i, c in (("ba", T.ba, -2, 0), ("bb", T.ba, -1, 1), ("bz", T.bz, -1, 0)):
-                    op("g", name, "", g.iota, slot(buf, p, i), [[0, p[1] - p[0]]], c, 0, allow_small_or_imprecise_dtypes=True)
+        lst, rl = T["lst%d" % t], T["rl%d" % t]
         n = len(topo.engines(frm if came is None else came[0], core))
         wrote["land"] = ("rx%d" % t, (2 if came is None else 3) * n)
         wrote["rl.0"], wrote["rl.1"] = ("rs%d" % t, n), ("rt%d" % t, n)
-        product(0, T.u2, T.u2s, 0, xq, xs, "u2 u2s xq%d" % t, 0, HALF)
-        product(7, T.u2, T.u2s, 0, xq, xs, "u2 u2s xq%d" % t, HALF, C)
-        product(1, T.u2, T.u2s, 0, xq, xs, "u2 u2s xq%d" % t)
-        tolist()
-        op("s", "sc.0", "b0", act, T.sc[:, 0:HALF], bank(0, 0, HALF), COPY)
-        op("v", "sc.1", "b7", tc, T.sc[:, HALF:C], bank(7, 0, C - HALF))
-        for i, p in enumerate(PARTS):
-            op("v", "m0.%d" % i, "sc# jl0", tc, cols(T.m0, p), ind(T.sc, jl(0, p[0], p[1])))
-        for k in range(5):
-            m, m2, n1, n2 = "m%d" % k, "m%d" % (k + 1), "n%d" % (k % 2), "n%d" % ((k + 1) % 2)
-            hop()
-            for i, p in enumerate(PARTS):
-                if k == 0:
-                    op("v", "m1.%d" % i, "sc# jl1 m0.%d" % i, tt, cols(T.m1, p), ind(T.sc, jl(1, p[0], p[1])), cols(T.m0, p), A.max)
-                else:
-                    op("v", "%s.%d" % (m2, i), "%s# jl%d %s.%d" % (m, k, n1, i), tt,
-                       cols(T[m2], p), ind(T[m], jl(k, p[0], p[1])), cols(T[n1], p), A.max)
-                if k < 4:
-                    op("s", "%s.%d" % (n2, i), "%s.%d" % (m2, i), act, cols(T[n2], p), cols(T[m2], p), COPY)
-            tolist()
-            if k == 2:
-                op("v", "sp", "b1 pen", tt, T.sp[:], bank(1), T.pen[:], A.min)
-            if t == 0 and k == 3:
-                op("v", "mtf", "mti", tc, T.mtf[:], T.mti[:])
-                op("v", "mtl", "mti", tc, T.mtl[:], T.mti[:])
-                op("s", "kb", "kk", act, T.kb[:], T.kk[:], COPY, scale=2.0 / KB)
-            if t == 0 and k == 4:
-                op("v", "mnf", "mtf cl", tt, T.mnf[:], T.mtf[:], T.cl[:], A.min)
-                op("v", "mxf", "mtf cl", tt, T.mxf[:], T.mtf[:], T.cl[:], A.max)
-            if k < 4:
-                product(2 + k, T.ec, T.ecs, 128 * k, xq, xs, "ec%d xq%d" % (k, t))
-        assert hops[0] == 8 and lists[0] == 8
+        assert made["lists"] == 8
 
         def topbit(e, cc):
             op("v", "bt%d" % e, "kb %s#" % cc, scan, T.bt[:, 16 * e:16 * e + 5 * C:5], T.kb[:], T[cc][:], 0.0, A.add, A.max)
@@ -353,9 +395,9 @@ def rank_program(g, core, T, topo):
             product(2 + b, T.ec, T.ecs, 128 * b, T["lc%d" % t], T["lp%d" % t], "land ec%d" % b)
         op("v", "top2", "top s5 c0k", tt, T.top[:, 2:5 * L:5], last(T.s5), T.c0k[:], A.subtract)
         op("v", "top1", "top s5 s6", tt, T.top[:, 1:5 * L:5], last(T.s6), last(T.s5), A.subtract)
-        op("v", "cc2#", "m5# jl6 sc#", tt, T.cc2[:], ind(T.m5, jl(6)), T.sc[:], A.is_le)
+        op("v", "jg0#", "m5# jl6 sc#", tt, T.jg0[:], ind(T.m5, jl(6)), T.sc[:], A.is_le)
         op("v", "cc#", "m5# b1", tt, T.cc[:], T.m5[:], bank(1), A.is_le)
-        topbit(1, "cc2")
+        topbit(1, "jg0")
         op("v", "cc2#", "n0# b1", tt, T.cc2[:], T.n0[:], bank(1), A.is_le)
         topbit(3, "cc")
         topbit(2, "cc2")
@@ -372,9 +414,6 @@ def rank_program(g, core, T, topo):
             none = T.nno[:, 5 * lo + 3:5 * hi:5]
             op("s", "bzn.%d" % i, "bz nno", act, slot(T.bz, p, 1), none, FN.Identity, bias=1.0, scale=-1.0)
             op("v", "vcn.%d" % i, "nno c0k", tt, slot(T.vc, p, 1), none, T.c0k[:, lo:hi], A.mult)
-        aside = {0: lambda: op("v", "nno", "five nn", scan, T.nno[:], T.five[:], T.nn[:], 1.0, A.mult, A.add),
-                 1: lambda: nones(0), 2: lambda: nones(1),
-                 18: lambda: op("s", "jm", "h0# mtl", act, T.jm[:], ind(T.h0, T.mtl[:, 0:L]), COPY)}
 
         def search(i):
             p = lo, hi, _ = PARTS[i]
@@ -384,7 +423,7 @@ def rank_program(g, core, T, topo):
                 return keys.replace("@", ".%d" % i)
 
             def o(q, writes, reads, *args, **kw):
-                return lambda: op(q, mine(writes), mine(reads), *args, **kw)
+                return later(q, mine(writes), mine(reads), *args, **kw)
 
             def both(*fs):
                 return lambda: [f() for f in fs]
@@ -419,109 +458,95 @@ def rank_program(g, core, T, topo):
                     send(to, rl[:, a:b], lst[:, a:b], sem)
                 else:
                     send(via[i], T["rr%d" % t][:, a:b], lst[:, a:b], sem)
-            return out + [
+            return series(out + [
                 o("v", "sk@", "kk jg1@", scan, cols(T.s6, p), cols(T.kk, p), cols(T.jg1, p), 0.0, A.add, A.max),
                 o("v", "v0n@", "vc@ v0p@", tt, slot(T.v0, p, 1), slot(T.vc, p, 0), slot(T.v0, p, 2), A.subtract),
                 o("v", "vcd@", "vc@ sk@", tt, slot(T.vc, p, -1), last(T.s6, lo, hi), slot(T.vc, p, 0), A.subtract),
                 o("v", "po@", "bz@ bzn@ v0@ v0n@ v0p@ v0x", scan, T.po[:, 3 * lo:3 * hi], three(T.bz, p, -1), three(T.v0, p, 1), 0.0, A.mult, A.add),
                 o("v", "bo@", "bz@ bzn@ vc@ vcd@ vcn@", scan, T.bo[:, 3 * lo:3 * hi], three(T.bz, p, -1), three(T.vc, p, -1), 0.0, A.mult, A.add),
                 offsets("lstp@", "po@", plist(lst, i), T.po[:, 3 * lo + 1:3 * hi:3]),
-                both(offsets("lstb@", "bo@", blist(lst, i), T.bo[:, 3 * lo + 2:3 * hi:3]), follow)]
+                both(offsets("lstb@", "bo@", blist(lst, i), T.bo[:, 3 * lo + 2:3 * hi:3]), follow)])
 
-        sa, sb = search(0), search(1)
-        for j in range(len(sa) + LEAD):
-            if j < len(sa):
-                sa[j]()
-            if j >= LEAD:
-                sb[j - LEAD]()
-            if j in aside:
-                aside[j]()
+        run([TURNS], dict(a=search(0), b=search(1), nonea=lambda: nones(0), noneb=lambda: nones(1),
+                          none=later("v", "nno", "five nn", scan, T.nno[:], T.five[:], T.nn[:], 1.0, A.mult, A.add),
+                          mates=later("s", "jm", "h0# mtl", act, T.jm[:], ind(T.h0, T.mtl[:, 0:L]), COPY)))
         wrote["s6"] = wrote["lstb.1"]
 
-        def unpack(planes):
-            for b in planes:
-                op("s", "fz%d" % b, "b%d" % (2 + b), act, plane(T.fz, b), bank(2 + b), COPY, scale=0.5)
-        unpack((0, 1))
-        op("v", "e1.0", "sc# lstb.0", tc, cols(T.e1, pa), ind(T.sc, blist(lst, 0)))
-        if t == 0:
-            op("v", "mnl", "mnf", tc, T.mnl[:], T.mnf[:])
-            op("v", "mxl", "mxf", tc, T.mxl[:], T.mxf[:])
-        op("s", "e1.1", "sc# lstb.1", act, cols(T.e1, pb), ind(T.sc, blist(lst, 1)), COPY)
-        op("v", "s5", "kk jm", scan, T.s5[:], T.kk[:], T.jm[:], 0.0, A.add, A.max)
-        op("s", "e2.1", "e1# mxl", act, cols(T.e2, pb), ind(T.e1, T.mxl[:, pb[0]:pb[1]]), COPY)
-        op("v", "e2.0", "e1# mxl", tc, cols(T.e2, pa), ind(T.e1, T.mxl[:, pa[0]:pa[1]]))
-        unpack((2, 3))
-        op("v", "fmf", "s5 fk", tt, T.fmf[:], last(T.s5), T.fk[:], A.subtract)
-        op("v", "cc#", "e1# e2# mnl", tt, T.cc[:], ind(T.e1, T.mnl[:, 0:L]), T.e2[:], A.is_gt)
-        op("v", "dl", "fmf kb2", ts, T.dl[:], T.fmf[:], kb2, None, A.mult)
-        if t == 1:
-            op("v", "vq", "vt", V.quantize_mx, T.vq[:, 0:128], T.vqs[:, 0:128], T.vt[:, 0:512])
-        rest = [lambda: (op("v", "sm", "kb cc#", scan, T.sm[:], T.kb[:], T.cc[:], 0.0, A.add, A.max),
-                         op("v", "fkx", "fk dl", tt, T.fkx[:], T.fk[:], T.dl[:], A.subtract)),
-                lambda: op("v", "dl", "sm fmf", tt, T.dl[:], last(T.sm), T.fmf[:], A.mult),
-                lambda: op("v", "fk", "fkx dl", tt, T.fk[:], T.fkx[:], T.dl[:], A.add),
-                lambda: key("jl0", "fk", jl(0), T.fk[:])]
+        def swap():
+            def halve(planes):
+                for b in planes:
+                    op("s", "fz%d" % b, "b%d" % (2 + b), act, plane(T.fz, b), bank(2 + b), COPY, scale=0.5)
+            halve((0, 1))
+            copy("v", "e1.0", "sc# lstb.0", cols(T.e1, pa), ind(T.sc, blist(lst, 0)))
+            if t == 0:
+                op("v", "mnl", "mnf", tc, T.mnl[:], T.mnf[:])
+                op("v", "mxl", "mxf", tc, T.mxl[:], T.mxf[:])
+            copy("s", "e1.1", "sc# lstb.1", cols(T.e1, pb), ind(T.sc, blist(lst, 1)))
+            op("v", "s5", "kk jm", scan, T.s5[:], T.kk[:], T.jm[:], 0.0, A.add, A.max)
+            copy("s", "e2.1", "e1# mxl", cols(T.e2, pb), ind(T.e1, T.mxl[:, pb[0]:pb[1]]))
+            copy("v", "e2.0", "e1# mxl", cols(T.e2, pa), ind(T.e1, T.mxl[:, pa[0]:pa[1]]))
+            halve((2, 3))
+            op("v", "fmf", "s5 fk", tt, T.fmf[:], last(T.s5), T.fk[:], A.subtract)
+            op("v", "cc#", "e1# e2# mnl", tt, T.cc[:], ind(T.e1, T.mnl[:, 0:L]), T.e2[:], A.is_gt)
+            op("v", "dl", "fmf kb2", ts, T.dl[:], T.fmf[:], kb2, None, A.mult)
+            if t == 1:
+                op("v", "vq", "vt", V.quantize_mx, T.vq[:, 0:128], T.vqs[:, 0:128], T.vt[:, 0:512])
+            op("v", "sm", "kb cc#", scan, T.sm[:], T.kb[:], T.cc[:], 0.0, A.add, A.max)
+            op("v", "fkx", "fk dl", tt, T.fkx[:], T.fk[:], T.dl[:], A.subtract)
+            op("v", "dl", "sm fmf", tt, T.dl[:], last(T.sm), T.fmf[:], A.mult)
+            op("v", "fk", "fkx dl", tt, T.fk[:], T.fkx[:], T.dl[:], A.add)
+            key("jl0", "fk", jl(0), T.fk[:])
+            made.update(hops=0, kept=1, lists=1)
 
-        def followers(shared):
-            if t < 2:
-                hops[0], lists[0] = 0, 1
-                hop(shared)
-                hop(shared)
-            else:
-                op("s", "n0#", "idt# jl0", act, T.n0[:], ind(T.idt, jl(0)), FN.Identity, bias=MID)
-                for i in range(8):
-                    store("y", "n0#", T.nf[i:i + 1, :], T.n0[16 * i:16 * i + 1, :])
-        if came is not None:
-            while rest:
-                rest.pop(0)()
-            followers(True)
-            tolist()
-        for i, p in enumerate(PARTS):
-            lo, hi = 16 * p[0], 16 * p[1]
-            for b in range(4):
-                op("s", "zp%d.%d" % (b, i), "fz%d rl.%d" % (b, i), act, plane(T.zp, b, lo, hi), ind(T.fz, plist(rl, i), C * b), COPY)
-                op("v", "zt%d.%d" % (b, i), "fz%d zp%d.%d rl.%d" % (b, b, i, i), tt, T.zt[:, 4 * lo + b:4 * hi:4],
-                   ind(T.fz, blist(rl, i), C * b), plane(T.zp, b, lo, hi), A.add)
-                if rest:
-                    rest.pop(0)()
-        if came is None:
-            followers(False)
-        else:
-            hop()
-        op("v", "zq", "zt0# zt1# zt2# zt3#", V.quantize_mx, T.zq[:, 0:C], T.zqs[:, 0:C], T.zt[:, 0:B4])
-        tolist()
+        def followers():
+            op("s", "n0#", "idt# jl0", act, T.n0[:], ind(T.idt, jl(0)), FN.Identity, bias=MID)
+            for i in range(8):
+                store("y", "n0#", T.nf[i:i + 1, :], T.n0[16 * i:16 * i + 1, :])
+
+        picks = [(i, b) for i in range(2) for b in range(4)]
+        adds = list(picks)
+
+        def pick(q):
+            i, b = picks.pop(0)
+            copy(q, "zp%d.%d" % (b, i), "fz%d rl.%d" % (b, i), plane(T.zp, b, 16 * PARTS[i][0], 16 * PARTS[i][1]), ind(T.fz, plist(rl, i), C * b))
+
+        def add():
+            i, b = adds.pop(0)
+            lo, hi = 16 * PARTS[i][0], 16 * PARTS[i][1]
+            op("v", "zt%d.%d" % (b, i), "fz%d zp%d.%d rl.%d" % (b, b, i, i), tt, T.zt[:, 4 * lo + b:4 * hi:4],
+               ind(T.fz, blist(rl, i), C * b), plane(T.zp, b, lo, hi), A.add)
+
         hb = [6, 7, 2, 3]
-        product(6, T.wl, T.wls, 0, T.zq, T.zqs, "wl wls zq", 0, HALF)
-        product(4, T.wl, T.wls, 0, T.zq, T.zqs, "wl wls zq", HALF, C)
-        for b in range(1, 4):
-            product(hb[b], T.wl, T.wls, 128 * b, T.zq, T.zqs, "wl wls zq")
-        op("s", "hh0", "b6", act, T.hh[:, 0:HALF], bank(6, 0, HALF), COPY, scale=0.03125)
-        for b in range(1, 4):
-            op("s", "hh%d" % b, "b%d" % hb[b], act, plane(T.hh, b), bank(hb[b]), COPY, scale=0.03125)
-        op("v", "hhb", "b4", ts, T.hh[:, HALF:C], bank(4, 0, C - HALF), 0.03125, None, A.mult)
 
-        def state(i, b):
+        def layer():
+            op("v", "zq", "zt0# zt1# zt2# zt3#", V.quantize_mx, T.zq[:, 0:C], T.zqs[:, 0:C], T.zt[:, 0:B4])
+            product(6, T.wl, T.wls, 0, T.zq, T.zqs, "wl wls zq", 0, HALF)
+            product(4, T.wl, T.wls, 0, T.zq, T.zqs, "wl wls zq", HALF, C)
+            for b in range(1, 4):
+                product(hb[b], T.wl, T.wls, 128 * b, T.zq, T.zqs, "wl wls zq")
+
+        def state(i):
             lo, hi = (0, C) if i is None else (16 * PARTS[i][0], 16 * PARTS[i][1])
             at, me = blist(lst, i), "#" if i is None else ".%d" % i
-            if b < 4:
-                op("v", "xt%d%s" % (b, me), "hh%d fo%d hhb lstb%s" % (b, b, me), tt, T.xt[:, 4 * lo + b:4 * hi:4],
-                   ind(T.hh, at, C * b), plane(T.fo, b, lo, hi), A.add)
-            else:
+
+            def outputs():
                 op("v", "xq3" + me, " ".join("xt%d%s" % (b, me) for b in range(4)), V.quantize_mx, T.xq3[:, lo:hi], T.xs3[:, lo:hi], T.xt[:, 4 * lo:4 * hi])
                 product(i, T.vq, T.vqs, 0, T.xq3, T.xs3, "vq xq3" + me, lo, hi)
                 store("y", "xq3" + me, T.oc[:, 4 * lo:4 * hi], T.xq3[:, lo:hi].bitcast(dt.uint8))
                 op("s", "yo" + me, "b%d" % i, act, T.yo[:, lo:hi], bank(i, 0, hi - lo), COPY)
                 store("s", "yo" + me, T.y[:, lo:hi], T.yo[:, lo:hi])
+            return series([later("v", "xt%d%s" % (b, me), "hh%d fo%d hhb lstb%s" % (b, b, me), tt, T.xt[:, 4 * lo + b:4 * hi:4],
+                                 ind(T.hh, at, C * b), plane(T.fo, b, lo, hi), A.add) for b in range(4)] + [outputs])
+        tail = dict(
+            swap=swap, nf=followers, pick=lambda: pick("s"), vpick=lambda: pick("v"), add=add, layer=layer,
+            h0a=later("s", "hh0", "b6", act, T.hh[:, 0:HALF], bank(6, 0, HALF), COPY, scale=0.03125),
+            h0b=later("v", "hhb", "b4", ts, T.hh[:, HALF:C], bank(4, 0, C - HALF), 0.03125, None, A.mult),
+            h=series(later("s", "hh%d" % b, "b%d" % hb[b], act, plane(T.hh, b), bank(hb[b]), COPY, scale=0.03125) for b in (1, 2, 3)),
+            x=state(None), xa=state(0), xb=state(1))
         if t < 2:
-            hop()
-            for b in range(4):
-                state(None, b)
-                if b == 2:
-                    tolist()
-                    hop()
+            run(ORDER["near" if came is None else "far"], hopping, tail, head(t + 1))
         else:
-            for i, b in ((0, 0), (0, 1), (0, 2), (0, 3), (1, 0), (0, 4), (1, 1), (1, 2), (1, 3), (1, 4)):
-                state(i, b)
+            run(ORDER["last"], tail)
     for k in range(4):
         store("y", "xq3#", T.osc[4 * k:4 * k + 4, 0:C], T.xs3[32 * k:32 * k + 4, 0:C])
     for q in ("v", "s", "t", "g"):

from concourse.mybir import dt, AluOpType, ActivationFunctionType

C = 288
L = 18
B4 = 4 * C
HALF = C // 2
STEP = [4, 1, 2]
N = 8
BIG = 1e29
KB = 1024.0
MID = 144.0
PARTS = ((0, 10, 32), (10, 18, 592))
SLOTS = 1024
RUNS = ((0, 20), (20, 36))
CUT = 5 * C // 8
F32, BF, I32, U16, F8, U8, F16 = "float32", "bfloat16", "int32", "uint16", "float8_e4m3fn_x4", "uint8", "float16"

MEANS = "pick " + "add pick " * 7 + "add"
ORDER = {
    "first": ["list0 e0 hop2 e1 e2 e3 hop2 uoff keep cl list leave unpack hop2 uq u2s c0k fkx keep u2 list fk hopv keep",
              "scores scb sca top3 list maxa maxb hop",
              "maxa copya keep maxb list copyb hop", "maxa copya maxb copyb keep list hop", "maxa copya maxb own copyb hop keep",
              "maxa copya maxb copyb keep mtf mtl list list kb", "maxa maxb mnf mxf"],
    "near": ["swap", MEANS, "hop layer hop2 h0a keep h0b h h list hop x h x x keep list x hop",
             "leave keep scores list unpack sca scb maxa maxb hop",
             "maxa copya keep maxb list copyb hop2", "maxa maxb keep vcopya list copyb hop", "maxa maxb vcopya copyb own hop",
             "maxa copya maxb keep copyb keep list", "maxa list maxb"],
    "far": ["swap hop2 hop2 keep list", MEANS, "layer hop keep h0b h0a h h list hop x h x x keep list x",
            "leave hop scores keep unpack list sca scb maxa maxb hop",
            "maxa copya keep maxb list copyb hop", "maxa copya maxb copyb keep hop", "maxa copya maxb own copyb keep",
            "maxa copya maxb copyb list list", "maxa maxb"],
    "last": ["swap nf vpick pick " + "add pick " * 6 + "add add", "layer h0b h0a h h h", "xa " * 5, "xb " * 5],
}
TURNS = "a b none a a nonea noneb " + "b a b a b b a b a a " * 4 + "mates " + "a a b " * 3 + "a " + "b " * 6


def _scratch():
    s = {}

    def sb(names, n, d):
        for k in names.split():
            s[k] = ("sbuf", [128, n], d)
    sb("pidx pi15", 1, I32)
    sb("icol kj kb2", 1, F32)
    sb("pen sc sp e1 e2 yo n0 n1 m0 m1 m2 m3 m4 m5", C, F32)
    sb("j16 dd idt kk kb rm cc cc2 sm jg0 jg1 jm h0 h1 h2 h3 h4 h5 h6 h7", C, BF)
    sb("sj s5 s6 s7", C, F16)
    sb("v0 v1 vc", SLOTS, F16)
    sb("ba bz", SLOTS, BF)
    sb("bt", 64 + 5 * C, BF)
    sb("top topo nn nno five", 5 * L, F16)
    sb("po bo", 3 * L, F16)
    sb("cl c0k dl fk fkx fmf mtf mnf mxf", L, F32)
    sb("nxi mti", L, I32)
    sb("mnl mxl mtl pl0 pl1", L, U16)
    sb("jls", 8 * L, U16)
    sb("lst0 lst1 lst2 rl0 rl1 rl2 rr0 rr1 rr2", 2 * L, U16)
    sb("uoi", 8, I32)
    sb("uoff", 8, U16)
    sb("ones wide", 516, BF)
    sb("ut vt", 512, BF)
    sb("x0 xt fo fz zp zt hh", B4, BF)
    for k, n in (("uq", 128), ("u2", 128), ("vq", 128), ("ec", 512), ("wl", 512), ("zq", C)):
        s[k] = ("sbuf", [128, n], F8)
        s[k + "s"] = ("sbuf", [128, n], U8)
    for t in range(4):
        s["xq%d" % t] = ("sbuf", [128, C], F8)
        s["xs%d" % t] = ("sbuf", [128, C], U8)
    for t in range(3):
        for a in "lr":
            s[a + "c%d" % t] = ("sbuf", [128, C], F8)
            s[a + "p%d" % t] = ("sbuf", [128, C], U8)
    s["ps"] = ("psum", [128, 4096], F32)
    return s


SCRATCH = _scratch()
SEMAPHORES = ["sv", "ss", "st", "sg", "ls", "out", "dx", "du", "dv", "dwc", "dws", "dn", "dm"] + [
    a + str(t) for t in range(3) for a in ("rx", "ry", "rz", "rs", "rt")]


def relay_of(topo, cores, a, b):
    if topo.may_write(a, b):
        return None
    q = [q for q in topo.cores_of(a) if q not in cores and topo.die(q) == topo.die(a) and topo.may_write(q, b)]
    return q[0], q[-1]


def rank_program(g, core, T, topo):
    cores = list(T.cores)
    rank = T.rank_of(core)
    nsent = [0]

    def send(dst, out, src, sem):
        rid, pid = topo.addr(dst, core)
        g.remote_dma(out, src, T.sem[sem], T.sem.ls, pid, rid, topo.mask(core, dst))
        nsent[0] += len(topo.engines(core, dst))

    if rank is None:
        for t, d in enumerate(STEP):
            for r in range(N):
                a, b = cores[r], cores[(r + d) % N]
                via = relay_of(topo, cores, a, b)
                if via is None or core not in via:
                    continue
                n = len(topo.engines(a, core))
                lc, rc = T["lc%d" % t], T["rc%d" % t]
                if core == via[0]:
                    g.wait_ge(T.sem["rx%d" % t], n)
                    send(b, lc[:, 0:CUT].bitcast(dt.uint8), rc[:, 0:CUT].bitcast(dt.uint8), "rx%d" % t)
                if core == via[1]:
                    g.wait_ge(T.sem["ry%d" % t], n)
                    send(b, lc[:, CUT:C].bitcast(dt.uint8), rc[:, CUT:C].bitcast(dt.uint8), "rx%d" % t)
                    g.wait_ge(T.sem["rz%d" % t], n)
                    send(b, T["lp%d" % t][:, 0:C], T["rp%d" % t][:, 0:C], "rx%d" % t)
                for i, (lo, hi) in enumerate(RUNS):
                    if core == via[i]:
                        sem = ("rs%d", "rt%d")[i] % t
                        g.wait_ge(T.sem[sem], n)
                        send(b, T["rl%d" % t][:, lo:hi], T["rr%d" % t][:, lo:hi], sem)
        if nsent[0]:
            g.wait_ge(T.sem.ls, nsent[0])
        return

    A = AluOpType
    FN = ActivationFunctionType
    COPY = FN.Copy
    queues = {"v": g.vector, "s": g.scalar, "t": g.tensor, "g": g, "y": g.sync}
    semname = {"v": "sv", "s": "ss", "t": "st", "g": "sg"}
    cnt = {"v": 0, "s": 0, "t": 0, "g": 0}
    seen, wrote, readers = {}, {}, {}

    def wait(q, sem, n):
        if seen.get((q, sem), 0) < n:
            queues[q].wait_ge(T.sem[sem], n)
            seen[(q, sem)] = n

    def names(keys):
        return [k for w in keys.split() for k in ((w[:-1] + ".0", w[:-1] + ".1") if w[-1] == "#" else (w,))]

    def before(q, reads, writes):
        need = {}
        for k in reads + writes:
            if k in wrote:
                s, n = wrote[k]
                need[s] = max(need.get(s, 0), n)
        for k in writes:
            for s, n in readers.get(k, {}).items():
                need[s] = max(need.get(s, 0), n)
        for s, n in need.items():
            wait(q, s, n)

    def op(q, writes, reads, fn, *args, **kw):
        writes, reads = names(writes), names(reads)
        before(q, reads, writes)
        cnt[q] += 1
        fn(*args, **kw).then_inc(T.sem[semname[q]], 1)
        for k in reads:
            readers.setdefault(k, {})[semname[q]] = cnt[q]
        for k in writes:
            wrote[k] = (semname[q], cnt[q])
            readers[k] = {}

    def later(*args, **kw):
        return lambda: op(*args, **kw)

    def series(calls):
        calls = list(calls)
        return lambda: calls.pop(0)()

    def run(order, *tables):
        calls = {k: f for x in tables for k, f in x.items()}
        for name in " ".join(order).split():
            calls[name]()

    V, S, P = g.vector, g.scalar, g.tensor
    ts, tt, tc, scan, act = V.tensor_scalar, V.tensor_tensor, V.tensor_copy, V.tensor_tensor_scan, S.activation

    def load(q, name, out, src, sem):
        queues[q].dma_start(out, src).then_inc(T.sem[sem], 16)
        wrote[name] = (sem, 16)

    nout = [0]

    def store(q, reads, out, src):
        before(q, names(reads), [])
        queues[q].dma_start(out, src).then_inc(T.sem.out, 16)
        nout[0] += 16

    def copy(q, writes, reads, out, src):
        if q == "s":
            op("s", writes, reads, act, out, src, COPY)
        else:
            op("v", writes, reads, tc, out, src)

    def bank(b, lo=0, hi=C):
        return T.ps[:, 512 * b + lo:512 * b + hi]

    def product(b, lhs, ls, a, rhs, rs, reads, lo=0, hi=C):
        op("t", "b%d" % b, reads, P.matmul_mx, bank(b, 0, hi - lo), lhs[:, a:a + 128], ls[:, a:a + 128], rhs[:, lo:hi], rs[:, lo:hi], True, True)

    def plane(buf, b, lo=0, hi=C):
        return buf[:, C * b + lo:C * b + hi]

    def last(buf, lo=0, hi=L):
        return buf[:, 16 * lo + 15:16 * hi:16]

    def ind(buf, lst, a=0):
        return buf[:, a:a + C].indirect(lst)

    def jl(k, lo=0, hi=L):
        return T.jls[:, L * k + lo:L * k + hi]

    def cols(buf, part):
        return buf[:, 16 * part[0]:16 * part[1]]

    def plist(buf, i):
        return buf[:, 0:10] if i == 0 else buf[:, 28:36]

    def blist(buf, i):
        return buf[:, 10:28] if i is None else buf[:, 10:20] if i == 0 else buf[:, 20:28]

    def spread3(buf, part):
        lo, hi, a = part
        return buf[:, a:a + 48 * (hi - lo):3]

    def slot(buf, part, i):
        lo, hi, a = part
        return buf[:, a + 45 + 16 * i:a + 45 + 16 * i + 48 * (hi - lo - 1) + 1:48]

    def three(buf, part, i):
        lo, hi, a = part
        return buf[:, a + 45 + 16 * i:a + 45 + 16 * i + 16 * (3 * (hi - lo) - 1) + 1:16]

    pa, pb = PARTS
    kj, kb2 = T.kj[:, 0:1], T.kb2[:, 0:1]

    def key(writes, reads, out, src):
        op("v", writes, reads + " kj", ts, out, src, kj, None, A.subtract)

    made = {"hops": 0, "kept": 1, "lists": 1}

    def hop(by):
        k = made["hops"]
        assert k <= 7 and made["lists"] >= min(k, 6)
        made["hops"] += 1
        w, l = ("idt", 0) if k == 0 else ("h6", 5) if k == 7 else ("h%d" % (k - 1), k - 1)
        if len(by) == 1:
            copy(by, "h%d#" % k, "%s# jl%d" % (w, l), T["h%d" % k][:], ind(T[w], jl(l)))
        else:
            for q, i in (("s", 1), ("v", 0)):
                p = PARTS[i]
                copy(q, "h%d.%d" % (k, i), "%s# jl%d" % (w, l), cols(T["h%d" % k], p), ind(T[w], jl(l, p[0], p[1])))

    def keep():
        k = made["kept"]
        assert k < made["hops"] and (k == made["lists"] or k > 5)
        made["kept"] += 1
        sj = "s%d" % k if k >= 5 else "sj"
        op("v", sj, "kk h%d#" % k, scan, T[sj][:], T.kk[:], T["h%d" % k][:], 0.0, A.add, A.max)

    def tolist():
        k = made["lists"]
        assert k < made["kept"]
        made["lists"] += 1
        sj = "s%d" % k if k >= 5 else "sj"
        key("jl%d" % k, sj, jl(k), last(T[sj]))
    hopping = dict(hop=lambda: hop("s"), hopv=lambda: hop("v"), hop2=lambda: hop("sv"), keep=keep, list=tolist)

    load("y", "x0", T.x0[:], T.x[:], "dx")
    load("s", "nxi", T.nxi[:], T.nx[:], "dn")
    load("s", "ut", T.ut[:], T.u[:], "du")
    load("s", "mti", T.mti[:], T.mt[:], "dm")
    wait("y", "dx", 16)
    wait("y", "du", 16)
    load("y", "wl", T.wl[:, 0:512].bitcast(dt.uint8), T.wc[:, 0:2048], "dwc")
    load("y", "wls", T.wls[:, 0:512], T.ws[:, 0:512], "dws")
    load("y", "vt", T.vt[:], T.v[:], "dv")

    op("g", "pidx", "", g.iota, T.pidx[:], [[0, 1]], 0, 1)
    op("g", "j16", "", g.iota, T.j16[:], [[0, L], [1, 16]], 0, 0, allow_small_or_imprecise_dtypes=True)
    op("v", "ones", "", V.memset, T.ones[:], 1.0)
    op("g", "wide", "ones", g.affine_select, T.wide[:], T.ones[:], [[-1, 516]], A.is_equal, 0.0, 3, 4)
    op("g", "dl", "", g.iota, T.dl[:], [[16, L]], 0, 0, allow_small_or_imprecise_dtypes=True)
    op("g", "uoi", "", g.iota, T.uoi[:], [[16, 8]], 0, 0)
    op("v", "pi15", "pidx", ts, T.pi15[:], T.pidx[:], 15, None, A.bitwise_and)
    op("v", "icol", "pi15", tc, T.icol[:], T.pi15[:])
    op("v", "idt#", "ones", scan, T.idt[:], T.ones[:, 0:C], T.ones[:, 0:C], -MID - 1.0, A.add, A.mult)
    op("v", "kb2", "icol", ts, T.kb2[:], T.icol[:], 15.0, 2.0, A.is_lt, A.mult)
    op("v", "dd", "j16 icol", ts, T.dd[:], T.j16[:], T.icol[:, 0:1], None, A.subtract)
    op("v", "kj", "kb2", ts, T.kj[:], T.kb2[:], KB / 2, MID, A.mult, A.subtract)
    op("v", "cc#", "dd", ts, T.cc[:], T.dd[:], 0.0, -4.0 * KB, A.is_equal, A.mult)
    op("v", "cc2#", "dd", ts, T.cc2[:], T.dd[:], 1.0, KB, A.is_equal, A.mult)
    op("v", "kk", "cc# cc2#", tt, T.kk[:], T.cc[:], T.cc2[:], A.add)
    op("s", "top", "ones", act, T.top[:], T.ones[:, 0:5 * L], COPY, scale=0.0)
    op("s", "nn", "ones", act, T.nn[:], T.ones[:, 0:5 * L], COPY, scale=0.0)
    a, b = [p[2] + 45 + 48 * (p[1] - p[0]) for p in PARTS]
    op("s", "v0x", "ones", act, T.v0[:, a:b + 1:b - a], T.ones[:, 0:2], COPY)
    op("s", "bt", "ones kb2", act, T.bt[:, 75:75 + 80 * L - 15:16], T.ones[:, 0:5 * L], COPY, scale=kb2)
    op("s", "rm", "j16", act, T.rm[:], T.j16[:], FN.Sign)
    op("s", "nn", "ones", act, T.nn[:, 4:5 * L:5], T.ones[:, 0:L], COPY)
    op("s", "e1#", "dd", act, T.e1[:], T.dd[:], FN.Abs)
    op("s", "e2#", "e1#", act, T.e2[:], T.e1[:], FN.Relu, bias=1.0, scale=-1.0)
    op("s", "pen", "e2#", act, T.pen[:], T.e2[:], FN.Identity, bias=-BIG, scale=2.0 * BIG)
    once = dict(
        list0=later("v", "jl0", "nxi", tc, jl(0), T.nxi[:]),
        fkx=later("v", "fkx", "nxi", tc, T.fkx[:], T.nxi[:]),
        fk=later("v", "fk", "fkx kj", ts, T.fk[:], T.fkx[:], kj, None, A.add),
        cl=later("v", "cl", "dl icol", ts, T.cl[:], T.dl[:], T.icol[:, 0:1], None, A.add),
        c0k=later("v", "c0k", "cl kj", ts, T.c0k[:], T.cl[:], kj, None, A.add),
        top3=later("s", "top3", "top c0k", act, T.top[:, 3:5 * L:5], T.c0k[:], COPY),
        uoff=later("v", "uoff", "uoi", tc, T.uoff[:], T.uoi[:]),
        uq=later("v", "uq", "ut", V.quantize_mx, T.uq[:, 0:128], T.uqs[:, 0:128], T.ut[:, 0:512]),
        u2=later("v", "u2", "uq uoff", tc, T.u2[:, 0:128].bitcast(dt.uint32), T.uq[:, 0:128].bitcast(dt.uint32).indirect(T.uoff[:, 0:8])),
        u2s=later("s", "u2s", "uq uoff", act, T.u2s[:, 0:128], T.uqs[:, 0:128].indirect(T.uoff[:, 0:8]), COPY),
        kb=later("s", "kb", "kk", act, T.kb[:], T.kk[:], COPY, scale=2.0 / KB),
        mtf=later("v", "mtf", "mti", tc, T.mtf[:], T.mti[:]),
        mtl=later("v", "mtl", "mti", tc, T.mtl[:], T.mti[:]),
        mnf=later("v", "mnf", "mtf cl", tt, T.mnf[:], T.mtf[:], T.cl[:], A.min),
        mxf=later("v", "mxf", "mtf cl", tt, T.mxf[:], T.mtf[:], T.cl[:], A.max))
    for k in range(4):
        once["e%d" % k] = later("v", "ec%d" % k, "wide", V.quantize_mx, T.ec[:, 128 * k:128 * k + 128], T.ecs[:, 128 * k:128 * k + 128], T.wide[:, 3 - k:515 - k])

    def head(t):
        to = cores[(rank + STEP[t]) % N]
        via = relay_of(topo, cores, core, to)
        xq, xs = T["xq%d" % t], T["xs%d" % t]

        def leave():
            op("v", "xq%d" % t, "xt0# xt1# xt2# xt3#" if t else "x0", V.quantize_mx, xq[:, 0:C], xs[:, 0:C], T["xt" if t else "x0"][:, 0:B4])
            before("g", ["xq%d" % t], [])
            if via is None:
                send(to, T["lc%d" % t][:, 0:C].bitcast(dt.uint8), xq[:, 0:C].bitcast(dt.uint8), "rx%d" % t)
                send(to, T["lp%d" % t][:, 0:C], xs[:, 0:C], "rx%d" % t)
            else:
                send(via[1], T["rc%d" % t][:, CUT:C].bitcast(dt.uint8), xq[:, CUT:C].bitcast(dt.uint8), "ry%d" % t)
                send(via[0], T["rc%d" % t][:, 0:CUT].bitcast(dt.uint8), xq[:, 0:CUT].bitcast(dt.uint8), "rx%d" % t)
                send(via[1], T["rp%d" % t][:, 0:C], xs[:, 0:C], "rz%d" % t)
            if t == 0:
                for p in PARTS:
                    for name, buf, i, c in (("ba", T.ba, -2, 0), ("bb", T.ba, -1, 1), ("bz", T.bz, -1, 0)):
                        op("g", name, "", g.iota, slot(buf, p, i), [[0, p[1] - p[0]]], c, 0, allow_small_or_imprecise_dtypes=True)

        def scores():
            product(0, T.u2, T.u2s, 0, xq, xs, "u2 u2s xq%d" % t, 0, HALF)
            product(7, T.u2, T.u2s, 0, xq, xs, "u2 u2s xq%d" % t, HALF, C)
            product(1, T.u2, T.u2s, 0, xq, xs, "u2 u2s xq%d" % t)

        def unpack():
            for k in range(4):
                product(2 + k, T.ec, T.ecs, 128 * k, xq, xs, "ec%d xq%d" % (k, t))
        level, copied = [0, 0], [1, 1]

        def maximum(i):
            k, p = level[i], PARTS[i]
            level[i] += 1
            assert made["lists"] >= max(k, 2) and min(level) >= k and copied[i] >= k
            if k == 0:
                op("v", "m0.%d" % i, "sc# jl0", tc, cols(T.m0, p), ind(T.sc, jl(0, p[0], p[1])))
            elif k == 1:
                op("v", "m1.%d" % i, "sc# jl1 m0.%d" % i, tt, cols(T.m1, p), ind(T.sc, jl(1, p[0], p[1])), cols(T.m0, p), A.max)
            else:
                m, n1 = "m%d" % (k - 1), "n%d" % ((k - 1) % 2)
                op("v", "m%d.%d" % (k, i), "%s# jl%d %s.%d" % (m, k - 1, n1, i), tt,
                   cols(T["m%d" % k], p), ind(T[m], jl(k - 1, p[0], p[1])), cols(T[n1], p), A.max)

        def twin(q, i):
            k, p = copied[i], PARTS[i]
            assert level[i] == k + 1
            copied[i] += 1
            copy(q, "n%d.%d" % (k % 2, i), "m%d.%d" % (k, i), cols(T["n%d" % (k % 2)], p), cols(T["m%d" % k], p))
        return dict(
            leave=leave, scores=scores, unpack=unpack, maxa=lambda: maximum(0), maxb=lambda: maximum(1),
            copya=lambda: twin("s", 0), copyb=lambda: twin("s", 1), vcopya=lambda: twin("v", 0), vcopyb=lambda: twin("v", 1),
            sca=later("s", "sc.0", "b0", act, T.sc[:, 0:HALF], bank(0, 0, HALF), COPY),
            scb=later("v", "sc.1", "b7", tc, T.sc[:, HALF:C], bank(7, 0, C - HALF)),
            own=later("v", "sp", "b1 pen", tt, T.sp[:], bank(1), T.pen[:], A.min))

    run(ORDER["first"], hopping, once, head(0))
    for t, d in enumerate(STEP):
        to, frm = cores[(rank + d) % N], cores[(rank - d) % N]
        via, came = relay_of(topo, cores, core, to), relay_of(topo, cores, frm, core)
        lst, rl = T["lst%d" % t], T["rl%d" % t]
        n = len(topo.engines(frm if came is None else came[0], core))
        wrote["land"] = ("rx%d" % t, (2 if came is None else 3) * n)
        wrote["rl.0"], wrote["rl.1"] = ("rs%d" % t, n), ("rt%d" % t, n)
        assert made["lists"] == 8

        def topbit(e, cc):
            op("v", "bt%d" % e, "kb %s#" % cc, scan, T.bt[:, 16 * e:16 * e + 5 * C:5], T.kb[:], T[cc][:], 0.0, A.add, A.max)
        op("s", "n0#", "m5# jl5", act, T.n0[:], ind(T.m5, jl(5)), COPY)
        op("s", "n1#", "m5# jl7", act, T.n1[:], ind(T.m5, jl(7)), COPY)
        for b in range(4):
            op("s", "fo%d" % b, "b%d" % (2 + b), act, plane(T.fo, b), bank(2 + b), COPY)
            product(2 + b, T.ec, T.ecs, 128 * b, T["lc%d" % t], T["lp%d" % t], "land ec%d" % b)
        op("v", "top2", "top s5 c0k", tt, T.top[:, 2:5 * L:5], last(T.s5), T.c0k[:], A.subtract)
        op("v", "top1", "top s5 s6", tt, T.top[:, 1:5 * L:5], last(T.s6), last(T.s5), A.subtract)
        op("v", "jg0#", "m5# jl6 sc#", tt, T.jg0[:], ind(T.m5, jl(6)), T.sc[:], A.is_le)
        op("v", "cc#", "m5# b1", tt, T.cc[:], T.m5[:], bank(1), A.is_le)
        topbit(1, "jg0")
        op("v", "cc2#", "n0# b1", tt, T.cc2[:], T.n0[:], bank(1), A.is_le)
        topbit(3, "cc")
        topbit(2, "cc2")
        op("v", "top0", "top s6 s7", tt, T.top[:, 0:5 * L:5], last(T.s7), last(T.s6), A.subtract)
        op("v", "five", "bt bt1 bt2 bt3 kb2", ts, T.five[:], T.bt[:, 75:75 + 80 * L - 15:16], kb2, None, A.subtract)
        op("v", "sm", "n1# b1", tt, T.sm[:], T.n1[:], bank(1), A.is_le)
        op("v", "topo", "five top0 top1 top2 top3", scan, T.topo[:], T.five[:], T.top[:], 0.0, A.mult, A.add)
        op("v", "s7", "kb sm", scan, T.s7[:], T.kb[:], T.sm[:], 0.0, A.add, A.max)
        key("pl0#", "topo", T.pl0[:], T.topo[:, 3:5 * L:5])
        op("v", "five", "s7 kb2", ts, T.five[:, 0:5 * L:5], last(T.s7), kb2, None, A.subtract)

        def nones(i):
            p = lo, hi, _ = PARTS[i]
            none = T.nno[:, 5 * lo + 3:5 * hi:5]
            op("s", "bzn.%d" % i, "bz nno", act, slot(T.bz, p, 1), none, FN.Identity, bias=1.0, scale=-1.0)
            op("v", "vcn.%d" % i, "nno c0k", tt, slot(T.vc, p, 1), none, T.c0k[:, lo:hi], A.mult)

        def search(i):
            p = lo, hi, _ = PARTS[i]
            here = T.topo[:, 5 * lo + 3:5 * hi:5]

            def mine(keys):
                return keys.replace("@", ".%d" % i)

            def o(q, writes, reads, *args, **kw):
                return later(q, mine(writes), mine(reads), *args, **kw)

            def both(*fs):
                return lambda: [f() for f in fs]

            def offsets(writes, reads, out, src):
                return lambda: key(mine(writes), mine(reads), out, src)
            out = []
            for k in (4, 3, 2, 1, 0):
                pl, jg, cc, v = "pl%d" % (k % 2), "jg%d" % (k % 2), "cc" if k % 2 else "cc2", "v%d" % (k % 2) if k else "vc"
                at, ba, w, pw = T[pl][:, lo:hi], "ba" if k else "bz", "v%d" % ((k + 1) % 2), "pl%d" % ((k + 1) % 2)
                look = [o("s", jg + "@", "h%d# %s@" % (k, pl), act, cols(T[jg], p), ind(T["h%d" % k], at), COPY)]
                if k == 0:
                    look.append(o("s", "jg1@", "h1# %s@" % pl, act, cols(T.jg1, p), ind(T.h1, at), COPY))
                look.append(o("v", cc + "@", "m%d# sp %s@" % (k, pl), tt, cols(T[cc], p), ind(T["m%d" % k], at), cols(T.sp, p), A.is_le))
                if 0 < k < 4:
                    look.append(o("s", v + "n@", v + "p@", act, slot(T[v], p, 1), slot(T[v], p, 2), COPY, scale=-1.0))
                if k == 4:
                    look.append(o("s", "v0p@", "topo", act, slot(T.v0, p, 2), here, COPY))
                    look.append(o("s", "v0n@", "topo", act, slot(T.v0, p, 1), here, COPY, scale=-1.0))
                out += [both(*look),
                        o("v", ba + "@", "%s bb rm %s@" % (ba, cc), scan, spread3(T[ba], p), cols(T.rm, p), cols(T[cc], p), 0.0, A.mult, A.add),
                        o("v", v + "@", "kk %s@" % jg, scan, spread3(T[v], p), cols(T.kk, p), cols(T[jg], p), 0.0, A.add, A.max)]
                if k:
                    out += [o("v", "%s@ %sn@ %sp@" % (w, w, w), "ba@ %s@ %sn@ %sp@" % (v, v, v), scan,
                              three(T[w], p, 0), three(T.ba, p, -2), three(T[v], p, 0), 0.0, A.mult, A.add),
                            offsets(pw + "@", w + "p@", T[pw][:, lo:hi], slot(T[w], p, 2))]

            def follow():
                (a, b), sem = RUNS[i], ("rs%d", "rt%d")[i] % t
                before("g", names(mine("lstb@ lstp@")), [])
                if via is None:
                    send(to, rl[:, a:b], lst[:, a:b], sem)
                else:
                    send(via[i], T["rr%d" % t][:, a:b], lst[:, a:b], sem)
            return series(out + [
                o("v", "sk@", "kk jg1@", scan, cols(T.s6, p), cols(T.kk, p), cols(T.jg1, p), 0.0, A.add, A.max),
                o("v", "v0n@", "vc@ v0p@", tt, slot(T.v0, p, 1), slot(T.vc, p, 0), slot(T.v0, p, 2), A.subtract),
                o("v", "vcd@", "vc@ sk@", tt, slot(T.vc, p, -1), last(T.s6, lo, hi), slot(T.vc, p, 0), A.subtract),
                o("v", "po@", "bz@ bzn@ v0@ v0n@ v0p@ v0x", scan, T.po[:, 3 * lo:3 * hi], three(T.bz, p, -1), three(T.v0, p, 1), 0.0, A.mult, A.add),
                o("v", "bo@", "bz@ bzn@ vc@ vcd@ vcn@", scan, T.bo[:, 3 * lo:3 * hi], three(T.bz, p, -1), three(T.vc, p, -1), 0.0, A.mult, A.add),
                offsets("lstp@", "po@", plist(lst, i), T.po[:, 3 * lo + 1:3 * hi:3]),
                both(offsets("lstb@", "bo@", blist(lst, i), T.bo[:, 3 * lo + 2:3 * hi:3]), follow)])

        run([TURNS], dict(a=search(0), b=search(1), nonea=lambda: nones(0), noneb=lambda: nones(1),
                          none=later("v", "nno", "five nn", scan, T.nno[:], T.five[:], T.nn[:], 1.0, A.mult, A.add),
                          mates=later("s", "jm", "h0# mtl", act, T.jm[:], ind(T.h0, T.mtl[:, 0:L]), COPY)))
        wrote["s6"] = wrote["lstb.1"]

        def swap():
            def halve(planes):
                for b in planes:
                    op("s", "fz%d" % b, "b%d" % (2 + b), act, plane(T.fz, b), bank(2 + b), COPY, scale=0.5)
            halve((0, 1))
            copy("v", "e1.0", "sc# lstb.0", cols(T.e1, pa), ind(T.sc, blist(lst, 0)))
            if t == 0:
                op("v", "mnl", "mnf", tc, T.mnl[:], T.mnf[:])
                op("v", "mxl", "mxf", tc, T.mxl[:], T.mxf[:])
            copy("s", "e1.1", "sc# lstb.1", cols(T.e1, pb), ind(T.sc, blist(lst, 1)))
            op("v", "s5", "kk jm", scan, T.s5[:], T.kk[:], T.jm[:], 0.0, A.add, A.max)
            copy("s", "e2.1", "e1# mxl", cols(T.e2, pb), ind(T.e1, T.mxl[:, pb[0]:pb[1]]))
            copy("v", "e2.0", "e1# mxl", cols(T.e2, pa), ind(T.e1, T.mxl[:, pa[0]:pa[1]]))
            halve((2, 3))
            op("v", "fmf", "s5 fk", tt, T.fmf[:], last(T.s5), T.fk[:], A.subtract)
            op("v", "cc#", "e1# e2# mnl", tt, T.cc[:], ind(T.e1, T.mnl[:, 0:L]), T.e2[:], A.is_gt)
            op("v", "dl", "fmf kb2", ts, T.dl[:], T.fmf[:], kb2, None, A.mult)
            if t == 1:
                op("v", "vq", "vt", V.quantize_mx, T.vq[:, 0:128], T.vqs[:, 0:128], T.vt[:, 0:512])
            op("v", "sm", "kb cc#", scan, T.sm[:], T.kb[:], T.cc[:], 0.0, A.add, A.max)
            op("v", "fkx", "fk dl", tt, T.fkx[:], T.fk[:], T.dl[:], A.subtract)
            op("v", "dl", "sm fmf", tt, T.dl[:], last(T.sm), T.fmf[:], A.mult)
            op("v", "fk", "fkx dl", tt, T.fk[:], T.fkx[:], T.dl[:], A.add)
            key("jl0", "fk", jl(0), T.fk[:])
            made.update(hops=0, kept=1, lists=1)

        def followers():
            op("s", "n0#", "idt# jl0", act, T.n0[:], ind(T.idt, jl(0)), FN.Identity, bias=MID)
            for i in range(8):
                store("y", "n0#", T.nf[i:i + 1, :], T.n0[16 * i:16 * i + 1, :])

        picks = [(i, b) for i in range(2) for b in range(4)]
        adds = list(picks)

        def pick(q):
            i, b = picks.pop(0)
            copy(q, "zp%d.%d" % (b, i), "fz%d rl.%d" % (b, i), plane(T.zp, b, 16 * PARTS[i][0], 16 * PARTS[i][1]), ind(T.fz, plist(rl, i), C * b))

        def add():
            i, b = adds.pop(0)
            lo, hi = 16 * PARTS[i][0], 16 * PARTS[i][1]
            op("v", "zt%d.%d" % (b, i), "fz%d zp%d.%d rl.%d" % (b, b, i, i), tt, T.zt[:, 4 * lo + b:4 * hi:4],
               ind(T.fz, blist(rl, i), C * b), plane(T.zp, b, lo, hi), A.add)

        hb = [6, 7, 2, 3]

        def layer():
            op("v", "zq", "zt0# zt1# zt2# zt3#", V.quantize_mx, T.zq[:, 0:C], T.zqs[:, 0:C], T.zt[:, 0:B4])
            product(6, T.wl, T.wls, 0, T.zq, T.zqs, "wl wls zq", 0, HALF)
            product(4, T.wl, T.wls, 0, T.zq, T.zqs, "wl wls zq", HALF, C)
            for b in range(1, 4):
                product(hb[b], T.wl, T.wls, 128 * b, T.zq, T.zqs, "wl wls zq")

        def state(i):
            lo, hi = (0, C) if i is None else (16 * PARTS[i][0], 16 * PARTS[i][1])
            at, me = blist(lst, i), "#" if i is None else ".%d" % i

            def outputs():
                op("v", "xq3" + me, " ".join("xt%d%s" % (b, me) for b in range(4)), V.quantize_mx, T.xq3[:, lo:hi], T.xs3[:, lo:hi], T.xt[:, 4 * lo:4 * hi])
                product(i, T.vq, T.vqs, 0, T.xq3, T.xs3, "vq xq3" + me, lo, hi)
                store("y", "xq3" + me, T.oc[:, 4 * lo:4 * hi], T.xq3[:, lo:hi].bitcast(dt.uint8))
                op("s", "yo" + me, "b%d" % i, act, T.yo[:, lo:hi], bank(i, 0, hi - lo), COPY)
                store("s", "yo" + me, T.y[:, lo:hi], T.yo[:, lo:hi])
            return series([later("v", "xt%d%s" % (b, me), "hh%d fo%d hhb lstb%s" % (b, b, me), tt, T.xt[:, 4 * lo + b:4 * hi:4],
                                 ind(T.hh, at, C * b), plane(T.fo, b, lo, hi), A.add) for b in range(4)] + [outputs])
        tail = dict(
            swap=swap, nf=followers, pick=lambda: pick("s"), vpick=lambda: pick("v"), add=add, layer=layer,
            h0a=later("s", "hh0", "b6", act, T.hh[:, 0:HALF], bank(6, 0, HALF), COPY, scale=0.03125),
            h0b=later("v", "hhb", "b4", ts, T.hh[:, HALF:C], bank(4, 0, C - HALF), 0.03125, None, A.mult),
            h=series(later("s", "hh%d" % b, "b%d" % hb[b], act, plane(T.hh, b), bank(hb[b]), COPY, scale=0.03125) for b in (1, 2, 3)),
            x=state(None), xa=state(0), xb=state(1))
        if t < 2:
            run(ORDER["near" if came is None else "far"], hopping, tail, head(t + 1))
        else:
            run(ORDER["last"], tail)
    for k in range(4):
        store("y", "xq3#", T.osc[4 * k:4 * k + 4, 0:C], T.xs3[32 * k:32 * k + 4, 0:C])
    for q in ("v", "s", "t", "g"):
        wait("g", semname[q], cnt[q])
    wait("g", "ls", nsent[0])
    wait("g", "out", nout[0])
